import numpy as np, ml_dtypes
CORES = [40,64,80,88,96,104,120,144]
N = 8
BF = ml_dtypes.bfloat16
W, A, T, M, RO, EPS, TH = 2048, 512, 256, 3, 3, 48, 640
WT = 15 * np.arange(16) + 7
RI, GI = np.arange(N)[:, None, None], np.arange(8)[None, :, None]
def clue(d):
    return np.add.reduce(d * WT, axis=-1)
def side(v):
    return (5 * v + (v >> 2)) & (A - 1)
def apart(cand, used):
    v = clue(cand); p, c = v & (A - 1), side(v)
    return cand[np.argmax((p != c) & ~np.isin(p, used) & ~np.isin(c, used))]
def rows128(a):
    return np.ascontiguousarray(np.swapaxes(a, 2, 3)).reshape(N, 128, -1)
def pack(X, S, K, z, l):
    return {"x0": rows128(X).astype(np.float32).astype(BF), "asc": rows128(S).astype(np.int32), "kw": rows128(K).astype(np.int32), "z0": rows128(z).astype(np.float32).astype(BF), "l0": np.ascontiguousarray(l).astype(np.int32)}
def parts(rng):
    mid = rng.integers(0, 256, (8, 32, 16)); order = np.argsort(rng.random((N, 8, W)), axis=-1); h = W >> 1
    X = rng.integers(0, 256, (N, 8, W, 16))
    X[RI, GI, order[:, :, :h]] = np.clip(mid[None, :, np.arange(h) % 32] + rng.integers(-20, 21, (N, 8, h, 16)), 0, 255)
    c = rng.integers(0, 32, (N, 8, T)); m = rng.random((N, 8, T, 1))
    z = np.clip(mid[GI, c] + rng.integers(-20, 21, (N, 8, T, 16)), 0, 255)
    z = np.where(m < 0.5, z, np.where(m < 0.8, rng.integers(0, 256, z.shape), rng.integers(96, 160, z.shape)))
    own = order[RI[..., None], GI[..., None], c[..., None] + 32 * rng.integers(0, W >> 6, (N, 8, T, 16))]
    share = rng.choice(np.array([0.0, 0.15, 0.5]), (N, 8, T, 1))
    K = np.where(rng.random((N, 8, T, 16)) < share, own, rng.integers(0, W, (N, 8, T, 16)))
    S = rng.integers(0, W, (N, 8, A, 16)); l = rng.choice(np.array([0, 0, 1, 1, 2, 3, 5, 8, 14, 15]), (N, 8, T))
    return X, S, K, z, l
def setup_inputs(rng):
    return pack(*parts(rng))
def setup_inputs_corners(rng):
    X, S, K, z, l = parts(rng)
    X[:, 6, 0] = 0; X[:, 6, W - 1] = 255
    S[:, 1] = (W - 1) * rng.integers(0, 2, (N, A, 16)); S[:, 3] = S[:, 3, :, :1].copy(); S[:, 5] = np.arange(A)[:, None]; S[:, 7] = rng.choice(np.array([0, 1, W - 2, W - 1]), (N, A, 16))
    mode = rng.integers(0, 8, (N, 8, T)); mo = mode[..., None]
    K = np.where((mo == 0) | (mo == 3), K[..., :1], np.where(mo == 1, (W - 1) * rng.integers(0, 2, K.shape), K))
    own = np.take_along_axis(K, rng.integers(0, 16, (N, 8, T, 1)), 3)[..., 0]
    z = np.where((mo == 2) | (mo == 3), X[RI, GI, own], np.where(mo == 7, 255 * rng.integers(0, 2, z.shape), z))
    l = np.where((mode == 4) | (mode == 7), 15, np.where(mode == 5, 14, np.where(mode == 6, 0, l)))
    zc = rng.integers(0, 256, 16); X[:, 2, W - 1] = zc; S[:, 2, 0] = rng.integers(0, W - 1, (N, 16)); S[::2, 2, 0, 15] = W - 1
    for t, n in ((0, 15), (T - 1, 14)):
        z[:, 2, t] = zc; K[:, 2, t] = W - 1; l[:, 2, t] = n
    lane = np.arange(T); bq = (np.arange(N)[:, None] + 1 + lane % M) % N; even = np.arange(N) % 2 == 0
    dl = rng.integers(1, 60, 16); z[:, 0] = rng.integers(64, 192, (N, T, 16)); z[:, 0, :, 0] = 0
    X[:, 0, :T] = z[:, 0] + dl * (2 * rng.integers(0, 2, (N, T, 16)) - 1); X[:, 0, :T, 0] = rng.permutation(T); K[:, 0] = lane[:, None]
    pat = rng.integers(0, 256, (16, 16))
    for m in range(4): X[:, 0, W - 64 + 16 * m:W - 48 + 16 * m] = pat
    S[:, 0] = W - 64 + 16 * (np.arange(N) % 4)[:, None, None] + np.argsort(rng.random((N, A, 16)), axis=-1)
    dl = rng.integers(0, 11, 16); z[:, 4] = np.where(bq % 2 == 0, 120, 135)[:, :, None] + rng.integers(-3, 4, (N, T, 16)); z[:, 4, :, 0] = 0
    X[:, 4] = np.where(even, 40, 215)[:, None, None] + rng.integers(-3, 4, (N, W, 16)); X[:, 4, :, 0] = 0
    X[:, 4, :T] = z[:, 4] + dl; X[:, 4, :T, 0] = rng.permutation(T); K[:, 4] = lane[:, None]
    S[:, 4] = T + np.argsort(rng.random((N, A, 1)), axis=1)
    lev = np.where(even, 100, 150); X[:, 5, :W - T] = lev[:, None, None] + rng.integers(-3, 4, (N, W - T, 16))
    z[:, 5] = lev[bq][:, :, None] + rng.integers(-3, 4, (N, T, 16)); X[:, 5, W - T:] = z[:, 5] + rng.integers(0, 11, (N, T, 16)); K[:, 5] = W - T + lane[:, None]
    return pack(X, S, K, z, l)
def setup_inputs_crowd(rng):
    X, S, K, z, l = parts(rng); lane = np.arange(T); bq = (np.arange(N)[:, None] + 1 + lane % M) % N
    for g in (0, 4):
        pat = rng.integers(40, 200, (16, 16)); pat[15] = rng.integers(0, 20, 16)
        if (clue(pat[15]) & (A - 1)) == side(clue(pat[15])): pat[15, 0] += 1
        X[:, g] = pat[np.arange(W) & 15]
        S[:, g] = np.argsort(rng.random((N, A, 16)), axis=-1) + 16 * rng.integers(0, W >> 4, (N, A, 16))
        z[:, g] = 0; l[:, g] = 0; K[:, g] = rng.integers(0, W, (N, T, 16)); K[:, g, :, 0] = (K[:, g, :, 0] >> 4) << 4
        if g == 4:
            K[:, g, 5] = 15 + 16 * rng.integers(0, W >> 4, (N, 16)); c = int(side(clue(pat[15])))
            S[:, g, c] = np.where((S[:, g, c] & 15) == 15, S[:, g, c] - 15, S[:, g, c])
    for g in (1, 5):
        dl = rng.integers(1, 60, 16)
        if (clue(dl) & (A - 1)) == 0: dl[0] += 1
        z[:, g] = rng.integers(64, 192, (N, T, 16)); X[:, g, :T] = z[:, g] + dl * (2 * rng.integers(0, 2, (N, T, 16)) - 1); K[:, g] = lane[:, None]
        pat = rng.integers(0, 256, (16, 16))
        for m in range(4): X[:, g, W - 64 + 16 * m:W - 48 + 16 * m] = pat
        S[:, g] = W - 64 + 16 * (np.arange(N) % 4)[:, None, None] + np.argsort(rng.random((N, 1, 16)), axis=-1)
        if g == 5: X[:, g, T] = z[:, g, 7]; K[:, g, 7] = T
    for g in (2, 6):
        X[:, g, W - 1] = np.where(np.arange(N) % 2 == 0, 40, 215)[:, None] + rng.integers(-3, 4, (N, 16)); S[:, g] = W - 1
        z[:, g] = np.where(bq % 2 == 0, 120, 135)[:, :, None] + rng.integers(-3, 4, (N, T, 16))
        X[:, g, :T] = z[:, g] + rng.integers(0, 21, (N, T, 16)); K[:, g] = lane[:, None]
        if g == 6: z[:, g, 9] = X[bq[:, 9], g, W - 1]; X[:, g, 9] = z[:, g, 9]
    for g in (3, 7):
        pat = rng.integers(0, 31, (16, 16)); pat[4] = rng.integers(185, 221, 16); pat[7] = 255; pat[8] = 0
        for q in range(3):
            e = rng.permutation(64); s = clue(pat[q]) + 7 * (e - pat[q, 0])
            pat[q, 0] = e[np.argmax(((s >> 2) & 15) == ((1 - 4 * q) & 15))]
        v = clue(pat[:3]); pat[3] = apart(rng.integers(0, 31, (64, 16)), np.concatenate([v & (A - 1), side(v)]))
        v = clue(pat[:4]); pat[6] = apart(rng.integers(0, 31, (64, 16)), np.concatenate([v & (A - 1), side(v)]))
        v3, v6 = int(clue(pat[3])), int(clue(pat[6])); a = ((RO - 1) * (T - (1 if g == 7 else 0))) & 31
        if g == 3: dl = np.concatenate([np.array([1, 2, 31]), rng.integers(1, 32, N - 3)])
        else: dl = np.concatenate([np.array([a - 1, a, a + 1]), a + rng.integers(-1, 3, N - 3)])
        dl = rng.permutation(dl)
        X[:, g] = pat[np.arange(W) & 15]; X[:, g, 5::16] = pat[4]; X[:, g, 5::16, 15] += dl[:, None]
        S[:, g] = 4 + 16 * rng.integers(0, W >> 4, (N, A, 16))
        S[:, g, side(v3)] += 1; S[:, g, v6 & (A - 1)] += 4; S[:, g, side(v6)] += 3
        z[:, g] = 0; K[:, g] = 4 - RO + 16 * rng.integers(0, W >> 4, (N, T, 16))
        if g == 7: K[:, g, T - 1] = 6 + 16 * rng.integers(0, W >> 4, (N, 16))
    return pack(X, S, K, z, l)
def setup_inputs_ends(rng):
    X = 255 * rng.integers(0, 2, (N, 8, W, 16)); pal = 255 * rng.integers(0, 2, (8, 8, 16)); pal[:, 0] = 0; pal[:, 1] = 255
    X = np.where(rng.random((N, 8, W, 1)) < 0.5, pal[GI, rng.integers(0, 8, (N, 8, W))], X)
    z = np.where(rng.random((N, 8, T, 1)) < 0.6, pal[GI, rng.integers(0, 8, (N, 8, T))], 255 * rng.integers(0, 2, (N, 8, T, 16)))
    S = np.where((np.arange(A) % 4 == 3)[:, None], rng.integers(0, W, (N, 8, A, 16)), (W - 1) * rng.integers(0, 2, (N, 8, A, 16)))
    K = np.where((np.arange(T) % 4 == 3)[:, None], rng.integers(0, W, (N, 8, T, 16)), (W - 1) * rng.integers(0, 2, (N, 8, T, 16)))
    l = 15 * rng.integers(0, 2, (N, 8, T)); top = int(clue(np.full(16, 255))); c1, c2 = top & (A - 1), int(side(top))
    for g in (0, 7):
        X[:, g, 0] = 0; X[:, g, W - 1] = 255
        for t in (0, T - 1): z[:, g, t] = 0; l[:, g, t] = 0; K[:, g, t] = 0; K[:, g, t, 1] = W - 1; K[:, g, t, 15] = W - 1
        for t in (1, T - 2): z[:, g, t] = 0; l[:, g, t] = 15; K[:, g, t] = 0; K[:, g, t, ::2] = W - 1
        for t in (2, T - 3): z[:, g, t] = 255; l[:, g, t] = 15; K[:, g, t] = 0
        for q in range(N):
            S[q, g, c1] = 0; S[q, g, c2] = 0; S[q, g, 0] = W - 1
            if q % 2 == 1: S[q, g, c1, 1] = W - 1; S[q, g, c1, 15] = W - 1
            if q % 3 == 1: S[q, g, c2, 2] = W - 1; S[q, g, c2, 15] = W - 1
            if q % 2 == 0: S[q, g, 0, 3] = 0; S[q, g, 0, 14] = 0
    return pack(X, S, K, z, l)
def setup_inputs_spread(rng):
    X = (np.exp2(8 * rng.random((N, 8, W, 1))) * rng.random((N, 8, W, 16))).astype(np.int64) * (rng.random((N, 8, W, 1)) > 0.0625)
    z = (np.exp2(8 * rng.random((N, 8, T, 1))) * rng.random((N, 8, T, 16))).astype(np.int64)
    X = np.where(rng.random((N, 8, W, 1)) < 0.3, 255 - X, X); z = np.where(rng.random((N, 8, T, 1)) < 0.5, 255 - z, z)
    S = (W * rng.random((N, 8, A, 16)) ** 3).astype(np.int64); K = (W * rng.random((N, 8, T, 16)) ** 4).astype(np.int64); l = (16 * rng.random((N, 8, T)) ** 3).astype(np.int64)
    return pack(X, S, K, z, l)
def setup_inputs_ties(rng):
    X, S, K, z, l = parts(rng); few = np.array([0, EPS, EPS + 1, 2 * EPS, 255])
    for g in (0, 2, 4, 6):
        s = few[:3] if g < 4 else few
        X[:, g] = rng.choice(s, (N, W, 16)); z[:, g] = rng.choice(s, (N, T, 16))
    for g, e in ((1, 1), (3, 31), (7, 32)):
        y = np.full((N, 16), 100); y[1::2, 15] += e; X[:, g, W - 1] = y; S[:, g] = W - 1
        dev = np.full((N, T, 16), TH >> 4); dev[..., 0] += rng.integers(-2, 3, (N, T))
        z[:, g] = 100 + (2 * rng.integers(0, 2, (N, T, 1)) - 1) * dev; X[:, g, :T] = z[:, g]; K[:, g] = np.arange(T)[:, None]
    lane = np.arange(T); bq = (np.arange(N)[:, None] + 1 + lane % M) % N; cq = (bq[:, 0] + 1) % N
    own = rng.integers(0, 251, (N, 16)); own[:, 0] = 30 * np.arange(N)
    order = rng.permutation(N); dl = rng.integers(1, 5, N); dl[order[:4]] = np.array([1, 2, 3, 1])
    near = np.roll(own, 1, axis=0); near[:, 15] += dl
    X[:, 5, W - 1] = own; X[:, 5, W - 2] = near
    S[:, 5, 0] = W - 1 - (np.argsort(rng.random((N, 16)), axis=-1) & 1)
    z[:, 5] = own[bq]; z[:, 5, 0] = np.where((cq != order[3])[:, None], near[cq], own[bq[:, 0]])
    X[:, 5, :T] = z[:, 5]; K[:, 5] = lane[:, None]
    return pack(X, S, K, z, l)
def check_inputs(d):
    bad = []
    for k, lo, hi in (("x0", 0, 255), ("asc", 0, W - 1), ("kw", 0, W - 1), ("z0", 0, 255), ("l0", 0, 15)):
        v = np.asarray(d[k]).astype(np.float64)
        if not (np.min(v) >= lo and np.max(v) <= hi): bad.append("range of " + k)
        elif np.any(v != np.floor(v)): bad.append("whole numbers of " + k)
    return bad
def reference(x0, asc, kw, z0, l0):
    def turn(a):
        return np.ascontiguousarray(np.swapaxes(a.astype(np.float32).astype(np.int32).reshape(N, 8, 16, -1), 2, 3))
    X, S, K, z, l = turn(x0), turn(asc), turn(kw), turn(z0), l0.astype(np.int32)
    ri, gi = np.arange(N)[:, None, None], np.arange(8)[None, :, None]; i16 = np.arange(16); wt = (15 * np.arange(16) + 7).astype(np.int32)
    b = (np.arange(N)[:, None] + 1 + np.arange(T)[None, :] % M) % N; c = (b + 1) % N
    al = np.zeros((N, 8), np.int32)
    def look(q, col, aim, dl):
        p = S[q[:, None, :], gi, col]; y = X[q[:, None, :, None], gi[..., None], p]
        e = np.add.reduce(np.abs(np.abs(y - aim[:, :, :, None]) - dl[:, :, :, None]), axis=-1); j = np.argmin(e, axis=-1)
        return p, j, np.take_along_axis(e, j[..., None], 3)[..., 0], np.take_along_axis(y, j[..., None, None], 3)[:, :, :, 0]
    for rnd in range(RO):
        x = X[ri[..., None], gi[..., None], K]; dx = np.abs(x - z[:, :, :, None])
        fit = ~np.any((dx > EPS) & (i16 < l[..., None])[:, :, :, None], axis=-1)
        may = fit | ~np.any(fit, axis=-1, keepdims=True)
        k = np.argmax(np.where(may, np.add.reduce(dx, axis=-1), -1), axis=-1)[..., None, None]
        de = np.take_along_axis(dx, k, 3)[:, :, :, 0]; xs = np.take_along_axis(x, k, 3)[:, :, :, 0]
        v = np.add.reduce(de * wt, axis=-1); cb = v & (A - 1); cc = (5 * v + (v >> 2)) & (A - 1)
        p, j, eb, y = look(b, cb, z, de); pg, g, ec, yg = look(c, cc, z, de)
        hit = ec <= eb + (al[c[:, None, :], gi] & 31); con = ~hit & (eb < TH); nei = ~hit & ~con
        zn = np.where(con[..., None], y, np.where(nei[..., None], (z + xs) >> 1, z)); ln = np.where(con, (l + 1) & 15, l)
        off = np.any((np.abs(x - zn[:, :, :, None]) > EPS) & (i16 < ln[..., None])[:, :, :, None], axis=-1)
        K = np.where(hit[..., None], (5 * K + (v >> 2)[..., None]) & (W - 1), np.where(con[..., None] & off, p, K))
        word = np.take_along_axis(p, j[..., None], 3)[..., 0]; new = (y + de) >> 1
        column = np.where(i16 == j[..., None], np.take_along_axis(pg, g[..., None], 3), p)
        for t in range(T):
            r, h = np.nonzero(nei[:, :, t]); X[b[r, t], h, word[r, h, t]] = new[r, h, t]
            r, h = np.nonzero(hit[:, :, t]); S[b[r, t], h, cb[r, h, t]] = column[r, h, t]
            al[c[:, t]] += hit[:, :, t]
        z, l = zn, ln
    def back(a):
        return np.ascontiguousarray(np.swapaxes(a, 2, 3)).reshape(N, 128, -1).astype(np.float32)
    return {"yx": back(X).astype(BF), "ya": back(S), "yk": back(K), "yz": back(z).astype(BF), "yl": l.astype(np.float32)}

@@ -1,0 +1,876 @@
+import math
+from concourse.bass import DstId, RemoteDMATransfer
+from concourse.mybir import AluOpType as ALU, AxisListType as AX, ActivationFunctionType as AF
+
+NF, NB, NI, NU, NH = 16384, 57344, 3072, 2048, 1536
+SCRATCH = {
+    "F": ("sbuf", [128, NF], "float32"), "B": ("sbuf", [128, NB], "bfloat16"), "I": ("sbuf", [128, NI], "int32"),
+    "U": ("sbuf", [128, NU], "uint16"), "H": ("sbuf", [128, NH], "float16"),
+    "W0": ("psum", [128, 1024], "float32"), "W1": ("psum", [128, 1024], "float32"),
+    "SA": ("psum", [128, 512], "float32"), "SB": ("psum", [128, 512], "float32"),
+    "M0": ("psum", [128, 512], "float32"), "M1": ("psum", [128, 512], "float32"),
+}
+KINDS = {"iz": (32, "bfloat16"), "il": (16, "int32"), "ik": (32, "int32"), "ix": (128, "bfloat16"), "iy": (128, "bfloat16"), "ia": (64, "int32"),
+         "oz": (32, "bfloat16"), "ol": (16, "float32"), "ox": (256, "bfloat16"), "oa": (64, "float32"), "ok": (32, "float32")}
+CALLS = [("iz", "il"), ("ik",), ("ix",), ("iy",), ("ia",), ("oz", "ol"), ("ox",), ("oa",), ("ok",)]
+for _k, (_n, _d) in KINDS.items():
+    SCRATCH["s" + _k] = ("dram", [1 if _k[1] == "l" else 8, 128, _n], _d)
+    SCRATCH["l" + _k] = ("dram", [8, 128, _n], _d)
+NDMA = 40
+SEMAPHORES = ["cV", "cA", "cP", "cG", "sent"] + ["arr%d" % i for i in range(len(CALLS))] + ["d%d" % i for i in range(NDMA)]
+PSUM = ("W0", "W1", "SA", "SB", "M0", "M1")
+MAGIC = 12582912.0
+OPT = {"sign1": (), "sign6": (), "relu": (5, 7), "krow": "A", "plist": "A", "glist": "A", "dd": "V", "lat": 0.1, "ga": 1.56, "actg": 1, "z4": "G", "ev": "V", "dg": "V", "iters": 2400, "amp": 0.5}
+
+
+def routes(T, topo):
+    cores = T.cores
+    n = len(cores)
+    way = {}
+    for s in range(n):
+        me = cores[s]
+        kin = [r for r in range(n) if r == s or topo.may_write(me, cores[r])]
+        far = [r for r in range(n) if r not in kin]
+        others = [c for c in topo.cores_of(me) if c != me]
+        port = [c for c in others if far and all(topo.may_write(c, cores[r]) for r in far)]
+        byd = [[c for c in port if topo.die(c) == topo.die(me)], [c for c in port if topo.die(c) != topo.die(me)]]
+        i = kin.index(s)
+        for j, r in enumerate(far):
+            side = byd[(i + j) % 2] if byd[(i + j) % 2] else byd[(i + j + 1) % 2]
+            way[(s, r)] = side.pop(0)
+        free = [c for c in others if c not in port and topo.die(c) != topo.die(me)]
+        for j in range(len(kin) - 1, 0, -1):
+            r = kin[(i + j) % len(kin)]
+            way[(s, r)] = free.pop(0) if free and j > 1 else me
+    return way
+
+
+def bits(es):
+    m = 0
+    for e in es:
+        m |= 1 << e
+    return m
+
+
+def first_hop(T, topo, way, s, ci):
+    me = T.cores[s]
+    items = [(k, r) for r in range(len(T.cores)) if r != s for k in CALLS[ci]]
+    items.sort(key=lambda it: way[(s, it[1])] != me)
+    per = 2 if len(CALLS[ci]) == 1 else 1
+    used, out = [], []
+    for k, r in items:
+        to = T.cores[r] if way[(s, r)] == me else way[(s, r)]
+        es = [e for e in topo.engines(me, to) if e not in used][:2 * per if to == T.cores[r] else per]
+        used += es
+        out.append((k, r, to, es))
+    return out
+
+
+def second_hop(T, topo, relay, r, ci):
+    es = topo.engines(relay, T.cores[r])
+    n = len(es) // len(CALLS[ci])
+    return [(k, es[i * n:(i + 1) * n]) for i, k in enumerate(CALLS[ci])]
+
+
+def arrivals(T, topo, way, r, ci):
+    tot = 0
+    for s in range(len(T.cores)):
+        if s == r:
+            continue
+        if way[(s, r)] == T.cores[s]:
+            tot += sum(len(es) for k, d, to, es in first_hop(T, topo, way, s, ci) if d == r)
+        else:
+            tot += sum(len(es) for k, es in second_hop(T, topo, way[(s, r)], r, ci))
+    return tot
+
+
+def relay_program(g, core, T, topo, way):
+    for (s, r), c in way.items():
+        if c != core:
+            continue
+        rid, pid = topo.addr(T.cores[r], core)
+        sent = 0
+        for ci in range(len(CALLS)):
+            g.wait_ge(T.sem["arr%d" % ci], sum(len(es) for k, d, to, es in first_hop(T, topo, way, s, ci) if d == r))
+            tr = []
+            for k, es in second_hop(T, topo, core, r, ci):
+                tr.append(RemoteDMATransfer(dst_ids=[DstId(rid=rid, pnc=pid)], dma_engine_mask=bits(es), remote_sem=T.sem["arr%d" % ci],
+                                            src=T["l" + k][s], dst=T["l" + k][s]))
+                sent += len(es)
+            g.remote_dma_fused(tr, local_sem=T.sem.sent)
+        g.wait_ge(T.sem.sent, sent)
+
+
+def rank_program(g, core, T, topo):
+    way = routes(T, topo)
+    rank = T.rank_of(core)
+    if rank is None:
+        relay_program(g, core, T, topo, way)
+        return
+    ops = build(g, core, rank, T, topo, way)
+    emit(g, T, ops)
+
+
+PLAN = {}
+
+
+def arrange(ops):
+    n, lat = len(ops), OPT["lat"]
+    hist, preds = {}, []
+    for i, o in enumerate(ops):
+        p = {}
+        for acc, isw in [(a, False) for a in o["r"]] + [(a, True) for a in o["w"]]:
+            name, lo, hi = acc[0], acc[1], acc[2]
+            ps = name in PSUM
+            if ps:
+                lo, hi = lo // 512 * 512, (hi + 511) // 512 * 512
+            for bk in range(lo // 256, (hi - 1) // 256 + 1):
+                keep = []
+                for (j, l2, h2, w2) in hist.get((name, bk), []):
+                    hit = l2 < hi and lo < h2
+                    same = ops[j]["e"] == o["e"] and not (o["dma"] or ops[j]["dma"])
+                    if j != i and hit and (isw or w2 or (ps and not same)):
+                        p[j] = p.get(j, False) or not ((same and o["e"] == "P") or name.startswith("call"))
+                    cover = lo <= max(l2, 256 * bk) and min(h2, 256 * bk + 256) <= hi
+                    if not (hit and isw and cover and j != i and not (ps and same and w2 and o["e"] != "P")):
+                        keep.append((j, l2, h2, w2))
+                keep.append((i, lo, hi, isw))
+                hist[(name, bk)] = keep
+        preds.append(p)
+    succ = [[] for _ in range(n)]
+    for i in range(n):
+        for j in preds[i]:
+            succ[j].append(i)
+    eng, c = [o["e"] for o in ops], [max(o["c"], 0.001) for o in ops]
+    lag = [{j: (ops[j]["x"] + lat if sem or ops[j]["x"] > 1 else 0.0) for j, sem in preds[k].items()} for k in range(n)]
+    fw = [list(lag[k].items()) for k in range(n)]
+    bw = [[(k, lag[k][j]) for k in succ[j]] for j in range(n)]
+
+    def place(seq, dep, head):
+        end = [0.0] * n
+        busy = {e: ([], []) for e in "VAPGS"}
+        for i in seq:
+            t = head[i]
+            for j, d in dep[i]:
+                if end[j] + d > t:
+                    t = end[j] + d
+            los, his = busy[eng[i]]
+            a, b = 0, len(his)
+            while a < b:
+                m = (a + b) // 2
+                if his[m] <= t:
+                    a = m + 1
+                else:
+                    b = m
+            while a < len(los) and los[a] < t + c[i] - 1e-9:
+                t = max(t, his[a])
+                a += 1
+            los.insert(a, t)
+            his.insert(a, t + c[i])
+            end[i] = t + c[i]
+        return end
+
+    def feasible(key, dep, nxt):
+        left = [len(d) for d in dep]
+        k2 = list(key)
+        for i in sorted(range(n), key=lambda i: topo_pos(i, dep is fw)):
+            for j, d in dep[i]:
+                if k2[j] >= k2[i]:
+                    k2[i] = k2[j] + 1e-7
+        return sorted(range(n), key=lambda i: k2[i])
+
+    def topo_pos(i, forward):
+        return i if forward else -i
+    zero, tailx = [0.0] * n, [o["x"] for o in ops]
+    prio = [0.0] * n
+    for i in range(n - 1, -1, -1):
+        prio[i] = c[i] + max([prio[k] + d for k, d in bw[i]] + [ops[i]["x"]])
+    key, best, seed = [-p for p in prio], None, 12345
+    for it in range(OPT["iters"]):
+        end = place(feasible(key, fw, bw), fw, zero)
+        span = max(end[i] + tailx[i] for i in range(n))
+        if best is None or span <= best[0]:
+            best = (span, end)
+        src = best[1] if it % 2 == 1 else end
+        noise = [0.0] * n
+        if it % 2 == 1:
+            seed = (seed * 1103515245 + 12345) % 2147483648
+            lo = best[0] * seed / 2147483648.0 - 4.0
+            amp = OPT["amp"] * (1 + seed // 64 % 6)
+            for i in range(n):
+                if lo < src[i] < lo + 8.0:
+                    seed = (seed * 1103515245 + 12345) % 2147483648
+                    noise[i] = amp * (seed / 2147483648.0 - 0.5)
+        back = place(feasible([-src[i] + noise[i] for i in range(n)], bw, fw), bw, tailx)
+        key = [-back[i] for i in range(n)]
+    start = [best[1][i] - c[i] for i in range(n)]
+    fin = [best[1][i] + tailx[i] for i in range(n)]
+    order = feasible(start, fw, bw)
+    pos, cnt = {}, {e: 0 for e in "VAPGS"}
+    for i in order:
+        cnt[ops[i]["e"]] += 1
+        pos[i] = cnt[ops[i]["e"]]
+    known = {e: {} for e in "VAPGS"}
+    snap, waits, need = {}, {}, set()
+    for i in order:
+        kn = known[ops[i]["e"]]
+        best = {}
+        for j, sem in preds[i].items():
+            if not sem:
+                continue
+            key = ("d", j) if ops[j]["dma"] else ops[j]["e"]
+            if key not in best or pos[j] > pos[best[key]]:
+                best[key] = j
+        ws = []
+        for key, j in sorted(best.items(), key=lambda kv: -fin[kv[1]]):
+            if kn.get(key, 0) >= pos[j]:
+                continue
+            ws.append(j)
+            need.add(j)
+            kn[key] = pos[j]
+            for k2, v in snap[j].items():
+                if kn.get(k2, 0) < v:
+                    kn[k2] = v
+        waits[i] = ws
+        snap[i] = dict(kn)
+    return order, waits, need, start, fin
+
+
+def emit(g, T, ops):
+    if "p" not in PLAN:
+        PLAN["p"] = arrange(ops)
+    order, waits, need, start, fin = PLAN["p"]
+    q = {"V": g.vector, "A": g.scalar, "P": g.tensor, "G": g, "S": g.sync}
+    num, cnt, nd, tail = {}, {e: 0 for e in "VAPG"}, 0, []
+    for i in order:
+        o = ops[i]
+        o["st"], o["fin"] = start[i], fin[i]
+        for j in waits[i]:
+            q[o["e"]].wait_ge(num[j][0], num[j][1])
+        for sem, v in o["ext"]:
+            q[o["e"]].wait_ge(sem, v)
+        ins = o["f"]()
+        if o["dma"]:
+            num[i] = (T.sem["d%d" % nd], 16)
+            nd += 1
+            ins.then_inc(num[i][0], 16)
+            if i not in need:
+                tail.append(i)
+        elif i in need:
+            cnt[o["e"]] += 1
+            num[i] = (T.sem["c" + o["e"]], cnt[o["e"]])
+            ins.then_inc(num[i][0], 1)
+    for i in tail:
+        g.wait_ge(num[i][0], 16)
+    for sem, v in ops[0]["end"]:
+        g.wait_ge(sem, v)
+
+
+def build(g, core, rank, T, topo, way):
+    ops = []
+    top = {"F": 0, "B": 0, "I": 0, "U": 0, "H": 0}
+    CY, GA, PC = 0.00083, OPT["ga"], 0.00042
+    two = ("B", "U", "H")
+
+    def new(pool, n):
+        lo = top[pool]
+        top[pool] = lo + (n + 15) // 16 * 16
+        assert top[pool] <= SCRATCH[pool][1][1], pool
+        return (pool, lo, lo + n, 1)
+
+    def sl(r, a, b, s=1):
+        return (r[0], r[1] + a, r[1] + b, s)
+
+    def part(r, i, n):
+        return sl(r, n * i, n * i + n)
+
+    def width(r):
+        return (r[2] - r[1] + r[3] - 1) // r[3]
+
+    def ind(win, off):
+        return ("ind", win, off)
+
+    def ap(r):
+        if r[0] == "ind":
+            return ap(r[1]).indirect(ap(r[2]))
+        if r[3] == 1:
+            return T[r[0]][:, r[1]:r[2]]
+        return T[r[0]][:, r[1]:r[2]:r[3]]
+
+    def isref(x):
+        return isinstance(x, tuple)
+
+    def val(x):
+        return ap(x) if isref(x) else x
+
+    def add(e, f, r, w, c, x=0.0, dma=False, ext=()):
+        rr = []
+        for a in r:
+            if isref(a):
+                rr += [a[1], a[2]] if a[0] == "ind" else [a]
+        ww = []
+        for a in w:
+            if a[0] == "ind":
+                ww.append(a[1])
+                rr.append(a[2])
+            else:
+                ww.append(a)
+        ops.append({"e": e, "f": f, "r": rr, "w": ww, "c": c, "x": x, "dma": dma, "ext": list(ext), "end": []})
+
+    def vcost(out, a, k=1.0):
+        if a[0] == "ind":
+            return 0.05 + width(out) * GA * CY
+        if out[0] == "ind":
+            return 0.05 + width(a) * 3.8 * CY
+        if k == 1.0 and out[0] in two and a[0] in two:
+            k = 0.5
+        return 0.02 + max(64, width(a) * k) * CY
+
+    def copy(out, a):
+        add("V", lambda: g.vector.tensor_copy(ap(out), ap(a)), [a], [out], vcost(out, a))
+
+    def tt(out, a, b, op):
+        k = 1.001 if a[0] in PSUM or b[0] in PSUM else 2.0
+        add("V", lambda: g.vector.tensor_tensor(ap(out), ap(a), ap(b), op), [a, b], [out], vcost(out, a, k))
+
+    def ts(out, a, s1, op0, s2=None, op1=None):
+        if op1 is None:
+            f = lambda: g.vector.tensor_scalar(ap(out), ap(a), val(s1), None, op0)
+        else:
+            f = lambda: g.vector.tensor_scalar(ap(out), ap(a), val(s1), val(s2), op0, op1)
+        add("V", f, [a, s1, s2], [out], vcost(out, a))
+
+    def tr(out, a):
+        add("V", lambda: g.vector.transpose(ap(out), ap(a)), [a], [out], vcost(out, a))
+
+    def fill(out, v):
+        add("V", lambda: g.vector.memset(ap(out), v), [], [out], vcost(out, out))
+
+    def act(out, a, fn, bias=None, scale=None):
+        def f():
+            if bias is None:
+                return g.scalar.activation(ap(out), ap(a), fn)
+            return g.scalar.activation(ap(out), ap(a), fn, bias=val(bias), scale=scale)
+        c = 0.065 + width(out) * GA * CY if a[0] == "ind" else 0.1 + max(64, width(out)) * CY
+        add("A", f, [a, bias], [out], c)
+
+    def move(e, out, a):
+        if e == "A":
+            act(out, a, AF.Copy)
+        elif e == "G":
+            add("G", lambda: g.affine_select(ap(out), ap(a), [[0, width(a)]], ALU.is_ge, 0.0, 0, 0), [a], [out], 0.17 + 2 * CY * width(a))
+        else:
+            copy(out, a)
+
+    def mm(items):
+        def f():
+            last = None
+            for out, l, r, st, sp in items:
+                last = g.tensor.matmul(ap(out), ap(l), ap(r), st, sp)
+            return last
+        c = sum(max(64, width(r)) * (4 if l[0] == "F" else 1) * PC for out, l, r, st, sp in items)
+        add("P", f, [x for it in items for x in it[1:3]], [it[0] for it in items], c, x=0.1)
+
+    def group(items):
+        mm([(o, l, r, i == 0, i == len(items) - 1) for i, (o, l, r) in enumerate(items)])
+
+    def apart(items):
+        mm([(o, l, r, True, True) for o, l, r in items])
+
+    def iota(out, rd=()):
+        n = width(out)
+        if out[0] == "F":
+            f = lambda: g.iota(ap(out), [[1, n]], 0, 0, allow_small_or_imprecise_dtypes=True)
+        else:
+            f = lambda: g.iota(ap(out), [[1, n]], 0, 1 if n == 1 else 0)
+        add("G", f, list(rd), [out], 0.13 + 2 * CY * n)
+
+    def dma(e, out, a, r, w, us, ext=()):
+        qq = {"S": g.sync, "A": g.scalar, "G": g}[e]
+        add(e, lambda: qq.dma_start(out, a), r, w, 0.1 if e != "G" else 1.0, x=2.0 + us, dma=True, ext=ext)
+
+    sent = [0]
+
+    def remote(ci):
+        trs = []
+        for k, r, to, es in first_hop(T, topo, way, rank, ci):
+            rid, pid = topo.addr(to, core)
+            trs.append(RemoteDMATransfer(dst_ids=[DstId(rid=rid, pnc=pid)], dma_engine_mask=bits(es), remote_sem=T.sem["arr%d" % ci],
+                                         src=T["s" + k][0 if k[1] == "l" else r], dst=T["l" + k][rank]))
+            sent[0] += len(es)
+        add("G", lambda: g.remote_dma_fused(trs, local_sem=T.sem.sent), [("s" + k, 0, 8) for k in CALLS[ci]] + [("callo", 0, 1)],
+            [("call%d" % ci, 0, 1), ("callo", 0, 1)], 1.0, x=0.0)
+        add("G", lambda: None, [("call%d" % ci, 0, 1)], [("call%d" % ci, 0, 1)], 0.0, x=7.0)
+
+    def arr(ci):
+        return [(T.sem["arr%d" % ci], arrivals(T, topo, way, rank, ci))]
+
+    def own(e, k, src, rd):
+        dma(e, T["l" + k][rank], src, rd, [("l" + k, 0, 1)], 0.1)
+
+    P = {k: (k, 0, SCRATCH[k][1][1], 1) for k in PSUM}
+    rows = slice(16 * rank, 16 * rank + 16)
+
+    WIN = new("F", 2592)
+    XW, SW = sl(WIN, 0, 2048), sl(WIN, 2048, 2560)
+    Xb = new("B", 2048)
+    CZ = [new("B", 768), new("B", 768)]
+    K, L = new("F", 256), new("F", 16)
+    KU = new("U", 256)
+    KI, LI, SI = new("I", 256), new("I", 16), new("I", 512)
+    Z = sl(CZ[0], 0, 256)
+
+    dma("S", T["six"][:], T.x0[:, 0:1024], [], [("six", 0, 8)], 0.8)
+    dma("S", T.siy[:], T.x0[:, 1024:2048], [], [("siy", 0, 8)], 1.5)
+    dma("A", T.siz[:], T.z0[:], [], [("siz", 0, 8)], 0.2)
+    dma("A", T.sil[:], T.l0[:], [], [("sil", 0, 8)], 0.1)
+    dma("A", T.sik[:], T.kw[:], [], [("sik", 0, 8)], 0.4)
+    dma("S", T.sia[:], T.asc[:], [], [("sia", 0, 8)], 0.8)
+    own("A", "iz", T.z0[rows, :], [])
+    own("A", "il", T.l0[:], [])
+    own("A", "ik", T.kw[rows, :], [])
+    own("S", "ix", T.x0[rows, 0:1024], [])
+    own("S", "iy", T.x0[rows, 1024:2048], [])
+    own("S", "ia", T.asc[rows, :], [])
+    for ci in range(5):
+        remote(ci)
+    dma("A", ap(Z), T.liz[:], [("liz", 0, 8), ("call0", 0, 1)], [Z], 0.3, ext=arr(0))
+    dma("A", ap(LI), T.lil[:, rows, :], [("lil", 0, 8), ("call0", 0, 1)], [LI], 0.1, ext=arr(0))
+    dma("A", ap(KI), T.lik[:], [("lik", 0, 8), ("call1", 0, 1)], [KI], 0.4, ext=arr(1))
+    for h, k in enumerate(("lix", "liy")):
+        dma("S", ap(part(Xb, h, 1024)), T[k][:], [(k, 0, 8), ("call%d" % (2 + h), 0, 1)], [part(Xb, h, 1024)], 0.8, ext=arr(2 + h))
+    dma("S", ap(SI), T.lia[:], [("lia", 0, 8), ("call4", 0, 1)], [SI], 0.8, ext=arr(4))
+    for h, k in enumerate(("lix", "liy")):
+        dma("G", ap(part(XW, h, 1024)), T[k][:], [(k, 0, 8), ("call4", 0, 1), Xb, SI], [part(XW, h, 1024)], 1.5)
+
+    pI, cI = new("I", 1), new("I", 256)
+    iota(pI)
+    iota(cI)
+    IOTA = new("F", 2608)
+    iota(IOTA, [("callo", 0, 1)])
+    cF = new("F", 256)
+    copy(cF, cI)
+    c16 = sl(cF, 0, 16)
+
+    def col(pool="F"):
+        return new(pool, 1)
+
+    def icol(src, s1, op0, s2=None, op1=None):
+        i, f = col("I"), col()
+        ts(i, src, s1, op0, s2, op1)
+        copy(f, i)
+        return f
+    pF = col()
+    copy(pF, pI)
+    uF = icol(pI, 15, ALU.bitwise_and)
+    kF = icol(pI, 112, ALU.bitwise_and)
+    hF = icol(pI, 4, ALU.arith_shift_right, 1, ALU.bitwise_and)
+    u7 = icol(pI, 7, ALU.bitwise_and)
+    u8 = icol(pI, 3, ALU.arith_shift_right, 1, ALU.bitwise_and)
+    ones = new("B", 128)
+    fill(ones, 1.0)
+    k16 = col()
+    ts(k16, kF, 16.0, ALU.add)
+    wcb, wc, wv = col("B"), col(), col()
+    LN2 = math.log(2.0)
+    b15, b17, bm48, bhalf = col(), col(), col(), col()
+    fill(b15, 15 * LN2)
+    fill(b17, 17 * LN2)
+    fill(bm48, -48.5)
+    fill(bhalf, 0.5)
+    act(wcb, uF, AF.Exp, b15, -LN2)
+    copy(wc, wcb)
+    ts(wv, uF, 15.0, ALU.mult, 7.0, ALU.add)
+
+    def slide(pool, w):
+        z = new(pool, 160)
+        ts(z, sl(cF, 0, 160), k16, ALU.is_equal, w, ALU.mult)
+        return z
+    Zd, Ze, Zc, Zv, Zh, Z1 = slide("B", -256.0), slide("B", 256.0), slide("B", wc), slide("B", wv), slide("H", 1.0), slide("B", 4096.0)
+
+    def zu(z, u):
+        return sl(z, 16 - u, 144 - u)
+    tri = new("B", 2048)
+    gt16 = new("F", 16)
+    ts(gt16, c16, uF, ALU.is_lt)
+    for u in range(16):
+        ts(part(tri, u, 128), zu(Z1, u), sl(gt16, u, u + 1), ALU.mult)
+    c127I, c127 = new("I", 256), new("F", 256)
+    ts(c127I, cI, 127, ALU.bitwise_and)
+    copy(c127, c127I)
+
+    def shifts(pool, w, a=0):
+        y = new(pool, 256)
+        ts(sl(y, a, 256), sl(c127, a, 256), pF, ALU.is_equal, w, ALU.mult)
+        return y
+    Y, YF = shifts("B", 1.0), shifts("F", 1.0)
+
+    def sh(y, k):
+        k %= 8
+        return sl(y, 128 - 16 * k, 256 - 16 * k)
+    I1, IN, IH, I2, IB = sh(Y, 0), sh(shifts("B", -1.0, 128), 0), sh(shifts("B", 0.5, 128), 0), sh(shifts("B", 2.0, 128), 0), sh(shifts("B", 524288.0, 128), 0)
+    c112I, c112 = new("I", 256), new("F", 256)
+    ts(c112I, cI, 112, ALU.bitwise_and)
+    copy(c112, c112I)
+    BOh, BOn, BOc, BO1 = new("H", 256), new("H", 128), new("B", 128), new("B", 128)
+    ts(BOh, c112, kF, ALU.is_equal)
+    ts(BOn, sl(c112, 0, 128), kF, ALU.is_equal, -1.0, ALU.mult)
+    ts(BOc, sl(c112, 0, 128), kF, ALU.is_equal, wc, ALU.mult)
+    ts(BO1, sl(c112, 0, 128), kF, ALU.is_equal)
+    PB, PF = [], []
+    for be in range(3):
+        qi, tc, t2, t3 = col("I"), col(), col("I"), col("I")
+        ts(qi, uF, 1.0 / 3, ALU.mult, (be - 1) / 3.0, ALU.add)
+        ts(tc, qi, 48.0, ALU.mult, kF, ALU.add)
+        ts(t2, uF, -15.0, ALU.mult, tc, ALU.add)
+        ts(t3, t2, float(128 - 16 - 16 * be), ALU.add)
+        t4 = icol(t3, 127, ALU.bitwise_and)
+        pb, pf = new("B", 128), new("F", 128)
+        ts(pb, sl(cF, 0, 128), t4, ALU.is_equal)
+        ts(pf, sl(cF, 0, 128), t4, ALU.is_equal)
+        PB.append(pb)
+        PF.append(pf)
+    eq16 = new("F", 16)
+    ts(eq16, c16, uF, ALU.is_equal)
+    IBIG = new("B", 4096)
+    for j in range(16):
+        ts(part(IBIG, j, 128), ones, sl(eq16, j, j + 1), ALU.mult)
+    copy(part(IBIG, 1, 2048), part(IBIG, 0, 2048))
+    cB = new("B", 256)
+    copy(cB, cF)
+    quarter = new("B", 256)
+    fill(quarter, -0.25)
+    sg1, sg6 = new("B", 256), new("B", 256)
+    for s, ch in ((sg1, OPT["sign1"]), (sg6, OPT["sign6"])):
+        for c in range(4):
+            fill(part(s, c, 64), 1.0 if c in ch else 0.0)
+    cz = new("B", 16)
+    ts(cz, c16, -1.0 / 16, ALU.mult, -2.0, ALU.add)
+    spare = col()
+    ts(spare, uF, 2560.0, ALU.add)
+    spare2, repo, ro1, eq2 = col(), new("U", 16), new("I", 16), new("B", 256)
+    ts(spare2, uF, 2576.0, ALU.add)
+    ts(ro1, sl(cI, 0, 16), 14, ALU.bitwise_and)
+    ts(repo, ro1, 1.0, ALU.add)
+    c421 = new("F", 16)
+    fill(sl(c421, 0, 8), 4.0)
+    fill(sl(c421, 8, 16), 21.0)
+    repb, repk, o9, reord, pickN = (new("U", 16) for _ in range(5))
+    pickW, pick9, pickL = new("U", 8), new("U", 9), new("U", 1)
+    copy(repb, c16)
+    e1, e2, e3, e4, e5 = new("I", 16), new("F", 16), col(), col(), col()
+    ts(e1, sl(cI, 0, 16), 8, ALU.bitwise_and)
+    ts(repk, e1, u7, ALU.add)
+    ts(e3, u8, 9.0, ALU.mult, u7, ALU.add)
+    ts(o9, c16, 18.0, ALU.mult, e3, ALU.add)
+    ts(e2, e1, 15.0, ALU.mult)
+    tt(e2, e2, c16, ALU.add)
+    ts(e4, uF, 8.0, ALU.mult)
+    ts(reord, e2, e4, ALU.add)
+    s1 = col("I")
+    tt(s1, uF, hF, ALU.add)
+    s2 = icol(s1, 1, ALU.bitwise_and)
+    s3 = col()
+    ts(e5, u7, 16.0, ALU.mult, u8, ALU.add)
+    ts(s3, s2, 144.0, ALU.mult, e5, ALU.add)
+    ts(pickW, sl(cF, 0, 8), 2.0, ALU.mult, s3, ALU.add)
+    ts(pickL, hF, 16.0, ALU.mult, uF, ALU.add)
+    n1, n2, n3 = new("I", 16), new("I", 16), new("F", 16)
+    ts(n1, c16, hF, ALU.add)
+    ts(n2, n1, 1, ALU.bitwise_and)
+    ts(n3, n2, 17.0, ALU.mult)
+    tt(n3, n3, c16, ALU.add)
+    ts(pickN, n3, 16.0, ALU.mult, uF, ALU.add)
+    m0, m1, m3, m4, m5, m6 = new("F", 9), new("I", 9), new("F", 9), new("I", 9), new("I", 9), new("F", 9)
+    ts(m0, sl(cF, 0, 9), 16.0, ALU.mult, uF, ALU.add)
+    ts(m1, m0, -4.0, ALU.add, 1.0 / 9, ALU.mult)
+    ts(m3, m1, -9.0, ALU.mult)
+    tt(m3, m3, m0, ALU.add)
+    ts(m3, m3, 7.0, ALU.min)
+    ts(m4, m3, hF, ALU.add)
+    ts(m5, m4, 1, ALU.bitwise_and)
+    ts(m6, m5, 9.0, ALU.mult)
+    tt(m6, m6, m3, ALU.add)
+    ts(m6, m6, 16.0, ALU.mult)
+    tt(m6, m6, m1, ALU.add)
+    copy(pick9, m6)
+
+    uH, uB, uC, aH, aB, aC, fB, fC, bad = (new("B", 4096) for _ in range(9))
+    Z4, ZB4, ZC4 = new("B", 1024), new("B", 1024), new("B", 1024)
+    DD = new("B", 512)
+    D, us, uj, dl, eq, mkB, sgn = (new("B", 256) for _ in range(7))
+    QP, QG, TP, TG = new("F", 288), new("F", 288), new("F", 576), new("F", 576)
+    for qq in (QP, QG):
+        fill(qq, 0.0)
+    fill(sl(WIN, 2560, 2592), 0.0)
+    Pn, Gn = sl(QP, 16, 272), sl(QG, 16, 272)
+    PU, GU = new("U", 256), new("U", 256)
+    P9, PH9 = new("F", 288), new("F", 288)
+    CV = new("F", 512)
+    KO, krow, vals, dP, kt = (new("F", 256) for _ in range(5))
+    kt2, K1 = new("I", 256), new("I", 256)
+    PM, GM = new("H", 256), new("H", 256)
+    lv = [[new("F", 64), new("F", 64), new("F", 32), new("F", 16)] for _ in range(2)]
+    thr, thr2 = new("B", 16), new("B", 16)
+    joff, moff, zoff = (new("U", 16) for _ in range(3))
+    soff, cU = new("U", 32), new("U", 32)
+    kvU, scU = new("U", 32), new("U", 32)
+    kS, kE, kG, lo1, lo2, lo3, qI, vH, eI = (new("I", 16) for _ in range(9))
+    vI, cIi = new("I", 32), new("I", 32)
+    kFf, cpd, cpot, cb2, mult, ne15, lose, fin = (new("F", 16) for _ in range(8))
+    thrE, HH, mulB, addB, kv = (new("F", 32) for _ in range(5))
+    hcB = new("B", 32)
+    q3, r3 = new("F", 48), new("F", 48)
+    LL, LT, LO = new("F", 32), new("F", 32), new("F", 16)
+    acc, a256, ar = col(), col(), col()
+    aI, aI2 = col("I"), col("I")
+    fill(acc, 0.0)
+    fill(a256, 256.0)
+    fill(sl(mulB, 16, 32), 256.0)
+    ts(sl(addB, 16, 32), c16, 16.0, ALU.mult, uF, ALU.add)
+
+    def turn(t, qq, h):
+        tr(sl(t, 288 * h, 288 * h + 128), sl(qq, 16 + 128 * h, 144 + 128 * h))
+        tr(sl(t, 288 * h + 128, 288 * h + 288), sl(qq, 128 * h, 160 + 128 * h))
+        return part(t, h, 288)
+
+    copy(Gn, KI)
+    for h in range(2):
+        t = turn(TG, QG, h)
+        copy(part(KU, h, 128), ind(t, pickW))
+        act(part(K, h, 128), ind(t, pickW), AF.Copy)
+    copy(sl(LL, 0, 16), LI)
+    copy(sl(LL, 16, 32), LI)
+    tr(LT, LL)
+    copy(L, ind(LT, pickL))
+    copy(SW, SI)
+
+    def tree(out, a, h, e="V"):
+        b = lv[h]
+        move(e, b[0], sl(a, 64, 128))
+        tt(b[1], sl(a, 0, 64), b[0], ALU.min)
+        tt(b[2], sl(b[1], 0, 32), sl(b[1], 32, 64), ALU.min)
+        tt(b[3], sl(b[2], 0, 16), sl(b[2], 16, 32), ALU.min)
+        tt(part(out, h, 8), sl(b[3], 0, 8), sl(b[3], 8, 16), ALU.min)
+
+    def place(off, lo, k):
+        ts(lo, k, 255, ALU.bitwise_and)
+        ts(off, lo, 16.0, ALU.mult, uF, ALU.add)
+
+    def sums(ps, z, src, c, stop):
+        mm([(part(ps, c % 2, 64), zu(z, u), sl(src, 1024 * c + u, 1024 * c + 1024, 16), False, stop and u == 15) for u in range(16)])
+
+    def gathers(u, win, off, z4, c):
+        for i in (2 * c, 2 * c + 1):
+            tt(part(u, i, 512), ind(win, part(off, i, 32)), part(z4, c // 2, 512), ALU.subtract)
+
+    def over(src, c, onact):
+        if onact:
+            act(part(bad, c, 1024), part(src, c, 1024), AF.Sign, bm48, 1.0)
+        else:
+            ts(part(bad, c, 1024), part(src, c, 1024), 48.0, ALU.is_gt, 2.0, ALU.mult)
+
+    def minus(w, terms, c, d):
+        for b in range(2):
+            it = [(part(w, b, 512), l, part(s, 2 * c + b, 512)) for l, s in terms]
+            group(it + [(part(w, 4 * b + i, 128), IN, d) for i in range(4)])
+
+    def lanes(out, src, k0, sg, h, n):
+        return [(sl(out, (m + h) % 3, n, 3), sh(Y, sg * (k0 + m)), sl(src, (m + h) % 3, n, 3)) for m in range(3)]
+
+    def bcast(ps, th, stop):
+        mm([(part(ps, k, 8), IN, th, False, stop and k == 15) for k in range(16)])
+
+    def wsum(out, z, src):
+        return [(out, zu(z, u), sl(src, u, 256, 16)) for u in range(16)]
+
+    wb = [P["W0"], P["W1"]]
+    S2 = [P["SA"], P["SB"]]
+    M0, M1 = P["M0"], P["M1"]
+    M0a, M0b, M1a, M1b = sl(M0, 0, 256), sl(M0, 256, 512), sl(M1, 0, 256), sl(M1, 256, 512)
+    Mh = [M0, M1]
+
+    for rnd in range(3):
+        last = rnd == 2
+        win = Xb if rnd == 0 else XW
+        cz_ = CZ[rnd % 2]
+        Z = sl(cz_, 0, 256)
+        for h in range(1 if OPT["actg"] else 2):
+            z4 = part(Z4, h, 512)
+            e = "V" if rnd == 0 else OPT["z4"]
+            move(e, sl(z4, 0, 128), part(Z, h, 128))
+            move(e, sl(z4, 128, 256), part(Z, h, 128))
+            move(e, sl(z4, 256, 512), sl(z4, 0, 256))
+        act(thr, L, AF.Exp, b17, -LN2)
+        ts(ne15, L, 15.0, ALU.not_equal)
+        ts(sl(q3, 32, 48), L, 1.0, ALU.add)
+        tt(sl(q3, 32, 48), sl(q3, 32, 48), ne15, ALU.mult)
+        tt(sl(q3, 16, 32), sl(q3, 32, 48), L, ALU.subtract)
+        for h in range(2):
+            for zz, k0, w in ((ZB4, 1, part(wb[h], 0, 512)), (ZC4, 2, part(wb[h], 1, 512))):
+                z4 = part(zz, h, 512)
+                apart(lanes(part(w, 0, 128), part(Z, h, 128), k0, 1, h, 128))
+                act(sl(z4, 0, 128), part(w, 0, 128), AF.Copy)
+                move("G", sl(z4, 128, 256), sl(z4, 0, 128))
+                move("G", sl(z4, 256, 512), sl(z4, 0, 256))
+            ds, cs = sl(S2[h], 0, 128), sl(Mh[h], 0, 128)
+            mm([(ds, I1, part(cB, 0, 128), True, False)])
+            mm([(cs, BOc, part(sg1, h, 128), True, False)])
+            bcast(cs, part(thr, h, 8), False)
+            for c in (2 * h, 2 * h + 1):
+                if h == 1 and OPT["actg"]:
+                    act(part(uH, c, 1024), ind(win, part(KU, c, 64)), AF.Copy)
+                    minus(wb[c % 2], [(I1, uH)], c, part(Z, h, 128))
+                    act(part(aH, c, 1024), wb[c % 2], AF.Abs)
+                else:
+                    gathers(uH, win, KU, Z4, c)
+                    act(part(aH, c, 1024), part(uH, c, 1024), AF.Abs)
+                over(aH, c, c in OPT["sign1"])
+                sums(ds, Zd, aH, c, False)
+                sums(cs, Zc, bad, c, c % 2 == 1)
+            act(part(sgn, h, 128), cs, AF.Sign, bhalf, 1.0)
+            mm([(ds, IB, part(sgn, h, 128), False, True)])
+            tree(kS, ds, h, OPT["ev"])
+            so = sl(soff, 16 * h, 16 * h + 8)
+            place(so, part(lo1, h, 8), part(kS, h, 8))
+            Dh = part(D, h, 128)
+            move(OPT["dg"], Dh, ind(part(aH, h, 2048), so))
+            act(part(us, h, 128), ind(part(uH, h, 2048), so), AF.Copy)
+            apart(lanes(sl(Mh[h], 0, 128), Dh, 1, 1, h, 128) + lanes(sl(Mh[h], 128, 256), Dh, 2, 1, h, 128))
+            move(OPT["dd"], part(DD, h, 256), sl(Mh[h], 0, 256))
+            group(wsum(sl(Mh[h], 256, 272), Zv, part(DD, h, 256)))
+            tt(part(vI, h, 16), sl(Mh[h], 256, 272), c421, ALU.mult)
+            ts(part(cIi, h, 16), part(vI, h, 16), 2, ALU.arith_shift_right, 511, ALU.bitwise_and)
+            copy(part(cU, h, 16), part(cIi, h, 16))
+            for qq, t, o, c0, e in ((QP, TP, PU, 0, OPT["plist"]), (QG, TG, GU, 8, OPT["glist"])):
+                move(e, sl(qq, 16 + 128 * h, 144 + 128 * h), ind(SW, sl(cU, 16 * h + c0, 16 * h + c0 + 8)))
+                copy(part(o, h, 128), ind(turn(t, qq, h), pickW))
+            ts(part(cb2, h, 8), sl(cIi, 16 * h, 16 * h + 8), 2048.0, ALU.add)
+            act(part(P9, h, 144), ind(part(TP, h, 288), pick9), AF.Copy)
+        nw = [0]
+        for u, a, f, off, z4, dc, kk in ((uB, aB, fB, PU, ZB4, 0, kE), (uC, aC, fC, GU, ZC4, 1, kG)):
+            for h in range(2):
+                es = sl(S2[h], 0, 128)
+                mm([(es, I1, part(cB, h, 128), True, False)])
+                for c in (2 * h, 2 * h + 1):
+                    w = wb[nw[0] % 2]
+                    nw[0] += 1
+                    gathers(u, win, off, z4, c)
+                    if 4 * dc + c in OPT["relu"]:
+                        ts(part(a, c, 1024), part(u, c, 1024), 0.0, ALU.max)
+                        minus(w, [(I2, a), (IN, u)], c, part(DD, 2 * h + dc, 128))
+                    else:
+                        act(part(a, c, 1024), part(u, c, 1024), AF.Abs)
+                        minus(w, [(I1, a)], c, part(DD, 2 * h + dc, 128))
+                    act(part(f, c, 1024), w, AF.Abs)
+                    sums(es, Ze, f, c, c % 2 == 1)
+                tree(kk, es, h)
+            if dc == 0:
+                group(wsum(sl(M0, 0, 16), Zv, D))
+                copy(vH, sl(M0, 0, 16))
+                ts(qI, vH, 2, ALU.arith_shift_right, 2047, ALU.bitwise_and)
+                copy(sl(q3, 0, 16), qI)
+                group([(M1a, I1, quarter), (M1a, IH, us)] + [(part(M1a, h, 128), IH if h == 1 and OPT["actg"] else I1, part(Z, h, 128)) for h in range(2)])
+                ts(sl(cz_, 512, 768), M1a, MAGIC, ALU.add, MAGIC, ALU.subtract)
+                apart([(sl(M0, 144 * h + be, 144 * h + 144, 3), PF[(be + 2 * h) % 3], sl(P9, 144 * h + be, 144 * h + 144, 3)) for h in range(2) for be in range(3)])
+                act(PH9, sl(M0, 0, 288), AF.Copy)
+                tt(dP, ind(PH9, o9), K, ALU.subtract)
+                place(joff, lo2, kE)
+                act(uj, ind(uB, joff), AF.Copy)
+                nd = 128 if OPT["actg"] else 256
+                apart(lanes(M0a, uj, 1, -1, 0, nd))
+                group([(M0b, I1, Z)] + lanes(M0b, uj, 1, -1, 0, 256))
+                act(sl(dl, 0, nd), sl(M0a, 0, nd), AF.Copy)
+                act(sl(cz_, 256, 512), M0b, AF.Copy)
+                group([(M1a, I1, quarter), (M1a, IH, uj)] + [(part(M1a, h, 128), IH, s) for h in range(2) for s in (sl(ZB4, 512 * h, 512 * h + 128), part(DD, 2 * h, 128))])
+                ts(sl(CV, 0, 256), M1a, MAGIC, ALU.add, MAGIC, ALU.subtract)
+                tt(PM, ind(IBIG, joff), Pn, ALU.mult)
+                act(mkB, ind(IBIG, joff), AF.Copy)
+                group(wsum(sl(M1, 256, 272), Zh, PM))
+                ts(cpd, kE, 640.0 * 256, ALU.is_lt, 2592.0, ALU.mult)
+                ts(cpot, kE, 640.0 * 256, ALU.is_lt)
+                tt(sl(addB, 0, 16), sl(M1, 256, 272), cpd, ALU.max)
+                tt(sl(mulB, 0, 16), cb2, sl(addB, 0, 16), ALU.subtract)
+                ts(eI, kE, 0xFFFF00, ALU.bitwise_and)
+                ts(sl(thrE, 0, 16), eI, a256, ALU.add)
+                ts(sl(thrE, 16, 32), eI, a256, ALU.add)
+        copy(kFf, kG)
+        place(moff, lo3, kG)
+        apart([(sl(M1, 0, 16), sh(YF, -1), kFf), (sl(M1, 16, 32), sh(YF, -1), kFf)])
+        tt(HH, sl(M1, 0, 32), thrE, ALU.is_lt)
+        tt(kv, HH, mulB, ALU.mult)
+        tt(kv, kv, addB, ALU.add)
+        copy(kvU, kv)
+        copy(sl(hcB, 0, 16), sl(HH, 0, 16))
+        tt(sl(hcB, 16, 32), cpot, sl(HH, 0, 16), ALU.is_gt)
+        hit, con = sl(hcB, 0, 16), sl(hcB, 16, 32)
+        apart([(sl(M0, 16 * i + be, 16 * i + 16, 3), PB[be], sl(s, be, 16, 3)) for i, s in enumerate((hit, con, con)) for be in range(3)])
+        group([(sl(M0, 48, 64), I1, cz)] + [(sl(M0, 48 + be, 64, 3), PB[be], sl(s, be, 16, 3)) for s in (hit, hit, con) for be in range(3)])
+        ts(zoff, sl(M0, 48, 64), -256.0, ALU.mult, uF, ALU.add)
+        tt(r3, sl(M0, 0, 48), q3, ALU.mult)
+        ts(mult, sl(M0, 0, 16), 4.0, ALU.mult, 1.0, ALU.add)
+        act(thr2, sl(r3, 32, 48), AF.Exp, b17, -LN2)
+        if last:
+            tt(sl(LL, 0, 16), L, sl(r3, 16, 32), ALU.add)
+            tt(sl(LL, 16, 32), L, sl(r3, 16, 32), ALU.add)
+            tr(LT, LL)
+            copy(LO, ind(LT, pickL))
+        else:
+            tt(L, L, sl(r3, 16, 32), ALU.add)
+        Z = sl(CZ[(rnd + 1) % 2], 0, 256)
+        act(Z, ind(cz_, zoff), AF.Copy)
+        tt(GM, ind(IBIG, moff), Gn, ALU.mult)
+        group([(M1b, sh(BOh, -1), GM), (M1b, BOn, PM)])
+        tt(M1b, M1b, mkB, ALU.mult)
+        tt(sl(CV, 256, 512), M1b, Pn, ALU.add)
+        move(OPT["krow"], krow, ind(IOTA, sl(kvU, 0, 16)))
+        act(vals, ind(CV, sl(kvU, 16, 32)), AF.Copy)
+        tt(eq, ind(sl(kv, 0, 16), repb), krow, ALU.is_equal)
+        tt(eq2, ind(sl(kv, 0, 16), repo), krow, ALU.is_equal)
+        mm([(sl(M1, 0, 16), sh(YF, 0), sl(kv, 0, 16), True, False)] + [(sl(M1, 0, 16), part(tri, u, 128), sl(eq, u, 256, 16), False, False) for u in range(16)])
+        mm([(sl(M1, 0, 16, 2), zu(Z1, u), sl(eq2, u, 256, 32), False, u == 15) for u in range(16)])
+        ts(sl(scU, 0, 16, 2), sl(M1, 0, 16, 2), spare, ALU.min)
+        ts(sl(scU, 1, 16, 2), sl(M1, 1, 16, 2), spare2, ALU.min)
+        for b in range(8):
+            copy(ind(WIN, part(scU, b, 2)), part(vals, b, 32))
+        if not last:
+            apart([(sl(M0, 64, 80), BO1, hit)])
+            add("V", lambda: g.vector.tensor_reduce(ap(ar), ap(sl(M0, 64, 80)), AX.X, ALU.add), [sl(M0, 64, 80)], [ar], 0.07)
+            tt(acc, acc, ar, ALU.add)
+            copy(aI, acc)
+            ts(aI2, aI, 31, ALU.bitwise_and)
+            ts(a256, aI2, 1.0, ALU.add, 256.0, ALU.mult)
+        tt(kt, ind(mult, repk), K, ALU.mult)
+        tt(kt2, ind(sl(r3, 0, 16), repk), kt, ALU.add)
+        ts(K1, kt2, 2047, ALU.bitwise_and)
+        for h in range(2):
+            cs = sl(S2[h], 0, 128)
+            mm([(cs, BOc, part(sg6, h, 128), True, False)])
+            for c in (2 * h, 2 * h + 1):
+                w = wb[nw[0] % 2]
+                nw[0] += 1
+                minus(w, [(I1, uH)], c, sl(cz_, 384, 512) if h == 1 and OPT["actg"] else part(dl, h, 128))
+                act(part(aB, c, 1024), w, AF.Abs)
+                over(aB, c, c in OPT["sign6"])
+                sums(cs, Zc, bad, c, False)
+            bcast(cs, part(thr2, h, 8), True)
+            ts(cs, cs, 0.0, ALU.is_ge)
+            tt(cs, cs, part(dP, h, 128), ALU.mult)
+            tt(part(K, h, 128), cs, part(K1, h, 128), ALU.add)
+            if not last:
+                copy(part(KU, h, 128), part(K, h, 128))
+
+    copy(Pn, ind(K, reord))
+    tr(sl(TP, 0, 256), sl(QP, 16, 272))
+    tr(sl(TP, 256, 544), sl(QP, 0, 288))
+    copy(KO, ind(sl(TP, 0, 544), pickN))
+    for ci, e, k, src, us_ in ((5, "S", "oz", Z, 0.3), (5, "S", "ol", LO, 0.1), (6, "G", "ox", XW, 1.5), (7, "S", "oa", SW, 0.8), (8, "S", "ok", KO, 0.4)):
+        dma(e, T["s" + k][:], ap(src), [src], [("s" + k, 0, 8)], us_)
+        own("S", k, T["s" + k][0 if k == "ol" else rank], [("s" + k, 0, 8)])
+        if k != "oz":
+            remote(ci)
+    for ci, e, k, y, us_ in ((5, "A", "oz", T.yz, 0.3), (5, "A", "ol", T.yl, 0.1), (6, "A", "ox", T.yx, 1.5), (7, "A", "oa", T.ya, 0.8), (8, "S", "ok", T.yk, 0.4)):
+        src = T.lol[:, rows, :] if k == "ol" else T["l" + k][:]
+        dma(e, y[:], src, [("l" + k, 0, 8), ("call%d" % ci, 0, 1)] + ([K] if e == "A" else []), [("y" + k, 0, 1)], us_, ext=arr(ci))
+    ops[0]["end"] = [(T.sem.sent, sent[0])]
+    return ops

@@ -2,7 +2,7 @@ import math
 from concourse.bass import DstId, RemoteDMATransfer
 from concourse.mybir import AluOpType as ALU, AxisListType as AX, ActivationFunctionType as AF
 
-NF, NB, NI, NU, NH = 16384, 57344, 3072, 2048, 1536
+NF, NB, NI, NU, NH = 19456, 69632, 3072, 1536, 1024
 SCRATCH = {
     "F": ("sbuf", [128, NF], "float32"), "B": ("sbuf", [128, NB], "bfloat16"), "I": ("sbuf", [128, NI], "int32"),
     "U": ("sbuf", [128, NU], "uint16"), "H": ("sbuf", [128, NH], "float16"),
@@ -11,16 +11,20 @@ SCRATCH = {
     "M0": ("psum", [128, 512], "float32"), "M1": ("psum", [128, 512], "float32"),
 }
 KINDS = {"iz": (32, "bfloat16"), "il": (16, "int32"), "ik": (32, "int32"), "ix": (128, "bfloat16"), "iy": (128, "bfloat16"), "ia": (64, "int32"),
-         "oz": (32, "bfloat16"), "ol": (16, "float32"), "ox": (256, "bfloat16"), "oa": (64, "float32"), "ok": (32, "float32")}
-CALLS = [("iz", "il"), ("ik",), ("ix",), ("iy",), ("ia",), ("oz", "ol"), ("ox",), ("oa",), ("ok",)]
+         "oz": (32, "bfloat16"), "ol": (16, "float32"), "ox": (128, "bfloat16"), "oy": (128, "bfloat16"), "oa": (64, "float32"), "ok": (32, "float32")}
+CALLS = [("iz", "il"), ("ik",), ("ix",), ("iy",), ("ia",), ("oz", "ol"), ("oa",), ("ox",), ("oy",), ("ok",)]
 for _k, (_n, _d) in KINDS.items():
     SCRATCH["s" + _k] = ("dram", [1 if _k[1] == "l" else 8, 128, _n], _d)
     SCRATCH["l" + _k] = ("dram", [8, 128, _n], _d)
-NDMA = 40
+NDMA = 44
 SEMAPHORES = ["cV", "cA", "cP", "cG", "sent"] + ["arr%d" % i for i in range(len(CALLS))] + ["d%d" % i for i in range(NDMA)]
 PSUM = ("W0", "W1", "SA", "SB", "M0", "M1")
 MAGIC = 12582912.0
-OPT = {"sign1": (), "sign6": (), "relu": (5, 7), "krow": "A", "plist": "A", "glist": "A", "dd": "V", "lat": 0.1, "ga": 1.56, "actg": 1, "z4": "G", "ev": "V", "dg": "V", "iters": 2400, "amp": 0.5}
+MAGIC128 = 1610612736.0
+OPT = {"rawH": (1,), "rawB": (), "rawC": (), "relu": (), "s6": "VVPP", "thr": "PP", "gw": 512,
+       "red": ("H0", "C1"), "cut": (), "order": ("B0", "C0", "B1", "S0", "C1", "D0", "S1", "D1"), "dd": "VA", "kg": "A", "ev": "V", "dg": "VV", "plist": "VA", "glist": "AA",
+       "cases": ((1.45, 2.0, 0.15), (1.25, 1.56, 0.3)), "slack": 1.0, "tied": 4, "moves": 0, "heat": 0.1, "s6bank": ("SA", "M0"), "pbank": "SB",
+       "pen": "VA", "rnd": "V", "kh": "VV", "hop": 5.0, "lat": 0.22, "ga": 1.56, "iters": 2000, "amp": 0.5}
 
 
 def routes(T, topo):
@@ -122,19 +126,20 @@ def arrange(ops):
         for acc, isw in [(a, False) for a in o["r"]] + [(a, True) for a in o["w"]]:
             name, lo, hi = acc[0], acc[1], acc[2]
             ps = name in PSUM
+            st = acc[3] if len(acc) > 3 and not ps else 1
             if ps:
                 lo, hi = lo // 512 * 512, (hi + 511) // 512 * 512
             for bk in range(lo // 256, (hi - 1) // 256 + 1):
                 keep = []
-                for (j, l2, h2, w2) in hist.get((name, bk), []):
-                    hit = l2 < hi and lo < h2
+                for (j, l2, h2, w2, s2) in hist.get((name, bk), []):
+                    hit = l2 < hi and lo < h2 and not (st == s2 and (lo - l2) % st)
                     same = ops[j]["e"] == o["e"] and not (o["dma"] or ops[j]["dma"])
                     if j != i and hit and (isw or w2 or (ps and not same)):
                         p[j] = p.get(j, False) or not ((same and o["e"] == "P") or name.startswith("call"))
-                    cover = lo <= max(l2, 256 * bk) and min(h2, 256 * bk + 256) <= hi
+                    cover = st == 1 and lo <= max(l2, 256 * bk) and min(h2, 256 * bk + 256) <= hi
                     if not (hit and isw and cover and j != i and not (ps and same and w2 and o["e"] != "P")):
-                        keep.append((j, l2, h2, w2))
-                keep.append((i, lo, hi, isw))
+                        keep.append((j, l2, h2, w2, s2))
+                keep.append((i, lo, hi, isw, st))
                 hist[(name, bk)] = keep
         preds.append(p)
     succ = [[] for _ in range(n)]
@@ -170,42 +175,132 @@ def arrange(ops):
             end[i] = t + c[i]
         return end
 
-    def feasible(key, dep, nxt):
-        left = [len(d) for d in dep]
+    def feasible(key, dep, forward):
         k2 = list(key)
-        for i in sorted(range(n), key=lambda i: topo_pos(i, dep is fw)):
+        for i in (range(n) if forward else range(n - 1, -1, -1)):
             for j, d in dep[i]:
                 if k2[j] >= k2[i]:
                     k2[i] = k2[j] + 1e-7
         return sorted(range(n), key=lambda i: k2[i])
 
-    def topo_pos(i, forward):
-        return i if forward else -i
     zero, tailx = [0.0] * n, [o["x"] for o in ops]
     prio = [0.0] * n
     for i in range(n - 1, -1, -1):
         prio[i] = c[i] + max([prio[k] + d for k, d in bw[i]] + [ops[i]["x"]])
+    cases = []
+    for f, ga, wake in OPT["cases"]:
+        cc = [c[i] if ops[i]["dma"] or ops[i]["ext"] or ops[i]["x"] > 1 else f * (c[i] + ops[i]["g"] * (ga - OPT["ga"])) for i in range(n)]
+        cases.append((cc, [[(j, d + wake - lat if preds[k][j] else d) for j, d in fw[k]] for k in range(n)]))
+
+    def replay(seq, cc, dep):
+        end, free = [0.0] * n, {e: 0.0 for e in "VAPGS"}
+        for i in seq:
+            t = free[eng[i]]
+            for j, d in dep[i]:
+                if end[j] + d > t:
+                    t = end[j] + d
+            end[i] = free[eng[i]] = t + cc[i]
+        return max(end[i] + tailx[i] for i in outs)
+    outs = [i for i in range(n) if not succ[i]]
+    twins = {}
+    for i, o in enumerate(ops):
+        twins.setdefault(o["tie"], []).append(i)
     key, best, seed = [-p for p in prio], None, 12345
     for it in range(OPT["iters"]):
-        end = place(feasible(key, fw, bw), fw, zero)
-        span = max(end[i] + tailx[i] for i in range(n))
-        if best is None or span <= best[0]:
-            best = (span, end)
+        end = place(feasible(key, fw, True), fw, zero)
+        span = max(end[i] + tailx[i] for i in outs)
+        if best is None or span <= best[2] + OPT["slack"]:
+            seq = sorted(range(n), key=lambda i: (end[i] - c[i], i))
+            tot = span + sum(replay(seq, cc, dep) for cc, dep in cases)
+            if best is None or tot <= best[0]:
+                best = (tot, end, span)
         src = best[1] if it % 2 == 1 else end
         noise = [0.0] * n
         if it % 2 == 1:
             seed = (seed * 1103515245 + 12345) % 2147483648
-            lo = best[0] * seed / 2147483648.0 - 4.0
+            lo = best[2] * seed / 2147483648.0 - 4.0
             amp = OPT["amp"] * (1 + seed // 64 % 6)
+            tied = seed // 1024 % 4 < OPT["tied"]
             for i in range(n):
                 if lo < src[i] < lo + 8.0:
                     seed = (seed * 1103515245 + 12345) % 2147483648
-                    noise[i] = amp * (seed / 2147483648.0 - 0.5)
-        back = place(feasible([-src[i] + noise[i] for i in range(n)], bw, fw), bw, tailx)
+                    for j in (twins[ops[i]["tie"]] if tied else (i,)):
+                        noise[j] = amp * (seed / 2147483648.0 - 0.5)
+        back = place(feasible([-src[i] + noise[i] for i in range(n)], bw, False), bw, tailx)
         key = [-back[i] for i in range(n)]
-    start = [best[1][i] - c[i] for i in range(n)]
-    fin = [best[1][i] + tailx[i] for i in range(n)]
-    order = feasible(start, fw, bw)
+    order = feasible([best[1][i] - c[i] for i in range(n)], fw, True)
+    cases = [(c, fw)] + cases
+    qi = ["VAPGS".index(e) for e in eng]
+
+    def times(seq, cc, dep, old, k0):
+        end, why = (list(old[0]), list(old[1])) if old else ([0.0] * n, [-1] * n)
+        lastq = [-1] * 5
+        k, miss = k0 - 1, 5
+        while k >= 0 and miss:
+            if lastq[qi[seq[k]]] < 0:
+                lastq[qi[seq[k]]] = seq[k]
+                miss -= 1
+            k -= 1
+        for k in range(k0, n):
+            i = seq[k]
+            w = lastq[qi[i]]
+            t = end[w] if w >= 0 else 0.0
+            for j, d in dep[i]:
+                if end[j] + d > t:
+                    t, w = end[j] + d, j
+            end[i], why[i] = t + cc[i], w
+            lastq[qi[i]] = i
+        e = max(outs, key=lambda i: end[i] + tailx[i])
+        return end, why, end[e] + tailx[e], e
+
+    cur = [times(order, cc, dep, None, 0) for cc, dep in cases]
+    tot = sum(x[2] for x in cur)
+    keep = (tot, order, cur[0][0])
+    for it in range(OPT["moves"]):
+        seed = (seed * 1103515245 + 12345) % 2147483648
+        end, why, span, i = cur[seed // 4096 % len(cases)]
+        arcs = []
+        while why[i] >= 0:
+            if qi[why[i]] == qi[i] and why[i] not in preds[i]:
+                arcs.append(i)
+            i = why[i]
+        if not arcs:
+            break
+        seed = (seed * 1103515245 + 12345) % 2147483648
+        v = arcs[seed // 256 % len(arcs)]
+        b = order.index(v)
+        a = order.index(why[v])
+        for _ in range(seed // 16 % 3):
+            k = a - 1
+            while k >= 0 and qi[order[k]] != qi[v]:
+                k -= 1
+            if k >= 0:
+                a = k
+        must, lastq, ok = set(preds[v]), set(), True
+        front = []
+        for k in range(b - 1, a - 1, -1):
+            i = order[k]
+            if i in must or qi[i] in lastq:
+                if qi[i] == qi[v]:
+                    ok = False
+                    break
+                front.append(i)
+                lastq.add(qi[i])
+                must.update(preds[i])
+        if not ok:
+            continue
+        moved = set(front)
+        seq = order[:a] + front[::-1] + [v] + [i for i in order[a:b] if i not in moved] + order[b + 1:]
+        new = [times(seq, cc, dep, cur[k], a) for k, (cc, dep) in enumerate(cases)]
+        t2 = sum(x[2] for x in new)
+        seed = (seed * 1103515245 + 12345) % 2147483648
+        if t2 <= tot - OPT["heat"] * (1.0 - it / OPT["moves"]) * math.log((seed + 1) / 2147483649.0):
+            order, cur, tot = seq, new, t2
+            if tot < keep[0]:
+                keep = (tot, order, cur[0][0])
+    order = keep[1]
+    start = [keep[2][i] - c[i] for i in range(n)]
+    fin = [keep[2][i] + tailx[i] for i in range(n)]
     pos, cnt = {}, {e: 0 for e in "VAPGS"}
     for i in order:
         cnt[ops[i]["e"]] += 1
@@ -244,7 +339,6 @@ def emit(g, T, ops):
     num, cnt, nd, tail = {}, {e: 0 for e in "VAPG"}, 0, []
     for i in order:
         o = ops[i]
-        o["st"], o["fin"] = start[i], fin[i]
         for j in waits[i]:
             q[o["e"]].wait_ge(num[j][0], num[j][1])
         for sem, v in o["ext"]:
@@ -271,12 +365,16 @@ def build(g, core, rank, T, topo, way):
     top = {"F": 0, "B": 0, "I": 0, "U": 0, "H": 0}
     CY, GA, PC = 0.00083, OPT["ga"], 0.00042
     two = ("B", "U", "H")
+    tie = ["once", 0]
 
     def new(pool, n):
         lo = top[pool]
         top[pool] = lo + (n + 15) // 16 * 16
         assert top[pool] <= SCRATCH[pool][1][1], pool
         return (pool, lo, lo + n, 1)
+
+    def pair(pool, n):
+        return [new(pool, n), new(pool, n)]
 
     def sl(r, a, b, s=1):
         return (r[0], r[1] + a, r[1] + b, s)
@@ -315,7 +413,9 @@ def build(g, core, rank, T, topo, way):
                 rr.append(a[2])
             else:
                 ww.append(a)
-        ops.append({"e": e, "f": f, "r": rr, "w": ww, "c": c, "x": x, "dma": dma, "ext": list(ext), "end": []})
+        gathered = sum(16 * width(a[2]) * CY for a in r if isref(a) and a[0] == "ind")
+        tie[1] += 1
+        ops.append({"e": e, "f": f, "r": rr, "w": ww, "c": c, "x": x, "dma": dma, "ext": list(ext), "end": [], "g": gathered, "tie": tuple(tie)})
 
     def vcost(out, a, k=1.0):
         if a[0] == "ind":
@@ -346,13 +446,22 @@ def build(g, core, rank, T, topo, way):
     def fill(out, v):
         add("V", lambda: g.vector.memset(ap(out), v), [], [out], vcost(out, out))
 
+    def reduce(out, a, op):
+        add("V", lambda: g.vector.tensor_reduce(ap(out), ap(a), AX.X, op), [a], [out], 0.07)
+
     def act(out, a, fn, bias=None, scale=None):
         def f():
-            if bias is None:
+            if bias is None and scale is None:
                 return g.scalar.activation(ap(out), ap(a), fn)
+            if bias is None:
+                return g.scalar.activation(ap(out), ap(a), fn, scale=val(scale))
             return g.scalar.activation(ap(out), ap(a), fn, bias=val(bias), scale=scale)
         c = 0.065 + width(out) * GA * CY if a[0] == "ind" else 0.1 + max(64, width(out)) * CY
-        add("A", f, [a, bias], [out], c)
+        add("A", f, [a, bias, scale], [out], c)
+
+    def scaled(out, a, w):
+        act(out, a, AF.Identity, None, w)
+        return out
 
     def move(e, out, a):
         if e == "A":
@@ -400,7 +509,8 @@ def build(g, core, rank, T, topo, way):
             sent[0] += len(es)
         add("G", lambda: g.remote_dma_fused(trs, local_sem=T.sem.sent), [("s" + k, 0, 8) for k in CALLS[ci]] + [("callo", 0, 1)],
             [("call%d" % ci, 0, 1), ("callo", 0, 1)], 1.0, x=0.0)
-        add("G", lambda: None, [("call%d" % ci, 0, 1)], [("call%d" % ci, 0, 1)], 0.0, x=7.0)
+        add("G", lambda: None, [("call%d" % ci, 0, 1)], [("call%d" % ci, 0, 1)], 0.0,
+            x=OPT["hop"] + KINDS[CALLS[ci][0]][0] / 64.0)
 
     def arr(ci):
         return [(T.sem["arr%d" % ci], arrivals(T, topo, way, rank, ci))]
@@ -411,14 +521,16 @@ def build(g, core, rank, T, topo, way):
     P = {k: (k, 0, SCRATCH[k][1][1], 1) for k in PSUM}
     rows = slice(16 * rank, 16 * rank + 16)
 
-    WIN = new("F", 2592)
-    XW, SW = sl(WIN, 0, 2048), sl(WIN, 2048, 2560)
+    X0 = 2080
+    WIN = new("F", 2 * X0)
+    XW, SW = sl(WIN, X0, X0 + 2048), sl(WIN, 0, 512)
     Xb = new("B", 2048)
-    CZ = [new("B", 768), new("B", 768)]
-    K, L = new("F", 256), new("F", 16)
-    KU = new("U", 256)
+    CZ = [pair("B", 512), pair("B", 512)]
+    KW = [pair("F", 384), pair("F", 384)]
+    L = new("F", 16)
+    KU, LU = new("U", 256), new("U", 16)
     KI, LI, SI = new("I", 256), new("I", 16), new("I", 512)
-    Z = sl(CZ[0], 0, 256)
+    ZO, KO = new("B", 256), new("F", 256)
 
     dma("S", T["six"][:], T.x0[:, 0:1024], [], [("six", 0, 8)], 0.8)
     dma("S", T.siy[:], T.x0[:, 1024:2048], [], [("siy", 0, 8)], 1.5)
@@ -434,9 +546,9 @@ def build(g, core, rank, T, topo, way):
     own("S", "ia", T.asc[rows, :], [])
     for ci in range(5):
         remote(ci)
-    dma("A", ap(Z), T.liz[:], [("liz", 0, 8), ("call0", 0, 1)], [Z], 0.3, ext=arr(0))
-    dma("A", ap(LI), T.lil[:, rows, :], [("lil", 0, 8), ("call0", 0, 1)], [LI], 0.1, ext=arr(0))
-    dma("A", ap(KI), T.lik[:], [("lik", 0, 8), ("call1", 0, 1)], [KI], 0.4, ext=arr(1))
+    dma("S", ap(ZO), T.liz[:], [("liz", 0, 8), ("call0", 0, 1)], [ZO], 0.3, ext=arr(0))
+    dma("S", ap(LI), T.lil[:, rows, :], [("lil", 0, 8), ("call0", 0, 1)], [LI], 0.1, ext=arr(0))
+    dma("S", ap(KI), T.lik[:], [("lik", 0, 8), ("call1", 0, 1)], [KI], 0.4, ext=arr(1))
     for h, k in enumerate(("lix", "liy")):
         dma("S", ap(part(Xb, h, 1024)), T[k][:], [(k, 0, 8), ("call%d" % (2 + h), 0, 1)], [part(Xb, h, 1024)], 0.8, ext=arr(2 + h))
     dma("S", ap(SI), T.lia[:], [("lia", 0, 8), ("call4", 0, 1)], [SI], 0.8, ext=arr(4))
@@ -446,7 +558,7 @@ def build(g, core, rank, T, topo, way):
     pI, cI = new("I", 1), new("I", 256)
     iota(pI)
     iota(cI)
-    IOTA = new("F", 2608)
+    IOTA = new("F", 2 * X0 + 16)
     iota(IOTA, [("callo", 0, 1)])
     cF = new("F", 256)
     copy(cF, cI)
@@ -467,26 +579,33 @@ def build(g, core, rank, T, topo, way):
     hF = icol(pI, 4, ALU.arith_shift_right, 1, ALU.bitwise_and)
     u7 = icol(pI, 7, ALU.bitwise_and)
     u8 = icol(pI, 3, ALU.arith_shift_right, 1, ALU.bitwise_and)
+    pm = col("I")
+    ts(pm, pI, 112.0, ALU.add)
+    kM = icol(pm, 112, ALU.bitwise_and)
     ones = new("B", 128)
     fill(ones, 1.0)
-    k16 = col()
+    k16, k16m = col(), col()
     ts(k16, kF, 16.0, ALU.add)
-    wcb, wc, wv = col("B"), col(), col()
+    ts(k16m, kM, 16.0, ALU.add)
+    wcb, wc, wqb, wq, wv = col("B"), col(), col("B"), col(), col()
     LN2 = math.log(2.0)
-    b15, b17, bm48, bhalf = col(), col(), col(), col()
+    b15, b17, b21, b30 = col(), col(), col(), col()
     fill(b15, 15 * LN2)
     fill(b17, 17 * LN2)
-    fill(bm48, -48.5)
-    fill(bhalf, 0.5)
+    fill(b21, 21 * LN2)
+    fill(b30, 30 * LN2)
     act(wcb, uF, AF.Exp, b15, -LN2)
     copy(wc, wcb)
+    act(wqb, uF, AF.Exp, b21, -3 * LN2)
+    copy(wq, wqb)
     ts(wv, uF, 15.0, ALU.mult, 7.0, ALU.add)
 
-    def slide(pool, w):
+    def slide(pool, w, at=k16):
         z = new(pool, 160)
-        ts(z, sl(cF, 0, 160), k16, ALU.is_equal, w, ALU.mult)
+        ts(z, sl(cF, 0, 160), at, ALU.is_equal, w, ALU.mult)
         return z
-    Zd, Ze, Zc, Zv, Zh, Z1 = slide("B", -256.0), slide("B", 256.0), slide("B", wc), slide("B", wv), slide("H", 1.0), slide("B", 4096.0)
+    Z0, Zh, Zf = slide("B", 1.0), slide("H", 1.0), slide("B", 256.0, k16m)
+    Zd, Zc, Zv, Ze, Z1, Zq = (scaled(new("B", 160), Z0, w) for w in (-256.0, wc, wv, 256.0, 8192.0, wq))
 
     def zu(z, u):
         return sl(z, 16 - u, 144 - u)
@@ -494,7 +613,7 @@ def build(g, core, rank, T, topo, way):
     gt16 = new("F", 16)
     ts(gt16, c16, uF, ALU.is_lt)
     for u in range(16):
-        ts(part(tri, u, 128), zu(Z1, u), sl(gt16, u, u + 1), ALU.mult)
+        scaled(part(tri, u, 128), zu(Z1, u), sl(gt16, u, u + 1))
     c127I, c127 = new("I", 256), new("F", 256)
     ts(c127I, cI, 127, ALU.bitwise_and)
     copy(c127, c127I)
@@ -508,16 +627,34 @@ def build(g, core, rank, T, topo, way):
     def sh(y, k):
         k %= 8
         return sl(y, 128 - 16 * k, 256 - 16 * k)
-    I1, IN, IH, I2, IB = sh(Y, 0), sh(shifts("B", -1.0, 128), 0), sh(shifts("B", 0.5, 128), 0), sh(shifts("B", 2.0, 128), 0), sh(shifts("B", 524288.0, 128), 0)
-    c112I, c112 = new("I", 256), new("F", 256)
-    ts(c112I, cI, 112, ALU.bitwise_and)
+
+    def eye(pool, w):
+        return scaled(new(pool, 128), sh(Y, 0), w)
+    I1, IN, IH, I2, IS, ISN = sh(Y, 0), eye("B", -1.0), eye("B", 0.5), eye("B", 2.0), eye("B", 1.3125), eye("B", -1.3125)
+    INF, I20, I5 = eye("F", -1.0), eye("F", 20.0), eye("F", 5.0)
+    IB, IR, IRN, IR2 = eye("B", 524288.0), eye("B", MAGIC), eye("B", -MAGIC), eye("B", 2048.0 * MAGIC)
+    bR, bR2, bhalf = col(), col(), col()
+    fill(bR, -MAGIC)
+    fill(bR2, -2048.0 * MAGIC)
+    fill(bhalf, 0.5)
+    IM, I2K, ones4, bM = eye("B", MAGIC128), eye("B", float(X0)), new("B", 512), col()
+    fill(ones4, 1.0)
+    fill(bM, -MAGIC128)
+    c112I, c112 = new("I", 128), new("F", 128)
+    ts(c112I, sl(cI, 0, 128), 112, ALU.bitwise_and)
     copy(c112, c112I)
-    BOh, BOn, BOc, BO1 = new("H", 256), new("H", 128), new("B", 128), new("B", 128)
+    BOh, BOn, BOv, BO1 = new("H", 128), new("H", 128), new("B", 128), new("B", 128)
     ts(BOh, c112, kF, ALU.is_equal)
-    ts(BOn, sl(c112, 0, 128), kF, ALU.is_equal, -1.0, ALU.mult)
-    ts(BOc, sl(c112, 0, 128), kF, ALU.is_equal, wc, ALU.mult)
-    ts(BO1, sl(c112, 0, 128), kF, ALU.is_equal)
-    PB, PF = [], []
+    ts(BOn, c112, kF, ALU.is_equal, -1.0, ALU.mult)
+    ts(BO1, c112, kF, ALU.is_equal)
+    scaled(BOv, BO1, wv)
+    BOq = scaled(new("B", 128), BOv, 0.25)
+    c38, c1k = new("B", 128), new("B", 128)
+    fill(c38, -0.375)
+    fill(c1k, -1024.0)
+    BO0 = new("B", 128)
+    fill(BO0, 0.0)
+    PB, PN = [], []
     for be in range(3):
         qi, tc, t2, t3 = col("I"), col(), col("I"), col("I")
         ts(qi, uF, 1.0 / 3, ALU.mult, (be - 1) / 3.0, ALU.add)
@@ -525,352 +662,426 @@ def build(g, core, rank, T, topo, way):
         ts(t2, uF, -15.0, ALU.mult, tc, ALU.add)
         ts(t3, t2, float(128 - 16 - 16 * be), ALU.add)
         t4 = icol(t3, 127, ALU.bitwise_and)
-        pb, pf = new("B", 128), new("F", 128)
+        pb, pn = new("B", 128), new("B", 128)
         ts(pb, sl(cF, 0, 128), t4, ALU.is_equal)
-        ts(pf, sl(cF, 0, 128), t4, ALU.is_equal)
+        scaled(pn, pb, -1.0)
         PB.append(pb)
-        PF.append(pf)
+        PN.append(pn)
     eq16 = new("F", 16)
     ts(eq16, c16, uF, ALU.is_equal)
-    IBIG = new("B", 4096)
+    IBIG = new("B", 2048)
     for j in range(16):
-        ts(part(IBIG, j, 128), ones, sl(eq16, j, j + 1), ALU.mult)
-    copy(part(IBIG, 1, 2048), part(IBIG, 0, 2048))
-    cB = new("B", 256)
-    copy(cB, cF)
-    quarter = new("B", 256)
+        scaled(part(IBIG, j, 128), ones, sl(eq16, j, j + 1))
+    cB = new("B", 128)
+    copy(cB, sl(cF, 0, 128))
+    quarter = new("B", 128)
     fill(quarter, -0.25)
-    sg1, sg6 = new("B", 256), new("B", 256)
-    for s, ch in ((sg1, OPT["sign1"]), (sg6, OPT["sign6"])):
-        for c in range(4):
-            fill(part(s, c, 64), 1.0 if c in ch else 0.0)
     cz = new("B", 16)
-    ts(cz, c16, -1.0 / 16, ALU.mult, -2.0, ALU.add)
-    spare = col()
-    ts(spare, uF, 2560.0, ALU.add)
-    spare2, repo, ro1, eq2 = col(), new("U", 16), new("I", 16), new("B", 256)
-    ts(spare2, uF, 2576.0, ALU.add)
-    ts(ro1, sl(cI, 0, 16), 14, ALU.bitwise_and)
-    ts(repo, ro1, 1.0, ALU.add)
+    for i in range(2):
+        ts(part(cz, i, 8), sl(cF, 0, 8), 0.125, ALU.mult)
+    spare, spare2 = col(), col()
+    ts(spare, uF, X0 + 2048.0, ALU.add)
+    ts(spare2, uF, X0 + 2064.0, ALU.add)
     c421 = new("F", 16)
     fill(sl(c421, 0, 8), 4.0)
     fill(sl(c421, 8, 16), 21.0)
-    repb, repk, o9, reord, pickN = (new("U", 16) for _ in range(5))
-    pickW, pick9, pickL = new("U", 8), new("U", 9), new("U", 1)
-    copy(repb, c16)
-    e1, e2, e3, e4, e5 = new("I", 16), new("F", 16), col(), col(), col()
-    ts(e1, sl(cI, 0, 16), 8, ALU.bitwise_and)
-    ts(repk, e1, u7, ALU.add)
-    ts(e3, u8, 9.0, ALU.mult, u7, ALU.add)
-    ts(o9, c16, 18.0, ALU.mult, e3, ALU.add)
-    ts(e2, e1, 15.0, ALU.mult)
-    tt(e2, e2, c16, ALU.add)
-    ts(e4, uF, 8.0, ALU.mult)
-    ts(reord, e2, e4, ALU.add)
-    s1 = col("I")
+    THR, l1, l2 = new("F", 16), new("F", 16), new("F", 16)
+    ts(l1, c16, 15.0, ALU.not_equal)
+    ts(l2, c16, 1.0, ALU.add)
+    tt(l2, l2, l1, ALU.mult)
+    act(THR, l2, AF.Exp, b30, -3 * LN2)
+    repb, repo, repk, pickW = (new("U", 8) for _ in range(4))
+    pickL = new("U", 1)
+    copy(repb, sl(cF, 0, 8))
+    ro1 = new("I", 8)
+    ts(ro1, sl(cI, 0, 8), 6, ALU.bitwise_and)
+    ts(repo, ro1, 1.0, ALU.add)
+    ts(repk, sl(cF, 0, 8), 0.0, ALU.mult, u7, ALU.add)
+    s1, s3, e5 = col("I"), col(), col()
     tt(s1, uF, hF, ALU.add)
     s2 = icol(s1, 1, ALU.bitwise_and)
-    s3 = col()
     ts(e5, u7, 16.0, ALU.mult, u8, ALU.add)
     ts(s3, s2, 144.0, ALU.mult, e5, ALU.add)
     ts(pickW, sl(cF, 0, 8), 2.0, ALU.mult, s3, ALU.add)
     ts(pickL, hF, 16.0, ALU.mult, uF, ALU.add)
-    n1, n2, n3 = new("I", 16), new("I", 16), new("F", 16)
-    ts(n1, c16, hF, ALU.add)
-    ts(n2, n1, 1, ALU.bitwise_and)
-    ts(n3, n2, 17.0, ALU.mult)
-    tt(n3, n3, c16, ALU.add)
-    ts(pickN, n3, 16.0, ALU.mult, uF, ALU.add)
-    m0, m1, m3, m4, m5, m6 = new("F", 9), new("I", 9), new("F", 9), new("I", 9), new("I", 9), new("F", 9)
-    ts(m0, sl(cF, 0, 9), 16.0, ALU.mult, uF, ALU.add)
-    ts(m1, m0, -4.0, ALU.add, 1.0 / 9, ALU.mult)
-    ts(m3, m1, -9.0, ALU.mult)
-    tt(m3, m3, m0, ALU.add)
-    ts(m3, m3, 7.0, ALU.min)
-    ts(m4, m3, hF, ALU.add)
-    ts(m5, m4, 1, ALU.bitwise_and)
-    ts(m6, m5, 9.0, ALU.mult)
-    tt(m6, m6, m3, ALU.add)
-    ts(m6, m6, 16.0, ALU.mult)
-    tt(m6, m6, m1, ALU.add)
-    copy(pick9, m6)
 
-    uH, uB, uC, aH, aB, aC, fB, fC, bad = (new("B", 4096) for _ in range(9))
-    Z4, ZB4, ZC4 = new("B", 1024), new("B", 1024), new("B", 1024)
-    DD = new("B", 512)
-    D, us, uj, dl, eq, mkB, sgn = (new("B", 256) for _ in range(7))
-    QP, QG, TP, TG = new("F", 288), new("F", 288), new("F", 576), new("F", 576)
+    GW = OPT["gw"]
+    uH, uB, uC, aH, aB, aC, fB, fC, bad, q6, a6 = (new("B", 4096) for _ in range(11))
+    Z4, ZB4, ZC4 = pair("B", GW), pair("B", GW), pair("B", GW)
+    DD = pair("B", 256)
+    D, us, uj, eq, eq2, mkB, thrR, thr6, sgn, kr = (pair("B", 128) for _ in range(10))
+    QP, QG, TP, TG, TK = new("F", 288), new("F", 288), pair("F", 288), pair("F", 288), pair("F", 288)
     for qq in (QP, QG):
         fill(qq, 0.0)
-    fill(sl(WIN, 2560, 2592), 0.0)
-    Pn, Gn = sl(QP, 16, 272), sl(QG, 16, 272)
+    move("A", sl(WIN, 512, X0), sl(IOTA, 512, X0))
+    fill(sl(WIN, X0 + 2048, 2 * X0), 0.0)
+    for kw in KW:
+        for h in range(2):
+            fill(sl(kw[h], 112, 128), 0.0)
+            fill(sl(kw[h], 256, 272), 0.0)
     PU, GU = new("U", 256), new("U", 256)
-    P9, PH9 = new("F", 288), new("F", 288)
-    CV = new("F", 512)
-    KO, krow, vals, dP, kt = (new("F", 256) for _ in range(5))
-    kt2, K1 = new("I", 256), new("I", 256)
-    PM, GM = new("H", 256), new("H", 256)
-    lv = [[new("F", 64), new("F", 64), new("F", 32), new("F", 16)] for _ in range(2)]
-    thr, thr2 = new("B", 16), new("B", 16)
-    joff, moff, zoff = (new("U", 16) for _ in range(3))
-    soff, cU = new("U", 32), new("U", 32)
-    kvU, scU = new("U", 32), new("U", 32)
-    kS, kE, kG, lo1, lo2, lo3, qI, vH, eI = (new("I", 16) for _ in range(9))
-    vI, cIi = new("I", 32), new("I", 32)
-    kFf, cpd, cpot, cb2, mult, ne15, lose, fin = (new("F", 16) for _ in range(8))
-    thrE, HH, mulB, addB, kv = (new("F", 32) for _ in range(5))
-    hcB = new("B", 32)
-    q3, r3 = new("F", 48), new("F", 48)
-    LL, LT, LO = new("F", 32), new("F", 32), new("F", 16)
-    acc, a256, ar = col(), col(), col()
+    CV = pair("F", 256)
+    krow, vals, GnB, pen, keys, asb, off = (pair("F", 128) for _ in range(7))
+    k1, k2 = pair("I", 128), pair("I", 128)
+    PM, GM = pair("H", 128), pair("H", 128)
+    lv = [[new("F", 64), new("F", 64), new("F", 32), new("F", 16), new("F", 8)] for _ in range(2)]
+    thr, NH_, s3w = new("B", 16), new("B", 16), new("B", 16)
+    joff, moff, soff, kvU, scU = (pair("U", 8) for _ in range(5))
+    cU, zs = pair("U", 16), pair("U", 16)
+    zoff, selU = [sl(z, 0, 8) for z in zs], [sl(z, 8, 16) for z in zs]
+    kS, kE, kG, lo1, lo2, lo3 = (pair("I", 8) for _ in range(6))
+    vI, cIi = pair("I", 16), pair("I", 16)
+    cp1, addB, thrE, kv, kvm = (pair("F", 8) for _ in range(5))
+    LL, LT, LO, lw, L2 = new("F", 32), new("F", 32), new("F", 16), new("F", 16), new("F", 16)
+    a256, ar = col(), [col(), col()]
     aI, aI2 = col("I"), col("I")
-    fill(acc, 0.0)
-    fill(a256, 256.0)
-    fill(sl(mulB, 16, 32), 256.0)
-    ts(sl(addB, 16, 32), c16, 16.0, ALU.mult, uF, ALU.add)
+    fill(a256, 128.0)
+    repk2 = new("U", 8)
+    ts(repk2, repk, 8.0, ALU.add)
 
-    def turn(t, qq, h):
-        tr(sl(t, 288 * h, 288 * h + 128), sl(qq, 16 + 128 * h, 144 + 128 * h))
-        tr(sl(t, 288 * h + 128, 288 * h + 288), sl(qq, 128 * h, 160 + 128 * h))
-        return part(t, h, 288)
+    def turn(t, qq, at):
+        tr(sl(t, 0, 128), sl(qq, at, at + 128))
+        tr(sl(t, 128, 288), sl(qq, at - 16, at + 144))
+        return t
 
-    copy(Gn, KI)
+    def spread(e, z4):
+        n = 128
+        while n < GW:
+            if n == 128:
+                move(e, sl(z4, 128, 256), sl(z4, 0, 128))
+            else:
+                move(e, sl(z4, n, 2 * n), sl(z4, 0, n))
+            n *= 2
+
     for h in range(2):
-        t = turn(TG, QG, h)
-        copy(part(KU, h, 128), ind(t, pickW))
-        act(part(K, h, 128), ind(t, pickW), AF.Copy)
+        copy(sl(KW[0][h], 128, 256), part(KI, h, 128))
+        copy(part(KU, h, 128), ind(turn(TK[h], KW[0][h], 128), pickW))
+        copy(sl(CZ[0][h], 0, 128), part(ZO, h, 128))
     copy(sl(LL, 0, 16), LI)
     copy(sl(LL, 16, 32), LI)
     tr(LT, LL)
     copy(L, ind(LT, pickL))
+    copy(LU, L)
     copy(SW, SI)
 
-    def tree(out, a, h, e="V"):
+    def least(out, a, h, name, first=None):
         b = lv[h]
-        move(e, b[0], sl(a, 64, 128))
-        tt(b[1], sl(a, 0, 64), b[0], ALU.min)
+        if name in OPT["red"]:
+            for i in range(8):
+                reduce(sl(b[4], i, i + 1), sl(a, i, 128, 8), ALU.min)
+            copy(out, b[4])
+            return b[4]
+        tt(b[1], sl(a, 64, 128), first if first else sl(a, 0, 64), ALU.min)
         tt(b[2], sl(b[1], 0, 32), sl(b[1], 32, 64), ALU.min)
         tt(b[3], sl(b[2], 0, 16), sl(b[2], 16, 32), ALU.min)
-        tt(part(out, h, 8), sl(b[3], 0, 8), sl(b[3], 8, 16), ALU.min)
+        tt(out, sl(b[3], 0, 8), sl(b[3], 8, 16), ALU.min)
+        return out
 
-    def place(off, lo, k):
+    def place(o, lo, k):
         ts(lo, k, 255, ALU.bitwise_and)
-        ts(off, lo, 16.0, ALU.mult, uF, ALU.add)
+        ts(o, lo, 16.0, ALU.mult, uF, ALU.add)
 
-    def sums(ps, z, src, c, stop):
-        mm([(part(ps, c % 2, 64), zu(z, u), sl(src, 1024 * c + u, 1024 * c + 1024, 16), False, stop and u == 15) for u in range(16)])
+    def pieces(tag, c):
+        n = 512 if tag in OPT["cut"] else 1024
+        return [(a0, a0 + n) for a0 in range(1024 * c, 1024 * c + 1024, n)]
 
-    def gathers(u, win, off, z4, c):
-        for i in (2 * c, 2 * c + 1):
-            tt(part(u, i, 512), ind(win, part(off, i, 32)), part(z4, c // 2, 512), ALU.subtract)
+    def sums(ps, z, src, c, first, stop=True):
+        out = part(ps, c % 2, 64)
+        mm(([(out, first[0], part(first[1], c % 2, 64), True, False)] if first else [])
+           + [(out, zu(z, u), sl(src, 1024 * c + u, 1024 * c + 1024, 16), False, stop and u == 15) for u in range(16)])
 
-    def over(src, c, onact):
-        if onact:
-            act(part(bad, c, 1024), part(src, c, 1024), AF.Sign, bm48, 1.0)
+    def rounded(out, ps, items):
+        if OPT["rnd"] == "V":
+            group(items)
+            ts(out, ps, MAGIC, ALU.add, MAGIC, ALU.subtract)
         else:
-            ts(part(bad, c, 1024), part(src, c, 1024), 48.0, ALU.is_gt, 2.0, ALU.mult)
+            group(items + [(ps, IR, ones)])
+            act(out, ps, AF.Identity, bR, 1.0)
 
-    def minus(w, terms, c, d):
+    def gathers(u, win, o, z4, c):
+        for i in range(1024 * c // GW, 1024 * (c + 1) // GW):
+            tt(part(u, i, GW), ind(win, part(o, i, GW // 16)), z4, ALU.subtract)
+
+    def minus(w, terms, c, d, neg=IN, rounds=False):
         for b in range(2):
             it = [(part(w, b, 512), l, part(s, 2 * c + b, 512)) for l, s in terms]
-            group(it + [(part(w, 4 * b + i, 128), IN, d) for i in range(4)])
+            group(it + [(part(w, 4 * b + i, 128), neg, d) for i in range(4)] + ([(part(w, b, 512), IM, ones4)] if rounds else []))
 
-    def lanes(out, src, k0, sg, h, n):
-        return [(sl(out, (m + h) % 3, n, 3), sh(Y, sg * (k0 + m)), sl(src, (m + h) % 3, n, 3)) for m in range(3)]
-
-    def bcast(ps, th, stop):
-        mm([(part(ps, k, 8), IN, th, False, stop and k == 15) for k in range(16)])
+    def lanes(out, src, k0, sg, h, y=Y):
+        return [(sl(out, (m + h) % 3, 128, 3), sh(y, sg * (k0 + m)), sl(src, (m + h) % 3, 128, 3)) for m in range(3)]
 
     def wsum(out, z, src):
-        return [(out, zu(z, u), sl(src, u, 256, 16)) for u in range(16)]
+        return [(out, zu(z, u), sl(src, u, width(src), 16)) for u in range(16)]
 
     wb = [P["W0"], P["W1"]]
     S2 = [P["SA"], P["SB"]]
-    M0, M1 = P["M0"], P["M1"]
-    M0a, M0b, M1a, M1b = sl(M0, 0, 256), sl(M0, 256, 512), sl(M1, 0, 256), sl(M1, 256, 512)
-    Mh = [M0, M1]
+    Mh = [P["M0"], P["M1"]]
+    nw, found = [0], [None, None]
 
-    for rnd in range(3):
+    def nextw():
+        nw[0] += 1
+        return wb[nw[0] % 2]
+
+    def one_round(rnd):
         last = rnd == 2
         win = Xb if rnd == 0 else XW
-        cz_ = CZ[rnd % 2]
-        Z = sl(cz_, 0, 256)
-        for h in range(1 if OPT["actg"] else 2):
-            z4 = part(Z4, h, 512)
-            e = "V" if rnd == 0 else OPT["z4"]
-            move(e, sl(z4, 0, 128), part(Z, h, 128))
-            move(e, sl(z4, 128, 256), part(Z, h, 128))
-            move(e, sl(z4, 256, 512), sl(z4, 0, 256))
-        act(thr, L, AF.Exp, b17, -LN2)
-        ts(ne15, L, 15.0, ALU.not_equal)
-        ts(sl(q3, 32, 48), L, 1.0, ALU.add)
-        tt(sl(q3, 32, 48), sl(q3, 32, 48), ne15, ALU.mult)
-        tt(sl(q3, 16, 32), sl(q3, 32, 48), L, ALU.subtract)
-        for h in range(2):
-            for zz, k0, w in ((ZB4, 1, part(wb[h], 0, 512)), (ZC4, 2, part(wb[h], 1, 512))):
-                z4 = part(zz, h, 512)
-                apart(lanes(part(w, 0, 128), part(Z, h, 128), k0, 1, h, 128))
-                act(sl(z4, 0, 128), part(w, 0, 128), AF.Copy)
-                move("G", sl(z4, 128, 256), sl(z4, 0, 128))
-                move("G", sl(z4, 256, 512), sl(z4, 0, 256))
-            ds, cs = sl(S2[h], 0, 128), sl(Mh[h], 0, 128)
-            mm([(ds, I1, part(cB, 0, 128), True, False)])
-            mm([(cs, BOc, part(sg1, h, 128), True, False)])
-            bcast(cs, part(thr, h, 8), False)
-            for c in (2 * h, 2 * h + 1):
-                if h == 1 and OPT["actg"]:
-                    act(part(uH, c, 1024), ind(win, part(KU, c, 64)), AF.Copy)
-                    minus(wb[c % 2], [(I1, uH)], c, part(Z, h, 128))
-                    act(part(aH, c, 1024), wb[c % 2], AF.Abs)
-                else:
-                    gathers(uH, win, KU, Z4, c)
-                    act(part(aH, c, 1024), part(uH, c, 1024), AF.Abs)
-                over(aH, c, c in OPT["sign1"])
-                sums(ds, Zd, aH, c, False)
-                sums(cs, Zc, bad, c, c % 2 == 1)
-            act(part(sgn, h, 128), cs, AF.Sign, bhalf, 1.0)
-            mm([(ds, IB, part(sgn, h, 128), False, True)])
-            tree(kS, ds, h, OPT["ev"])
-            so = sl(soff, 16 * h, 16 * h + 8)
-            place(so, part(lo1, h, 8), part(kS, h, 8))
-            Dh = part(D, h, 128)
-            move(OPT["dg"], Dh, ind(part(aH, h, 2048), so))
-            act(part(us, h, 128), ind(part(uH, h, 2048), so), AF.Copy)
-            apart(lanes(sl(Mh[h], 0, 128), Dh, 1, 1, h, 128) + lanes(sl(Mh[h], 128, 256), Dh, 2, 1, h, 128))
-            move(OPT["dd"], part(DD, h, 256), sl(Mh[h], 0, 256))
-            group(wsum(sl(Mh[h], 256, 272), Zv, part(DD, h, 256)))
-            tt(part(vI, h, 16), sl(Mh[h], 256, 272), c421, ALU.mult)
-            ts(part(cIi, h, 16), part(vI, h, 16), 2, ALU.arith_shift_right, 511, ALU.bitwise_and)
-            copy(part(cU, h, 16), part(cIi, h, 16))
-            for qq, t, o, c0, e in ((QP, TP, PU, 0, OPT["plist"]), (QG, TG, GU, 8, OPT["glist"])):
-                move(e, sl(qq, 16 + 128 * h, 144 + 128 * h), ind(SW, sl(cU, 16 * h + c0, 16 * h + c0 + 8)))
-                copy(part(o, h, 128), ind(turn(t, qq, h), pickW))
-            ts(part(cb2, h, 8), sl(cIi, 16 * h, 16 * h + 8), 2048.0, ALU.add)
-            act(part(P9, h, 144), ind(part(TP, h, 288), pick9), AF.Copy)
-        nw = [0]
-        for u, a, f, off, z4, dc, kk in ((uB, aB, fB, PU, ZB4, 0, kE), (uC, aC, fC, GU, ZC4, 1, kG)):
-            for h in range(2):
-                es = sl(S2[h], 0, 128)
-                mm([(es, I1, part(cB, h, 128), True, False)])
-                for c in (2 * h, 2 * h + 1):
-                    w = wb[nw[0] % 2]
-                    nw[0] += 1
-                    gathers(u, win, off, z4, c)
-                    if 4 * dc + c in OPT["relu"]:
-                        ts(part(a, c, 1024), part(u, c, 1024), 0.0, ALU.max)
-                        minus(w, [(I2, a), (IN, u)], c, part(DD, 2 * h + dc, 128))
-                    else:
-                        act(part(a, c, 1024), part(u, c, 1024), AF.Abs)
-                        minus(w, [(I1, a)], c, part(DD, 2 * h + dc, 128))
-                    act(part(f, c, 1024), w, AF.Abs)
-                    sums(es, Ze, f, c, c % 2 == 1)
-                tree(kk, es, h)
-            if dc == 0:
-                group(wsum(sl(M0, 0, 16), Zv, D))
-                copy(vH, sl(M0, 0, 16))
-                ts(qI, vH, 2, ALU.arith_shift_right, 2047, ALU.bitwise_and)
-                copy(sl(q3, 0, 16), qI)
-                group([(M1a, I1, quarter), (M1a, IH, us)] + [(part(M1a, h, 128), IH if h == 1 and OPT["actg"] else I1, part(Z, h, 128)) for h in range(2)])
-                ts(sl(cz_, 512, 768), M1a, MAGIC, ALU.add, MAGIC, ALU.subtract)
-                apart([(sl(M0, 144 * h + be, 144 * h + 144, 3), PF[(be + 2 * h) % 3], sl(P9, 144 * h + be, 144 * h + 144, 3)) for h in range(2) for be in range(3)])
-                act(PH9, sl(M0, 0, 288), AF.Copy)
-                tt(dP, ind(PH9, o9), K, ALU.subtract)
-                place(joff, lo2, kE)
-                act(uj, ind(uB, joff), AF.Copy)
-                nd = 128 if OPT["actg"] else 256
-                apart(lanes(M0a, uj, 1, -1, 0, nd))
-                group([(M0b, I1, Z)] + lanes(M0b, uj, 1, -1, 0, 256))
-                act(sl(dl, 0, nd), sl(M0a, 0, nd), AF.Copy)
-                act(sl(cz_, 256, 512), M0b, AF.Copy)
-                group([(M1a, I1, quarter), (M1a, IH, uj)] + [(part(M1a, h, 128), IH, s) for h in range(2) for s in (sl(ZB4, 512 * h, 512 * h + 128), part(DD, 2 * h, 128))])
-                ts(sl(CV, 0, 256), M1a, MAGIC, ALU.add, MAGIC, ALU.subtract)
-                tt(PM, ind(IBIG, joff), Pn, ALU.mult)
-                act(mkB, ind(IBIG, joff), AF.Copy)
-                group(wsum(sl(M1, 256, 272), Zh, PM))
-                ts(cpd, kE, 640.0 * 256, ALU.is_lt, 2592.0, ALU.mult)
-                ts(cpot, kE, 640.0 * 256, ALU.is_lt)
-                tt(sl(addB, 0, 16), sl(M1, 256, 272), cpd, ALU.max)
-                tt(sl(mulB, 0, 16), cb2, sl(addB, 0, 16), ALU.subtract)
-                ts(eI, kE, 0xFFFF00, ALU.bitwise_and)
-                ts(sl(thrE, 0, 16), eI, a256, ALU.add)
-                ts(sl(thrE, 16, 32), eI, a256, ALU.add)
-        copy(kFf, kG)
-        place(moff, lo3, kG)
-        apart([(sl(M1, 0, 16), sh(YF, -1), kFf), (sl(M1, 16, 32), sh(YF, -1), kFf)])
-        tt(HH, sl(M1, 0, 32), thrE, ALU.is_lt)
-        tt(kv, HH, mulB, ALU.mult)
-        tt(kv, kv, addB, ALU.add)
-        copy(kvU, kv)
-        copy(sl(hcB, 0, 16), sl(HH, 0, 16))
-        tt(sl(hcB, 16, 32), cpot, sl(HH, 0, 16), ALU.is_gt)
-        hit, con = sl(hcB, 0, 16), sl(hcB, 16, 32)
-        apart([(sl(M0, 16 * i + be, 16 * i + 16, 3), PB[be], sl(s, be, 16, 3)) for i, s in enumerate((hit, con, con)) for be in range(3)])
-        group([(sl(M0, 48, 64), I1, cz)] + [(sl(M0, 48 + be, 64, 3), PB[be], sl(s, be, 16, 3)) for s in (hit, hit, con) for be in range(3)])
-        ts(zoff, sl(M0, 48, 64), -256.0, ALU.mult, uF, ALU.add)
-        tt(r3, sl(M0, 0, 48), q3, ALU.mult)
-        ts(mult, sl(M0, 0, 16), 4.0, ALU.mult, 1.0, ALU.add)
-        act(thr2, sl(r3, 32, 48), AF.Exp, b17, -LN2)
-        if last:
-            tt(sl(LL, 0, 16), L, sl(r3, 16, 32), ALU.add)
-            tt(sl(LL, 16, 32), L, sl(r3, 16, 32), ALU.add)
-            tr(LT, LL)
-            copy(LO, ind(LT, pickL))
-        else:
-            tt(L, L, sl(r3, 16, 32), ALU.add)
-        Z = sl(CZ[(rnd + 1) % 2], 0, 256)
-        act(Z, ind(cz_, zoff), AF.Copy)
-        tt(GM, ind(IBIG, moff), Gn, ALU.mult)
-        group([(M1b, sh(BOh, -1), GM), (M1b, BOn, PM)])
-        tt(M1b, M1b, mkB, ALU.mult)
-        tt(sl(CV, 256, 512), M1b, Pn, ALU.add)
-        move(OPT["krow"], krow, ind(IOTA, sl(kvU, 0, 16)))
-        act(vals, ind(CV, sl(kvU, 16, 32)), AF.Copy)
-        tt(eq, ind(sl(kv, 0, 16), repb), krow, ALU.is_equal)
-        tt(eq2, ind(sl(kv, 0, 16), repo), krow, ALU.is_equal)
-        mm([(sl(M1, 0, 16), sh(YF, 0), sl(kv, 0, 16), True, False)] + [(sl(M1, 0, 16), part(tri, u, 128), sl(eq, u, 256, 16), False, False) for u in range(16)])
-        mm([(sl(M1, 0, 16, 2), zu(Z1, u), sl(eq2, u, 256, 32), False, u == 15) for u in range(16)])
-        ts(sl(scU, 0, 16, 2), sl(M1, 0, 16, 2), spare, ALU.min)
-        ts(sl(scU, 1, 16, 2), sl(M1, 1, 16, 2), spare2, ALU.min)
-        for b in range(8):
-            copy(ind(WIN, part(scU, b, 2)), part(vals, b, 32))
-        if not last:
-            apart([(sl(M0, 64, 80), BO1, hit)])
-            add("V", lambda: g.vector.tensor_reduce(ap(ar), ap(sl(M0, 64, 80)), AX.X, ALU.add), [sl(M0, 64, 80)], [ar], 0.07)
-            tt(acc, acc, ar, ALU.add)
-            copy(aI, acc)
-            ts(aI2, aI, 31, ALU.bitwise_and)
-            ts(a256, aI2, 1.0, ALU.add, 256.0, ALU.mult)
-        tt(kt, ind(mult, repk), K, ALU.mult)
-        tt(kt2, ind(sl(r3, 0, 16), repk), kt, ALU.add)
-        ts(K1, kt2, 2047, ALU.bitwise_and)
-        for h in range(2):
-            cs = sl(S2[h], 0, 128)
-            mm([(cs, BOc, part(sg6, h, 128), True, False)])
-            for c in (2 * h, 2 * h + 1):
-                w = wb[nw[0] % 2]
-                nw[0] += 1
-                minus(w, [(I1, uH)], c, sl(cz_, 384, 512) if h == 1 and OPT["actg"] else part(dl, h, 128))
-                act(part(aB, c, 1024), w, AF.Abs)
-                over(aB, c, c in OPT["sign6"])
-                sums(cs, Zc, bad, c, False)
-            bcast(cs, part(thr2, h, 8), True)
-            ts(cs, cs, 0.0, ALU.is_ge)
-            tt(cs, cs, part(dP, h, 128), ALU.mult)
-            tt(part(K, h, 128), cs, part(K1, h, 128), ALU.add)
-            if not last:
-                copy(part(KU, h, 128), part(K, h, 128))
+        cz_, kw_ = CZ[rnd % 2], KW[rnd % 2]
+        Z = [sl(cz_[h], 0, 128) for h in range(2)]
+        K = [sl(kw_[h], 128, 256) for h in range(2)]
+        Pn = [sl(QP, 16 + 128 * h, 144 + 128 * h) for h in range(2)]
+        Gn = [sl(QG, 16 + 128 * h, 144 + 128 * h) for h in range(2)]
 
-    copy(Pn, ind(K, reord))
-    tr(sl(TP, 0, 256), sl(QP, 16, 272))
-    tr(sl(TP, 256, 544), sl(QP, 0, 288))
-    copy(KO, ind(sl(TP, 0, 544), pickN))
-    for ci, e, k, src, us_ in ((5, "S", "oz", Z, 0.3), (5, "S", "ol", LO, 0.1), (6, "G", "ox", XW, 1.5), (7, "S", "oa", SW, 0.8), (8, "S", "ok", KO, 0.4)):
-        dma(e, T["s" + k][:], ap(src), [src], [("s" + k, 0, 8)], us_)
-        own("S", k, T["s" + k][0 if k == "ol" else rank], [("s" + k, 0, 8)])
-        if k != "oz":
-            remote(ci)
-    for ci, e, k, y, us_ in ((5, "A", "oz", T.yz, 0.3), (5, "A", "ol", T.yl, 0.1), (6, "A", "ox", T.yx, 1.5), (7, "A", "oa", T.ya, 0.8), (8, "S", "ok", T.yk, 0.4)):
-        src = T.lol[:, rows, :] if k == "ol" else T["l" + k][:]
-        dma(e, y[:], src, [("l" + k, 0, 8), ("call%d" % ci, 0, 1)] + ([K] if e == "A" else []), [("y" + k, 0, 1)], us_, ext=arr(ci))
+        def speaker(h):
+            M, raw = Mh[h], h in OPT["rawH"]
+            if not raw:
+                e = "V" if rnd == 0 else "G"
+                move(e, sl(Z4[h], 0, 128), Z[h])
+                spread(e, Z4[h])
+            if OPT["thr"][h] != "P":
+                move(OPT["thr"][h], thrR[h], ind(thr, repk2 if h else repk))
+            apart(lanes(sl(M, 0, 128), Z[h], 1, 1, h) + lanes(sl(M, 128, 256), Z[h], 2, 1, h))
+            for i, zz in enumerate((ZB4[h], ZC4[h])):
+                act(sl(zz, 0, 128), part(M, i, 128), AF.Copy)
+                spread("G", zz)
+            ds, cs = sl(S2[h], 0, 128), sl(M, 0, 128)
+            for c in (2 * h, 2 * h + 1):
+                cut = pieces("H%d%d" % (h, c % 2), c)
+                if raw:
+                    w = nextw()
+                    act(part(uH, c, 1024), ind(win, part(KU, c, 64)), AF.Copy)
+                    minus(w, [(I1, uH)], c, Z[h])
+                else:
+                    gathers(uH, win, KU, Z4[h], c)
+                for a0, a1 in cut:
+                    act(sl(aH, a0, a1), sl(w, a0 - 1024 * c, a1 - 1024 * c) if raw else sl(uH, a0, a1), AF.Abs)
+                    ts(sl(bad, a0, a1), sl(aH, a0, a1), 48.0, ALU.is_gt, 2.0, ALU.mult)
+                if OPT["pen"][h] == "V":
+                    sums(ds, Zd, aH, c, (I1, cB))
+                else:
+                    if c % 2 == 0:
+                        mm([(ds, I1, cB, True, False)])
+                    sums(ds, Zd, aH, c, None, False)
+                if OPT["thr"][h] == "P":
+                    mm([(part(cs, c % 2, 64), BO0, sl(cB, 0, 64), True, False)]
+                       + [(part(cs, k, 8), IN, part(thr, h, 8), False, False) for k in range(8 * (c % 2), 8 * (c % 2) + 8)])
+                    sums(cs, Zc, bad, c, None)
+                else:
+                    sums(cs, Zc, bad, c, (IN, thrR[h]))
+            if OPT["pen"][h] == "V":
+                ts(pen[h], cs, 0.0, ALU.is_ge, 1048576.0, ALU.mult)
+                tt(keys[h], ds, pen[h], ALU.add)
+                least(kS[h], keys[h], h, "H%d" % h)
+            else:
+                act(sgn[h], cs, AF.Sign, bhalf, 1.0)
+                mm([(ds, IB, sgn[h], False, True)])
+                if "H%d" % h not in OPT["red"]:
+                    move(OPT["ev"], lv[h][0], sl(ds, 0, 64))
+                least(kS[h], ds, h, "H%d" % h, lv[h][0])
+            place(soff[h], lo1[h], kS[h])
+            move(OPT["dg"][h], D[h], ind(part(aH, h, 2048), soff[h]))
+            act(us[h], ind(part(uH, h, 2048), soff[h]), AF.Copy)
+            apart(lanes(sl(M, 0, 128), D[h], 1, 1, h) + lanes(sl(M, 128, 256), D[h], 2, 1, h))
+            move(OPT["dd"][h], DD[h], sl(M, 0, 256))
+            group(wsum(sl(M, 256, 272), Zv, DD[h]))
+            tt(vI[h], sl(M, 256, 272), c421, ALU.mult)
+            ts(cIi[h], vI[h], 2, ALU.arith_shift_right, 511, ALU.bitwise_and)
+            copy(cU[h], cIi[h])
+            for qq, t, o, i, e in ((QP, TP, PU, 0, OPT["plist"][h]), (QG, TG, GU, 1, OPT["glist"][h])):
+                move(e, sl(qq, 16 + 128 * h, 144 + 128 * h), ind(SW, part(cU[h], i, 8)))
+                copy(part(o, h, 128), ind(turn(t[h], qq, 16 + 128 * h), pickW))
+            S = S2[h]
+            o = sl(S, 0, 128)
+            if OPT["kh"][h] == "V":
+                group([(o, I20, K[h]), (o, BOv, D[h])])
+                copy(k1[h], o)
+                ts(k2[h], k1[h], 2, ALU.arith_shift_right, 2047, ALU.bitwise_and)
+                copy(sl(kw_[h], 0, 128), k2[h])
+            else:
+                o2 = sl(S, 256, 384)
+                group([(o2, I5, K[h]), (o2, BOq, D[h]), (o2, I1, c1k), (o2, IH, quarter), (o2, IN, quarter), (o2, IR2, ones)])
+                act(kr[h], o2, AF.Identity, bR2, 1.0)
+                group([(o, I5, K[h]), (o, BOq, D[h]), (o, I1, c38), (o, IR, ones), (o, IRN, ones), (o, IN, kr[h])])
+                move("A", sl(kw_[h], 0, 128), o)
+            o = sl(S, 128, 256)
+            rounded(sl(cz_[h], 128, 256), o, [(o, I1, quarter), (o, IH, us[h]), (o, IH if raw else I1, Z[h])])
+            apart([(sl(M, 0, 128), sh(YF, -1), Gn[h])])
+            act(GnB[h], sl(M, 0, 128), AF.Copy)
+
+        def look(name, h, u, a, f, o, z4, d, z, kk):
+            es = sl(S2[h], 0, 128)
+            for c in (2 * h, 2 * h + 1):
+                tag = "%s%d%d" % (name, h, c % 2)
+                if tag in OPT["rawC"] or (name == "B" and h in OPT["rawB"]):
+                    w = nextw()
+                    act(part(u, c, 1024), ind(win, part(o, c, 64)), AF.Copy)
+                    minus(w, [(I1, u)], c, sl(z4, 0, 128))
+                    act(part(a, c, 1024), w, AF.Abs)
+                    terms = [(I1, a)]
+                else:
+                    gathers(u, win, o, z4, c)
+                    for a0, a1 in pieces(tag, c):
+                        if tag in OPT["relu"]:
+                            ts(sl(a, a0, a1), sl(u, a0, a1), 0.0, ALU.max)
+                        else:
+                            act(sl(a, a0, a1), sl(u, a0, a1), AF.Abs)
+                    terms = [(I2, a), (IN, u)] if tag in OPT["relu"] else [(I1, a)]
+                w = nextw()
+                minus(w, terms, c, d)
+                for a0, a1 in pieces(tag, c):
+                    act(sl(f, a0, a1), sl(w, a0 - 1024 * c, a1 - 1024 * c), AF.Abs)
+                sums(es, z, f, c, (I1, cB))
+                if c % 2 == 0 and name + str(h) not in OPT["red"]:
+                    move(OPT["ev"], lv[h][0], sl(es, 0, 64))
+            return least(kk, es, h, name + str(h), lv[h][0])
+
+        def partner(h):
+            M, raw, rawb = Mh[h], h in OPT["rawH"], h in OPT["rawB"]
+            look("B", h, uB, aB, fB, PU, ZB4[h], sl(DD[h], 0, 128), Ze, kE[h])
+            place(joff[h], lo2[h], kE[h])
+            tt(PM[h], ind(IBIG, joff[h]), Pn[h], ALU.mult)
+            act(uj[h], ind(part(uB, h, 2048), joff[h]), AF.Copy)
+            act(mkB[h], ind(IBIG, joff[h]), AF.Copy)
+            group([(sl(M, 384, 392), I2K, sl(ones, 0, 8))] + wsum(sl(M, 384, 392), Zh, PM[h]))
+            ts(cp1[h], kE[h], 640.0 * 256, ALU.is_lt, 1.0, ALU.add)
+            tt(addB[h], sl(M, 384, 392), cp1[h], ALU.mult)
+            ts(thrE[h], kE[h], a256, ALU.add)
+            back = lambda out: lanes(out, uj[h], 1, -1, h)
+            if not raw:
+                if rawb:
+                    group([(sl(M, 128, 256), IN, Z[h])] + back(sl(M, 128, 256)))
+                else:
+                    apart(back(sl(M, 128, 256)))
+            if rawb:
+                apart(back(sl(M, 0, 128)))
+            else:
+                group([(sl(M, 0, 128), I1, Z[h])] + back(sl(M, 0, 128)))
+            n = 128 if raw else 256
+            act(sl(cz_[h], 256, 256 + n), sl(M, 0, n), AF.Copy)
+            o = sl(M, 256, 384)
+            rounded(sl(CV[h], 128, 256), o, [(o, I1, quarter), (o, IH, uj[h]), (o, IH, sl(DD[h], 0, 128))] + ([] if rawb else [(o, IH, sl(ZB4[h], 0, 128))]))
+
+        def contact(h):
+            S = P[OPT["s6bank"][h]]
+            cs, dp = sl(S, 0, 128), sl(S, 128, 256)
+            sizes = "V" not in OPT["s6"][2 * h:2 * h + 2]
+            if sizes:
+                act(thr6[h], ind(THR, part(LU, h, 8)), AF.Copy)
+                mm([(cs, IN, thr6[h], True, False)])
+            for c in (2 * h, 2 * h + 1):
+                w = nextw()
+                minus(w, [(IS, uH)], c, sl(cz_[h], 256, 384) if h in OPT["rawH"] else sl(cz_[h], 384, 512), ISN, OPT["s6"][c] == "P")
+                if OPT["s6"][c] == "V":
+                    ts(part(q6, c, 1024), w, MAGIC128, ALU.add, MAGIC128, ALU.subtract)
+                elif OPT["s6"][c] == "P":
+                    act(part(q6, c, 1024), w, AF.Abs, bM, 1.0)
+                else:
+                    act(part(a6, c, 1024), w, AF.Abs)
+                    ts(part(q6, c, 1024), part(a6, c, 1024), 63.5, ALU.is_gt, 128.0, ALU.mult)
+                mm([(cs, zu(Zq, k), part(q6, 16 * h + k, 128), k == 0 and not sizes, k == 15) for k in range(8 * (c % 2), 8 * (c % 2) + 8)])
+            group([(dp, INF, K[h])] + lanes(dp, Pn[h], 1, -1, h, YF))
+            if sizes:
+                ts(off[h], cs, 0.0, ALU.is_ge)
+            else:
+                act(asb[h], cs, AF.Abs)
+                tt(off[h], ind(THR, part(LU, h, 8)), asb[h], ALU.is_le)
+            tt(dp, dp, off[h], ALU.mult)
+            tt(sl(kw_[h], 256, 384), dp, K[h], ALU.add)
+
+        def guesser(h):
+            found[h] = look("C", h, uC, aC, fC, GU, ZC4[h], sl(DD[h], 128, 256), Zf, kG[h])
+
+        def decide(h):
+            M = Mh[h]
+            nh, s3 = part(NH_, h, 8), part(s3w, h, 8)
+            tt(nh, found[h], thrE[h], ALU.is_ge)
+            tt(kvm[h], nh, addB[h], ALU.mult)
+            tt(kv[h], kvm[h], sl(cIi[h], 0, 8), ALU.max)
+            ts(kvU[h], kv[h], 2.0 * X0, ALU.min)
+            tt(s3, nh, cp1[h], ALU.mult)
+            place(moff[h], lo3[h], kG[h])
+            group([(sl(M, 0, 16), I1, cz), (sl(M, 8, 16), I1, nh)]
+                  + [(sl(M, b, 8, 3), PB[(b + 2 * h) % 3], sl(s3, b, 8, 3)) for b in range(3)])
+            ts(zs[h], sl(M, 0, 16), 128.0, ALU.mult, uF, ALU.add)
+            tt(GM[h], ind(IBIG, moff[h]), GnB[h], ALU.mult)
+            act(krow[h], ind(IOTA, kvU[h]), AF.Copy)
+            o = sl(M, 128, 256)
+            group([(o, BOh, GM[h]), (o, BOn, PM[h])])
+            tt(o, o, mkB[h], ALU.mult)
+            tt(sl(CV[h], 0, 128), o, Pn[h], ALU.add)
+            act(vals[h], ind(CV[h], selU[h]), AF.Copy)
+            tt(eq[h], ind(kv[h], repb), krow[h], ALU.is_equal)
+            tt(eq2[h], ind(kv[h], repo), krow[h], ALU.is_equal)
+            o = sl(S2[h] if h else M, 16, 24)
+            mm([(o, sh(YF, 0), kv[h], True, False)])
+            mm([(o, part(tri, u, 128), sl(eq[h], u, 128, 16), False, False) for u in range(16)])
+            mm([(sl(o, 0, 8, 2), zu(Z1, u), sl(eq2[h], u, 128, 32), False, u == 15) for u in range(16)])
+            ts(sl(scU[h], 0, 8, 2), sl(o, 0, 8, 2), spare, ALU.min)
+            ts(sl(scU[h], 1, 8, 2), sl(o, 1, 8, 2), spare2, ALU.min)
+
+        def prefix():
+            o = sl(P[OPT["pbank"]], 48, 64)
+            mm([(sl(o, b, 16, 3), l[b], sl(s, b, 16, 3), l is PB, l is PN) for b in range(3) for l, s in ((PB, s3w), (PN, NH_))])
+            tt(L2, o, L, ALU.add)
+            ts(lw, L2, 16.0, ALU.is_ge, -16.0, ALU.mult)
+            tt(L, L2, lw, ALU.add)
+
+        def settle(h):
+            if last:
+                act(part(ZO, h, 128), ind(sl(cz_[h], 0, 384), zoff[h]), AF.Copy)
+                move(OPT["kg"], part(KO, h, 128), ind(kw_[h], zoff[h]))
+                return
+            nk = KW[(rnd + 1) % 2][h]
+            act(sl(CZ[(rnd + 1) % 2][h], 0, 128), ind(sl(cz_[h], 0, 384), zoff[h]), AF.Copy)
+            move(OPT["kg"], sl(nk, 128, 256), ind(kw_[h], zoff[h]))
+            copy(part(KU, h, 128), ind(turn(TK[h], nk, 128), pickW))
+
+        tie[0:2] = ["round", 0]
+        act(thr, L, AF.Exp, b17, -LN2)
+        for h in range(2):
+            speaker(h)
+        step = {"B": partner, "C": guesser, "S": contact, "D": decide}
+        for s in OPT["order"]:
+            step[s[0]](int(s[1]))
+        for h in range(2):
+            for b in range(4):
+                copy(ind(WIN, part(scU[h], b, 2)), part(vals[h], b, 32))
+        tie[0:2] = ["end" if last else "next", 0]
+        for h in range(2):
+            settle(h)
+        prefix()
+        if last:
+            for i in range(2):
+                copy(part(LL, i, 16), L)
+        else:
+            copy(LU, L)
+            o = sl(Mh[1], 32, 48)
+            apart([(o, BO1, NH_)])
+            reduce(ar[rnd], o, ALU.add)
+            if rnd == 0:
+                ts(aI, ar[0], -1.0, ALU.mult, 1024.0, ALU.add)
+            else:
+                tt(ar[1], ar[1], ar[0], ALU.add)
+                ts(aI, ar[1], -1.0, ALU.mult, 1024.0, ALU.add)
+            ts(aI2, aI, 31, ALU.bitwise_and)
+            ts(a256, aI2, 0.5, ALU.add, 256.0, ALU.mult)
+
+    for rnd in range(3):
+        one_round(rnd)
+
+    tr(LT, LL)
+    copy(LO, ind(LT, pickL))
+    for h, e in enumerate("VA"):
+        move(e, part(Xb, h, 1024), part(XW, h, 1024))
+    out = {"oz": (ZO, T.yz[:], 0.3), "ol": (LO, T.yl[:], 0.1), "oa": (SW, T.ya[:], 0.8), "ox": (part(Xb, 0, 1024), T.yx[:, 0:1024], 0.8),
+           "oy": (part(Xb, 1, 1024), T.yx[:, 1024:2048], 0.8), "ok": (KO, T.yk[:], 0.4)}
+    for ci in range(5, len(CALLS)):
+        for k in CALLS[ci]:
+            dma("S", T["s" + k][:], ap(out[k][0]), [out[k][0]], [("s" + k, 0, 8)], out[k][2])
+            own("S", k, T["s" + k][0 if k == "ol" else rank], [("s" + k, 0, 8)])
+        remote(ci)
+    for ci in range(5, len(CALLS)):
+        for k in CALLS[ci]:
+            src = T.lol[:, rows, :] if k == "ol" else T["l" + k][:]
+            dma("A", out[k][1], src, [("l" + k, 0, 8), ("call%d" % ci, 0, 1), KO, Xb], [("y" + k, 0, 1)], out[k][2], ext=arr(ci))
     ops[0]["end"] = [(T.sem.sent, sent[0])]
     return ops

@@ -2,7 +2,7 @@ import math
 from concourse.bass import DstId, RemoteDMATransfer
 from concourse.mybir import AluOpType as ALU, AxisListType as AX, ActivationFunctionType as AF
 
-NF, NB, NI, NU, NH = 19456, 69632, 3072, 1536, 1024
+NF, NB, NI, NU, NH = 19968, 69632, 3072, 1536, 1024
 SCRATCH = {
     "F": ("sbuf", [128, NF], "float32"), "B": ("sbuf", [128, NB], "bfloat16"), "I": ("sbuf", [128, NI], "int32"),
     "U": ("sbuf", [128, NU], "uint16"), "H": ("sbuf", [128, NH], "float16"),
@@ -21,10 +21,10 @@ SEMAPHORES = ["cV", "cA", "cP", "cG", "sent"] + ["arr%d" % i for i in range(len(
 PSUM = ("W0", "W1", "SA", "SB", "M0", "M1")
 MAGIC = 12582912.0
 MAGIC128 = 1610612736.0
-OPT = {"rawH": (1,), "rawB": (), "rawC": (), "relu": (), "s6": "VVPP", "thr": "PP", "gw": 512,
-       "red": ("H0", "C1"), "cut": (), "order": ("B0", "C0", "B1", "S0", "C1", "D0", "S1", "D1"), "dd": "VA", "kg": "A", "ev": "V", "dg": "VV", "plist": "VA", "glist": "AA",
-       "cases": ((1.45, 2.0, 0.15), (1.25, 1.56, 0.3)), "slack": 1.0, "tied": 4, "moves": 0, "heat": 0.1, "s6bank": ("SA", "M0"), "pbank": "SB",
-       "pen": "VA", "rnd": "V", "kh": "VV", "hop": 5.0, "lat": 0.22, "ga": 1.56, "iters": 2000, "amp": 0.5}
+OPT = {"rawH": (1, 3), "rawB": (), "rawC": (), "relu": (), "s6": "VVAP", "thr": "PP", "gw": 1024, "zm": "A",
+       "red": ("H0", "C1"), "cut": ("H00",), "order": ("B0", "C0", "B1", "S0", "T0", "C1", "D0", "S1", "T1", "D1"), "early": 0, "dd": "AA", "kg": "A", "ev": "V", "dg": "AA", "plist": "AA", "glist": "AA",
+       "cases": ((1.45, 2.0, 0.15), (1.25, 1.56, 0.3)), "slack": 1.0, "tied": 4, "moves": 0, "heat": 0.1, "ncase": 2, "same": 0, "whole": 0, "span": 8, "s6w": ((), ()), "fast": (0,), "T": ("H0", "H1", "B0", "B1", "C0", "C1"), "s6bank": ("SA", "M0"), "pbank": "SB",
+       "pen": "VV", "rnd": "A", "kh": "VV", "dp": (0,), "give": 0.0, "seed": 12345, "leg": 300, "starts": 3, "gwH": (512, 512), "hop": 3.5, "lat": 0.22, "ga": 1.56, "iters": 2800, "amp": 0.5}
 
 
 def routes(T, topo):
@@ -205,15 +205,27 @@ def arrange(ops):
     twins = {}
     for i, o in enumerate(ops):
         twins.setdefault(o["tie"], []).append(i)
-    key, best, seed = [-p for p in prio], None, 12345
+    steps = {}
+    for i, o in enumerate(ops):
+        if o["tie"][0] != "once":
+            steps.setdefault((o["tie"][0], o["tie"][1] // OPT["span"], o["e"] if o["c"] > 0.4 else ""), []).append(i)
+    steps = list(steps.values())
+    key, best, top, seed = [-p for p in prio], None, None, OPT["seed"]
     for it in range(OPT["iters"]):
+        if it and it % OPT["leg"] == 0 and it <= OPT["leg"] * OPT["starts"]:
+            if it < OPT["leg"] * OPT["starts"]:
+                key, best = [-p for p in prio], None
+            else:
+                key, best = [top[1][i] - c[i] for i in range(n)], top
         end = place(feasible(key, fw, True), fw, zero)
         span = max(end[i] + tailx[i] for i in outs)
         if best is None or span <= best[2] + OPT["slack"]:
             seq = sorted(range(n), key=lambda i: (end[i] - c[i], i))
             tot = span + sum(replay(seq, cc, dep) for cc, dep in cases)
-            if best is None or tot <= best[0]:
+            if best is None or tot <= best[0] + OPT["give"] * (1.0 - it / OPT["iters"]):
                 best = (tot, end, span)
+                if top is None or tot < top[0]:
+                    top = best
         src = best[1] if it % 2 == 1 else end
         noise = [0.0] * n
         if it % 2 == 1:
@@ -221,6 +233,14 @@ def arrange(ops):
             lo = best[2] * seed / 2147483648.0 - 4.0
             amp = OPT["amp"] * (1 + seed // 64 % 6)
             tied = seed // 1024 % 4 < OPT["tied"]
+            if seed // 8192 % 4 < OPT["whole"]:
+                lo = -9.0
+                for _ in range(2):
+                    seed = (seed * 1103515245 + 12345) % 2147483648
+                    step = steps[seed // 256 % len(steps)]
+                    seed = (seed * 1103515245 + 12345) % 2147483648
+                    for i in step:
+                        noise[i] = 2 * amp * (seed / 2147483648.0 - 0.5)
             for i in range(n):
                 if lo < src[i] < lo + 8.0:
                     seed = (seed * 1103515245 + 12345) % 2147483648
@@ -228,6 +248,7 @@ def arrange(ops):
                         noise[j] = amp * (seed / 2147483648.0 - 0.5)
         back = place(feasible([-src[i] + noise[i] for i in range(n)], bw, False), bw, tailx)
         key = [-back[i] for i in range(n)]
+    best = top
     order = feasible([best[1][i] - c[i] for i in range(n)], fw, True)
     cases = [(c, fw)] + cases
     qi = ["VAPGS".index(e) for e in eng]
@@ -253,6 +274,34 @@ def arrange(ops):
         e = max(outs, key=lambda i: end[i] + tailx[i])
         return end, why, end[e] + tailx[e], e
 
+    def ahead(seq, v, u):
+        a, b = seq.index(u), seq.index(v)
+        if a > b:
+            return None
+        must, lastq, front = set(preds[v]), set(), []
+        for k in range(b - 1, a - 1, -1):
+            i = seq[k]
+            if i in must or qi[i] in lastq:
+                if qi[i] == qi[v]:
+                    return None
+                front.append(i)
+                lastq.add(qi[i])
+                must.update(preds[i])
+        moved = set(front)
+        return seq[:a] + front[::-1] + [v] + [i for i in seq[a:b] if i not in moved] + seq[b + 1:], a
+
+    cases = cases[:OPT["ncase"]]
+    if OPT["same"]:
+        st = [best[1][i] - c[i] for i in range(n)]
+        mark = twins[("round", OPT["same"])]
+        key = list(st)
+        for tw in twins.values():
+            if len(tw) > 1:
+                for r, i in enumerate(tw):
+                    key[i] = st[tw[1]] - st[mark[1]] + st[mark[r]]
+        alike = feasible(key, fw, True)
+        if sum(times(alike, cc, dep, None, 0)[2] for cc, dep in cases) < sum(times(order, cc, dep, None, 0)[2] for cc, dep in cases) + 6:
+            order = alike
     cur = [times(order, cc, dep, None, 0) for cc, dep in cases]
     tot = sum(x[2] for x in cur)
     keep = (tot, order, cur[0][0])
@@ -268,7 +317,6 @@ def arrange(ops):
             break
         seed = (seed * 1103515245 + 12345) % 2147483648
         v = arcs[seed // 256 % len(arcs)]
-        b = order.index(v)
         a = order.index(why[v])
         for _ in range(seed // 16 % 3):
             k = a - 1
@@ -276,22 +324,18 @@ def arrange(ops):
                 k -= 1
             if k >= 0:
                 a = k
-        must, lastq, ok = set(preds[v]), set(), True
-        front = []
-        for k in range(b - 1, a - 1, -1):
-            i = order[k]
-            if i in must or qi[i] in lastq:
-                if qi[i] == qi[v]:
-                    ok = False
-                    break
-                front.append(i)
-                lastq.add(qi[i])
-                must.update(preds[i])
-        if not ok:
+        u = order[a]
+        tv, tu = twins[ops[v]["tie"]], twins[ops[u]["tie"]]
+        shift = tu.index(u) - tv.index(v)
+        pairs = [(tv[r], tu[r + shift]) for r in range(len(tv)) if 0 <= r + shift < len(tu)] if seed // 4 % 4 < OPT["tied"] else [(v, u)]
+        seq, low = order, n
+        for v2, u2 in pairs:
+            got = ahead(seq, v2, u2)
+            if got:
+                seq, low = got[0], min(low, got[1])
+        if low == n:
             continue
-        moved = set(front)
-        seq = order[:a] + front[::-1] + [v] + [i for i in order[a:b] if i not in moved] + order[b + 1:]
-        new = [times(seq, cc, dep, cur[k], a) for k, (cc, dep) in enumerate(cases)]
+        new = [times(seq, cc, dep, cur[k], low) for k, (cc, dep) in enumerate(cases)]
         t2 = sum(x[2] for x in new)
         seed = (seed * 1103515245 + 12345) % 2147483648
         if t2 <= tot - OPT["heat"] * (1.0 - it / OPT["moves"]) * math.log((seed + 1) / 2147483649.0):
@@ -410,7 +454,7 @@ def build(g, core, rank, T, topo, way):
         for a in w:
             if a[0] == "ind":
                 ww.append(a[1])
-                rr.append(a[2])
+                rr += [a[1], a[2]]
             else:
                 ww.append(a)
         gathered = sum(16 * width(a[2]) * CY for a in r if isref(a) and a[0] == "ind")
@@ -705,15 +749,62 @@ def build(g, core, rank, T, topo, way):
     ts(pickW, sl(cF, 0, 8), 2.0, ALU.mult, s3, ALU.add)
     ts(pickL, hF, 16.0, ALU.mult, uF, ALU.add)
 
+    Sel1, SelF, SelG = new("B", 8), new("F", 8), new("B", 8)
+    ts(Sel1, sl(cF, 0, 128, 16), kF, ALU.is_equal)
+    ts(SelF, sl(cF, 0, 128, 16), kF, ALU.is_equal)
+    ts(SelG, sl(cF, 0, 128, 16), kM, ALU.is_equal, 256.0, ALU.mult)
+    SelD, SelC, SelE = (scaled(new("B", 8), Sel1, w) for w in (-256.0, wc, 256.0))
+    BOm = scaled(new("B", 128), BO1, -1.0)
+    c15I, c15, E128, RST, cP, bF = new("I", 128), new("F", 128), new("B", 128), new("F", 128), new("B", 128), col()
+    ts(c15I, sl(cI, 0, 128), 15, ALU.bitwise_and)
+    copy(c15, c15I)
+    ts(E128, c15, uF, ALU.is_equal)
+    ts(RST, c15, 0.0, ALU.is_equal, 8388608.0, ALU.mult)
+    ts(bF, kF, 1.0 / 16, ALU.mult, -64.0, ALU.add)
+    SelN, IM8, IM8N, u1k = scaled(new("F", 8), Sel1, -1.0), eye("B", 256.0 * MAGIC), eye("B", -256.0 * MAGIC), col()
+    ts(u1k, uF, 1024.0, ALU.add)
+    ts(cP, c15, 8.0, ALU.mult, bF, ALU.add)
+    rep15, repb2 = new("U", 8), new("U", 8)
+    ts(rep15, sl(cF, 0, 8), 16.0, ALU.mult, 15.0, ALU.add)
+    ts(repb2, sl(cF, 0, 8), 8.0, ALU.add)
+    run16, wide = pair("F", 128), pair("F", 128)
+    SelDV, cP2, E256, RS0, half128 = new("B", 16), new("B", 256), new("B", 256), new("F", 128), new("B", 128)
+    scaled(part(SelDV, 0, 8), Sel1, -256.0)
+    scaled(part(SelDV, 1, 8), Sel1, wv)
+    copy(part(cP2, 0, 128), cP)
+    fill(part(cP2, 1, 128), -256.0)
+    fill(half128, 0.5)
+    for i in range(2):
+        move("A", part(E256, i, 128), E128)
+    ts(RS0, c15, 0.0, ALU.not_equal)
+    IM9, IM9N = eye("B", 512.0 * MAGIC), eye("B", -512.0 * MAGIC)
+    away, cc = pair("U", 16), new("F", 16)
+    ts(part(cc, 0, 8), sl(cF, 0, 8), 7.0, ALU.add)
+    ts(part(cc, 1, 8), sl(cF, 0, 8), 6.0, ALU.add)
+    for h in range(2):
+        q3, m3, m4, a1, a2 = col("I"), col(), col(), new("I", 16), new("I", 16)
+        ts(q3, pF, 1.0 / 3, ALU.mult, (2 * h - 1) / 3.0, ALU.add)
+        ts(m3, q3, 3.0, ALU.mult, -2.0 * h, ALU.add)
+        tt(m4, m3, pF, ALU.subtract)
+        ts(a1, cc, m4, ALU.add)
+        ts(a2, a1, 7, ALU.bitwise_and)
+        ts(away[h], a2, 16.0, ALU.mult, 15.0, ALU.add)
+    eqm, vm, runV, cbF = pair("F", 128), pair("F", 128), pair("F", 128), pair("F", 8)
+    wideV = pair("F", 256)
+
     GW = OPT["gw"]
-    uH, uB, uC, aH, aB, aC, fB, fC, bad, q6, a6 = (new("B", 4096) for _ in range(11))
-    Z4, ZB4, ZC4 = pair("B", GW), pair("B", GW), pair("B", GW)
+    uH, uB, uC, aH, aB, aC, fB, fC, bad, q6 = (new("B", 4096) for _ in range(10))
+    a6 = aC
+    Z8, ZB4, ZC4 = pair("B", 2048), pair("B", GW), pair("B", GW)
+    Z4 = [sl(z, 0, GW) for z in Z8]
     DD = pair("B", 256)
-    D, us, uj, eq, eq2, mkB, thrR, thr6, sgn, kr = (pair("B", 128) for _ in range(10))
+    D, us, uj, eq, eq2, mkB, thrR, thr6, sgn, kr, zm = (pair("B", 128) for _ in range(11))
+    for h in range(2):
+        scaled(part(Z8[h], 1, 1024), sl(IBIG, 0, 1024), 0.0)
     QP, QG, TP, TG, TK = new("F", 288), new("F", 288), pair("F", 288), pair("F", 288), pair("F", 288)
     for qq in (QP, QG):
         fill(qq, 0.0)
-    move("A", sl(WIN, 512, X0), sl(IOTA, 512, X0))
+    move("G", sl(WIN, 512, X0), sl(IOTA, 512, X0))
     fill(sl(WIN, X0 + 2048, 2 * X0), 0.0)
     for kw in KW:
         for h in range(2):
@@ -777,6 +868,40 @@ def build(g, core, rank, T, topo, way):
         tt(out, sl(b[3], 0, 8), sl(b[3], 8, 16), ALU.min)
         return out
 
+    def sums_t(ps, sel, src, c, stop=True):
+        mm([(sl(ps, k % 16, width(ps), 16), part(src, k, 128), sel, False, stop and k % 16 == 15) for k in range(8 * c, 8 * c + 8)])
+
+    def hashed(h):
+        tt(eqm[h], ind(run16[h], rep15), keys[h], ALU.is_equal)
+        tt(vm[h], sl(S2[h], 128, 256), eqm[h], ALU.mult)
+        add("V", lambda: g.vector.tensor_tensor_scan(ap(runV[h]), ap(RS0), ap(vm[h]), 0.0, ALU.mult, ALU.add), [RS0, vm[h]], [runV[h]], 0.13)
+        for i in range(2):
+            tt(part(wideV[h], i, 128), ind(runV[h], part(away[h], i, 8)), E128, ALU.mult)
+        o, w = sl(Mh[h], 256, 264), part(wideV[h], 0, 128)
+        group([(o, w, SelN), (o, IM9, sl(ones, 0, 8)), (o, IM9N, sl(ones, 0, 8)), (o, w, SelF)])
+        ts(part(cU[h], 0, 8), o, 255.5, ALU.add)
+        ts(cbF[h], o, 255.5, ALU.add)
+        o = sl(Mh[h], 264, 272)
+        apart([(o, part(wideV[h], 1, 128), SelF)])
+        ts(part(vI[h], 1, 8), o, 255.5, ALU.add, 21.0, ALU.mult)
+        ts(part(cIi[h], 1, 8), part(vI[h], 1, 8), 2, ALU.arith_shift_right, 511, ALU.bitwise_and)
+        copy(part(cU[h], 1, 8), part(cIi[h], 1, 8))
+
+    def least_t(out, a, h, key=None, then=None):
+        add("V", lambda: g.vector.tensor_tensor_scan(ap(run16[h]), ap(RST), ap(a), 0.0, ALU.add, ALU.min), [RST, a], [run16[h]], 0.13)
+        if then:
+            then()
+        tt(wide[h], ind(run16[h], rep15), E128, ALU.mult)
+        o, p = sl(S2[h], 384, 392), sl(S2[h], 392, 400)
+        if key:
+            apart([(o, wide[h], SelF)])
+        if key and out is moff[h]:
+            key(o)
+        group([(p, wide[h], SelN), (p, IM8, sl(ones, 0, 8)), (p, IM8N, sl(ones, 0, 8)), (p, wide[h], SelF)])
+        if key and out is not moff[h]:
+            key(o)
+        ts(out, p, 16.0, ALU.mult, u1k, ALU.add)
+
     def place(o, lo, k):
         ts(lo, k, 255, ALU.bitwise_and)
         ts(o, lo, 16.0, ALU.mult, uF, ALU.add)
@@ -798,9 +923,9 @@ def build(g, core, rank, T, topo, way):
             group(items + [(ps, IR, ones)])
             act(out, ps, AF.Identity, bR, 1.0)
 
-    def gathers(u, win, o, z4, c):
-        for i in range(1024 * c // GW, 1024 * (c + 1) // GW):
-            tt(part(u, i, GW), ind(win, part(o, i, GW // 16)), z4, ALU.subtract)
+    def gathers(u, win, o, z4, c, n=GW):
+        for i in range(1024 * c // n, 1024 * (c + 1) // n):
+            tt(part(u, i, n), ind(win, part(o, i, n // 16)), sl(z4, 0, n), ALU.subtract)
 
     def minus(w, terms, c, d, neg=IN, rounds=False):
         for b in range(2):
@@ -832,12 +957,15 @@ def build(g, core, rank, T, topo, way):
         Gn = [sl(QG, 16 + 128 * h, 144 + 128 * h) for h in range(2)]
 
         def speaker(h):
-            M, raw = Mh[h], h in OPT["rawH"]
-            if not raw:
+            M, raws = Mh[h], [c in OPT["rawH"] for c in (2 * h, 2 * h + 1)]
+            if not all(raws):
                 e = "V" if rnd == 0 else "G"
                 move(e, sl(Z4[h], 0, 128), Z[h])
                 spread(e, Z4[h])
-            if OPT["thr"][h] != "P":
+            turned, fast = "H%d" % h in OPT["T"], h in OPT["fast"]
+            if turned:
+                tt(thrR[h], ind(thr, repb2 if h else repb), E128, ALU.mult)
+            elif OPT["thr"][h] != "P":
                 move(OPT["thr"][h], thrR[h], ind(thr, repk2 if h else repk))
             apart(lanes(sl(M, 0, 128), Z[h], 1, 1, h) + lanes(sl(M, 128, 256), Z[h], 2, 1, h))
             for i, zz in enumerate((ZB4[h], ZC4[h])):
@@ -845,16 +973,32 @@ def build(g, core, rank, T, topo, way):
                 spread("G", zz)
             ds, cs = sl(S2[h], 0, 128), sl(M, 0, 128)
             for c in (2 * h, 2 * h + 1):
-                cut = pieces("H%d%d" % (h, c % 2), c)
+                cut, raw = pieces("H%d%d" % (h, c % 2), c), raws[c % 2]
                 if raw:
                     w = nextw()
                     act(part(uH, c, 1024), ind(win, part(KU, c, 64)), AF.Copy)
                     minus(w, [(I1, uH)], c, Z[h])
                 else:
-                    gathers(uH, win, KU, Z4[h], c)
+                    gathers(uH, win, KU, Z4[h], c, OPT["gwH"][h])
+                    if c == 0 and OPT["early"]:
+                        ops[-OPT["early"]]["r"].append(KU)
                 for a0, a1 in cut:
                     act(sl(aH, a0, a1), sl(w, a0 - 1024 * c, a1 - 1024 * c) if raw else sl(uH, a0, a1), AF.Abs)
                     ts(sl(bad, a0, a1), sl(aH, a0, a1), 48.0, ALU.is_gt, 2.0, ALU.mult)
+                if turned:
+                    both = sl(S2[h], 0, 256)
+                    if c % 2 == 0:
+                        if fast:
+                            mm([(both, I1, cP2, True, False), (part(both, 1, 128), I1, half128, False, False)])
+                        else:
+                            mm([(ds, I1, cP, True, False)])
+                        mm([(cs, thrR[h], BOm, True, False)])
+                    if fast:
+                        sums_t(both, SelDV, aH, c)
+                    else:
+                        sums_t(ds, SelD, aH, c, OPT["pen"][h] == "V")
+                    sums_t(cs, SelC, bad, c)
+                    continue
                 if OPT["pen"][h] == "V":
                     sums(ds, Zd, aH, c, (I1, cB))
                 else:
@@ -870,22 +1014,32 @@ def build(g, core, rank, T, topo, way):
             if OPT["pen"][h] == "V":
                 ts(pen[h], cs, 0.0, ALU.is_ge, 1048576.0, ALU.mult)
                 tt(keys[h], ds, pen[h], ALU.add)
-                least(kS[h], keys[h], h, "H%d" % h)
+                if fast:
+                    least_t(soff[h], keys[h], h, None, lambda: hashed(h))
+                elif turned:
+                    least_t(soff[h], keys[h], h)
+                else:
+                    least(kS[h], keys[h], h, "H%d" % h)
             else:
                 act(sgn[h], cs, AF.Sign, bhalf, 1.0)
                 mm([(ds, IB, sgn[h], False, True)])
-                if "H%d" % h not in OPT["red"]:
-                    move(OPT["ev"], lv[h][0], sl(ds, 0, 64))
-                least(kS[h], ds, h, "H%d" % h, lv[h][0])
-            place(soff[h], lo1[h], kS[h])
+                if turned:
+                    least_t(soff[h], ds, h)
+                else:
+                    if "H%d" % h not in OPT["red"]:
+                        move(OPT["ev"], lv[h][0], sl(ds, 0, 64))
+                    least(kS[h], ds, h, "H%d" % h, lv[h][0])
+            if not turned:
+                place(soff[h], lo1[h], kS[h])
             move(OPT["dg"][h], D[h], ind(part(aH, h, 2048), soff[h]))
             act(us[h], ind(part(uH, h, 2048), soff[h]), AF.Copy)
             apart(lanes(sl(M, 0, 128), D[h], 1, 1, h) + lanes(sl(M, 128, 256), D[h], 2, 1, h))
             move(OPT["dd"][h], DD[h], sl(M, 0, 256))
-            group(wsum(sl(M, 256, 272), Zv, DD[h]))
-            tt(vI[h], sl(M, 256, 272), c421, ALU.mult)
-            ts(cIi[h], vI[h], 2, ALU.arith_shift_right, 511, ALU.bitwise_and)
-            copy(cU[h], cIi[h])
+            if not fast:
+                group(wsum(sl(M, 256, 272), Zv, DD[h]))
+                tt(vI[h], sl(M, 256, 272), c421, ALU.mult)
+                ts(cIi[h], vI[h], 2, ALU.arith_shift_right, 511, ALU.bitwise_and)
+                copy(cU[h], cIi[h])
             for qq, t, o, i, e in ((QP, TP, PU, 0, OPT["plist"][h]), (QG, TG, GU, 1, OPT["glist"][h])):
                 move(e, sl(qq, 16 + 128 * h, 144 + 128 * h), ind(SW, part(cU[h], i, 8)))
                 copy(part(o, h, 128), ind(turn(t[h], qq, 16 + 128 * h), pickW))
@@ -903,7 +1057,11 @@ def build(g, core, rank, T, topo, way):
                 group([(o, I5, K[h]), (o, BOq, D[h]), (o, I1, c38), (o, IR, ones), (o, IRN, ones), (o, IN, kr[h])])
                 move("A", sl(kw_[h], 0, 128), o)
             o = sl(S, 128, 256)
-            rounded(sl(cz_[h], 128, 256), o, [(o, I1, quarter), (o, IH, us[h]), (o, IH if raw else I1, Z[h])])
+            aim = [(o, IH if any(raws) else I1, Z[h])]
+            if raws[0] != raws[1]:
+                move(OPT["zm"], zm[h], ind(Z8[h], soff[h]))
+                aim.append((o, IH, zm[h]))
+            rounded(sl(cz_[h], 128, 256), o, [(o, I1, quarter), (o, IH, us[h])] + aim)
             apart([(sl(M, 0, 128), sh(YF, -1), Gn[h])])
             act(GnB[h], sl(M, 0, 128), AF.Copy)
 
@@ -929,22 +1087,25 @@ def build(g, core, rank, T, topo, way):
                 minus(w, terms, c, d)
                 for a0, a1 in pieces(tag, c):
                     act(sl(f, a0, a1), sl(w, a0 - 1024 * c, a1 - 1024 * c), AF.Abs)
-                sums(es, z, f, c, (I1, cB))
-                if c % 2 == 0 and name + str(h) not in OPT["red"]:
-                    move(OPT["ev"], lv[h][0], sl(es, 0, 64))
-            return least(kk, es, h, name + str(h), lv[h][0])
+                if c % 2 == 0:
+                    mm([(es, I1, cP, True, False)])
+                sums_t(es, SelE if name == "B" else SelG, f, c)
+            least_t(kk, es, h, z)
 
         def partner(h):
-            M, raw, rawb = Mh[h], h in OPT["rawH"], h in OPT["rawB"]
-            look("B", h, uB, aB, fB, PU, ZB4[h], sl(DD[h], 0, 128), Ze, kE[h])
-            place(joff[h], lo2[h], kE[h])
+            M, raw, rawb = Mh[h], 2 * h in OPT["rawH"] and 2 * h + 1 in OPT["rawH"], h in OPT["rawB"]
+            def bounds(key):
+                ts(cp1[h], key, 640.0 * 256 - 100, ALU.is_lt, 1.0, ALU.add)
+                ts(thrE[h], key, a256, ALU.add)
+            look("B", h, uB, aB, fB, PU, ZB4[h], sl(DD[h], 0, 128), bounds, joff[h])
+            if h in OPT["dp"]:
+                o = sl(S2[h], 256, 384)
+                group([(o, INF, K[h])] + lanes(o, Pn[h], 1, -1, h, YF))
             tt(PM[h], ind(IBIG, joff[h]), Pn[h], ALU.mult)
             act(uj[h], ind(part(uB, h, 2048), joff[h]), AF.Copy)
             act(mkB[h], ind(IBIG, joff[h]), AF.Copy)
             group([(sl(M, 384, 392), I2K, sl(ones, 0, 8))] + wsum(sl(M, 384, 392), Zh, PM[h]))
-            ts(cp1[h], kE[h], 640.0 * 256, ALU.is_lt, 1.0, ALU.add)
             tt(addB[h], sl(M, 384, 392), cp1[h], ALU.mult)
-            ts(thrE[h], kE[h], a256, ALU.add)
             back = lambda out: lanes(out, uj[h], 1, -1, h)
             if not raw:
                 if rawb:
@@ -961,15 +1122,19 @@ def build(g, core, rank, T, topo, way):
             rounded(sl(CV[h], 128, 256), o, [(o, I1, quarter), (o, IH, uj[h]), (o, IH, sl(DD[h], 0, 128))] + ([] if rawb else [(o, IH, sl(ZB4[h], 0, 128))]))
 
         def contact(h):
-            S = P[OPT["s6bank"][h]]
-            cs, dp = sl(S, 0, 128), sl(S, 128, 256)
-            sizes = "V" not in OPT["s6"][2 * h:2 * h + 2]
-            if sizes:
-                act(thr6[h], ind(THR, part(LU, h, 8)), AF.Copy)
-                mm([(cs, IN, thr6[h], True, False)])
             for c in (2 * h, 2 * h + 1):
+                if OPT["s6w"][h]:
+                    d = sl(cz_[h], 256, 384) if c in OPT["rawH"] else sl(cz_[h], 384, 512)
+                    for b in (2 * c, 2 * c + 1):
+                        w, onact = P[OPT["s6w"][h][b % len(OPT["s6w"][h])]], OPT["s6"][c] == "P"
+                        group([(w, IS, part(uH, b, 512))] + [(part(w, i, 128), ISN, d) for i in range(4)] + ([(w, IM, ones4)] if onact else []))
+                        if onact:
+                            act(part(q6, b, 512), w, AF.Abs, bM, 1.0)
+                        else:
+                            ts(part(q6, b, 512), w, MAGIC128, ALU.add, MAGIC128, ALU.subtract)
+                    continue
                 w = nextw()
-                minus(w, [(IS, uH)], c, sl(cz_[h], 256, 384) if h in OPT["rawH"] else sl(cz_[h], 384, 512), ISN, OPT["s6"][c] == "P")
+                minus(w, [(IS, uH)], c, sl(cz_[h], 256, 384) if c in OPT["rawH"] else sl(cz_[h], 384, 512), ISN, OPT["s6"][c] == "P")
                 if OPT["s6"][c] == "V":
                     ts(part(q6, c, 1024), w, MAGIC128, ALU.add, MAGIC128, ALU.subtract)
                 elif OPT["s6"][c] == "P":
@@ -977,8 +1142,20 @@ def build(g, core, rank, T, topo, way):
                 else:
                     act(part(a6, c, 1024), w, AF.Abs)
                     ts(part(q6, c, 1024), part(a6, c, 1024), 63.5, ALU.is_gt, 128.0, ALU.mult)
-                mm([(cs, zu(Zq, k), part(q6, 16 * h + k, 128), k == 0 and not sizes, k == 15) for k in range(8 * (c % 2), 8 * (c % 2) + 8)])
-            group([(dp, INF, K[h])] + lanes(dp, Pn[h], 1, -1, h, YF))
+
+        def replace(h):
+            S = P[OPT["s6bank"][h]]
+            cs, dp = sl(S, 0, 128), sl(S, 128, 256)
+            sizes = "V" not in OPT["s6"][2 * h:2 * h + 2]
+            if sizes:
+                act(thr6[h], ind(THR, part(LU, h, 8)), AF.Copy)
+                mm([(cs, IN, thr6[h], True, False)])
+            for c in range(2):
+                mm([(cs, zu(Zq, k), part(q6, 16 * h + k, 128), k == 0 and not sizes, k == 15) for k in range(8 * c, 8 * c + 8)])
+            if h in OPT["dp"]:
+                dp = sl(S2[h], 256, 384)
+            else:
+                group([(dp, INF, K[h])] + lanes(dp, Pn[h], 1, -1, h, YF))
             if sizes:
                 ts(off[h], cs, 0.0, ALU.is_ge)
             else:
@@ -988,17 +1165,15 @@ def build(g, core, rank, T, topo, way):
             tt(sl(kw_[h], 256, 384), dp, K[h], ALU.add)
 
         def guesser(h):
-            found[h] = look("C", h, uC, aC, fC, GU, ZC4[h], sl(DD[h], 128, 256), Zf, kG[h])
+            look("C", h, uC, aC, fC, GU, ZC4[h], sl(DD[h], 128, 256), lambda key: tt(part(NH_, h, 8), key, thrE[h], ALU.is_ge), moff[h])
 
         def decide(h):
             M = Mh[h]
             nh, s3 = part(NH_, h, 8), part(s3w, h, 8)
-            tt(nh, found[h], thrE[h], ALU.is_ge)
             tt(kvm[h], nh, addB[h], ALU.mult)
-            tt(kv[h], kvm[h], sl(cIi[h], 0, 8), ALU.max)
+            tt(kv[h], kvm[h], cbF[h] if h in OPT["fast"] else sl(cIi[h], 0, 8), ALU.max)
             ts(kvU[h], kv[h], 2.0 * X0, ALU.min)
             tt(s3, nh, cp1[h], ALU.mult)
-            place(moff[h], lo3[h], kG[h])
             group([(sl(M, 0, 16), I1, cz), (sl(M, 8, 16), I1, nh)]
                   + [(sl(M, b, 8, 3), PB[(b + 2 * h) % 3], sl(s3, b, 8, 3)) for b in range(3)])
             ts(zs[h], sl(M, 0, 16), 128.0, ALU.mult, uF, ALU.add)
@@ -1039,7 +1214,7 @@ def build(g, core, rank, T, topo, way):
         act(thr, L, AF.Exp, b17, -LN2)
         for h in range(2):
             speaker(h)
-        step = {"B": partner, "C": guesser, "S": contact, "D": decide}
+        step = {"B": partner, "C": guesser, "S": contact, "T": replace, "D": decide}
         for s in OPT["order"]:
             step[s[0]](int(s[1]))
         for h in range(2):
@@ -1084,4 +1259,12 @@ def build(g, core, rank, T, topo, way):
             src = T.lol[:, rows, :] if k == "ol" else T["l" + k][:]
             dma("A", out[k][1], src, [("l" + k, 0, 8), ("call%d" % ci, 0, 1), KO, Xb], [("y" + k, 0, 1)], out[k][2], ext=arr(ci))
     ops[0]["end"] = [(T.sem.sent, sent[0])]
-    return ops
+    used, kept = {}, []
+    for o in ops[::-1]:
+        if o["tie"][0] == "once" and o["e"] in "VA" and not o["dma"] and not any(
+                lo < w[2] and w[1] < hi for w in o["w"] for lo, hi in used.get(w[0], ())):
+            continue
+        kept.append(o)
+        for a in o["r"]:
+            used.setdefault(a[0], set()).add((a[1], a[2]))
+    return kept[::-1]

@@ -2,7 +2,7 @@ import math
 from concourse.bass import DstId, RemoteDMATransfer
 from concourse.mybir import AluOpType as ALU, AxisListType as AX, ActivationFunctionType as AF
 
-NF, NB, NI, NU, NH = 19968, 69632, 3072, 1536, 1024
+NF, NB, NI, NU, NH = 17408, 71680, 3072, 1536, 2560
 SCRATCH = {
     "F": ("sbuf", [128, NF], "float32"), "B": ("sbuf", [128, NB], "bfloat16"), "I": ("sbuf", [128, NI], "int32"),
     "U": ("sbuf", [128, NU], "uint16"), "H": ("sbuf", [128, NH], "float16"),
@@ -12,40 +12,72 @@ SCRATCH = {
 }
 KINDS = {"iz": (32, "bfloat16"), "il": (16, "int32"), "ik": (32, "int32"), "ix": (128, "bfloat16"), "iy": (128, "bfloat16"), "ia": (64, "int32"),
          "oz": (32, "bfloat16"), "ol": (16, "float32"), "ox": (128, "bfloat16"), "oy": (128, "bfloat16"), "oa": (64, "float32"), "ok": (32, "float32")}
-CALLS = [("iz", "il"), ("ik",), ("ix",), ("iy",), ("ia",), ("oz", "ol"), ("oa",), ("ox",), ("oy",), ("ok",)]
+CALLS = [("ik",), ("ix",), ("iy",), ("iz", "il"), ("ia",), ("oz", "ol"), ("ox",), ("oy",), ("oa",), ("ok",)]
 for _k, (_n, _d) in KINDS.items():
     SCRATCH["s" + _k] = ("dram", [1 if _k[1] == "l" else 8, 128, _n], _d)
     SCRATCH["l" + _k] = ("dram", [8, 128, _n], _d)
-NDMA = 44
+NDMA, WORLD = 44, 256
+PLAN = {}
 SEMAPHORES = ["cV", "cA", "cP", "cG", "sent"] + ["arr%d" % i for i in range(len(CALLS))] + ["d%d" % i for i in range(NDMA)]
 PSUM = ("W0", "W1", "SA", "SB", "M0", "M1")
 MAGIC = 12582912.0
-MAGIC128 = 1610612736.0
-OPT = {"rawH": (1, 3), "rawB": (), "rawC": (), "relu": (), "s6": "VVAP", "thr": "PP", "gw": 1024, "zm": "A",
-       "red": ("H0", "C1"), "cut": ("H00",), "order": ("B0", "C0", "B1", "S0", "T0", "C1", "D0", "S1", "T1", "D1"), "early": 0, "dd": "AA", "kg": "A", "ev": "V", "dg": "AA", "plist": "AA", "glist": "AA",
-       "cases": ((1.45, 2.0, 0.15), (1.25, 1.56, 0.3)), "slack": 1.0, "tied": 4, "moves": 0, "heat": 0.1, "ncase": 2, "same": 0, "whole": 0, "span": 8, "s6w": ((), ()), "fast": (0,), "T": ("H0", "H1", "B0", "B1", "C0", "C1"), "s6bank": ("SA", "M0"), "pbank": "SB",
-       "pen": "VV", "rnd": "A", "kh": "VV", "dp": (0,), "give": 0.0, "seed": 12345, "leg": 300, "starts": 3, "gwH": (512, 512), "hop": 3.5, "lat": 0.22, "ga": 1.56, "iters": 2800, "amp": 0.5}
+OPT = {"split": 9.0, "raw": ("H01", "H11"), "relu": (), "cut": {"H00": 512, "H01": 512, "C10": 512, "C11": 512}, "s6": "VVPP", "fast": (0,), "kh": "PP",
+       "order": "H00 H01 h0 H10 H11 h1 B00 B01 b0 C00 C01 c0 B10 S00 B11 b1 S01 t0 C10 C11 c1 S10 S11 t1 d0 d1 w0 w1 e0 e1 p0", "cs": "AA",
+       "eng": {"thr": "AA", "dg": "AA", "us": "AA", "dd": "AA", "pl": "AA", "gl": "AA", "kh": "VV", "zm": "AA", "uj": "AA", "mk": "AA", "cz": "AA",
+               "cv": "AA", "gn": "AA", "kr": "AA", "t6": "AA", "zz": "AA", "zs": "AA", "zf": "AA"},
+       "gw": 1024, "gwH": 512, "cases": ((1.0, 1.56, 0.22), (1.0, 1.56, 0.32), (1.4, 2.0, 0.15), (1.15, 1.56, 0.42), (1.25, 1.1, 0.18)), "slack": 1.5, "seed": 2,
+       "vfix": 0.005, "afix": 0.065, "dma": 1.5, "hop": 2.8, "lat": 0.25, "slow": 1.12, "ga": 1.56, "iters": 5200, "polish": 4000, "heat": 0.2, "rough": 200, "near": 3.0, "again": 0.6,
+       "table": {"H00": 0, "H01": 0, "H10": 3, "H11": 6, "B00": 7, "B01": 9, "C00": 12, "C01": 14, "B10": 16, "B11": 18, "C10": 20, "C11": 22, "S00": 16,
+                 "S01": 19, "S10": 26, "S11": 27, "h0": 4, "h1": 10, "b0": 13, "c0": 18, "b1": 21, "c1": 25, "w0": 23, "w1": 29, "e0": 26, "e1": 32, "round": 34}}
 
 
 def routes(T, topo):
+    if "way" in PLAN:
+        return PLAN["way"]
     cores = T.cores
-    n = len(cores)
+    chip = lambda c: topo.cores_of(c)[0]
+    mate = {chip(c): [m for m in range(WORLD) if topo.mates(c, m)] for c in cores}
+    mate.update({chip(m[0]): topo.cores_of(c) for c, m in list(mate.items())})
+
+    def links(a, b):
+        if chip(a) == chip(b):
+            return []
+        if topo.same_plane(a, b):
+            return [("out", chip(a), topo.die(a)), ("in", chip(b), topo.die(a))]
+        over = [("mate", chip(a), topo.die(a))]
+        return over if topo.mates(a, b) else over + [("out", chip(mate[chip(a)][0]), topo.die(a)), ("in", chip(b), topo.die(a))]
+
+    can = {}
+    for s, a in enumerate(cores):
+        for r, b in enumerate(cores):
+            if s != r:
+                can[(s, r)] = [c for c in topo.cores_of(a) + mate[chip(b)] if (c == a or (c not in cores and topo.may_write(a, c))) and topo.may_write(c, b)]
+    cost = {p: {c: links(cores[p[0]], c) + links(c, cores[p[1]]) + [("off", p[0])] * (c == cores[p[0]] or chip(c) != chip(cores[p[0]]))
+                for c in cs} for p, cs in can.items()}
+
+    def price(way):
+        load = {}
+        for p, c in way.items():
+            for l in cost[p][c]:
+                load[l] = load.get(l, 0) + 1
+        return sum((v + (l[0] == "off")) ** 4 for l, v in load.items())
     way = {}
-    for s in range(n):
-        me = cores[s]
-        kin = [r for r in range(n) if r == s or topo.may_write(me, cores[r])]
-        far = [r for r in range(n) if r not in kin]
-        others = [c for c in topo.cores_of(me) if c != me]
-        port = [c for c in others if far and all(topo.may_write(c, cores[r]) for r in far)]
-        byd = [[c for c in port if topo.die(c) == topo.die(me)], [c for c in port if topo.die(c) != topo.die(me)]]
-        i = kin.index(s)
-        for j, r in enumerate(far):
-            side = byd[(i + j) % 2] if byd[(i + j) % 2] else byd[(i + j + 1) % 2]
-            way[(s, r)] = side.pop(0)
-        free = [c for c in others if c not in port and topo.die(c) != topo.die(me)]
-        for j in range(len(kin) - 1, 0, -1):
-            r = kin[(i + j) % len(kin)]
-            way[(s, r)] = free.pop(0) if free and j > 1 else me
+    for p in sorted(can, key=lambda p: len(can[p])):
+        way[p] = min((c for c in can[p] if c == cores[p[0]] or c not in way.values()), key=lambda c: price(dict(way, **{}) | {p: c}))
+    best, moved = price(way), True
+    while moved:
+        moved = False
+        for p in can:
+            for q in can:
+                for c in can[p]:
+                    for d in (can[q] if p < q and (p[0] == q[0] or p[1] == q[1]) else [way[q]] if p == q else []):
+                        new = dict(way)
+                        new[q] = d
+                        new[p] = c
+                        relays = [x for x in new.values() if x not in cores]
+                        if len(set(relays)) == len(relays) and price(new) < best:
+                            way, best, moved = new, price(new), True
+    PLAN["way"] = way
     return way
 
 
@@ -59,14 +91,17 @@ def bits(es):
 def first_hop(T, topo, way, s, ci):
     me = T.cores[s]
     items = [(k, r) for r in range(len(T.cores)) if r != s for k in CALLS[ci]]
-    items.sort(key=lambda it: way[(s, it[1])] != me)
+    to = {r: T.cores[r] if way[(s, r)] == me else way[(s, r)] for k, r in items}
+    items.sort(key=lambda it: len(topo.engines(me, to[it[1]])))
     per = 2 if len(CALLS[ci]) == 1 else 1
+    spare = len(topo.engines(me, me)) - per * len(items)
     used, out = [], []
     for k, r in items:
-        to = T.cores[r] if way[(s, r)] == me else way[(s, r)]
-        es = [e for e in topo.engines(me, to) if e not in used][:2 * per if to == T.cores[r] else per]
+        more = per if spare >= per and to[r] not in topo.cores_of(me) else 0
+        spare -= more
+        es = [e for e in topo.engines(me, to[r]) if e not in used][:per + more]
         used += es
-        out.append((k, r, to, es))
+        out.append((k, r, to[r], es))
     return out
 
 
@@ -115,65 +150,100 @@ def rank_program(g, core, T, topo):
     emit(g, T, ops)
 
 
-PLAN = {}
-
-
-def arrange(ops):
-    n, lat = len(ops), OPT["lat"]
-    hist, preds = {}, []
+def depend(ops):
+    hist, preds, starts, held = {}, [], {}, {}
     for i, o in enumerate(ops):
         p = {}
         for acc, isw in [(a, False) for a in o["r"]] + [(a, True) for a in o["w"]]:
             name, lo, hi = acc[0], acc[1], acc[2]
-            ps = name in PSUM
-            st = acc[3] if len(acc) > 3 and not ps else 1
-            if ps:
-                lo, hi = lo // 512 * 512, (hi + 511) // 512 * 512
+            st = acc[3] if len(acc) > 3 else 1
             for bk in range(lo // 256, (hi - 1) // 256 + 1):
                 keep = []
                 for (j, l2, h2, w2, s2) in hist.get((name, bk), []):
                     hit = l2 < hi and lo < h2 and not (st == s2 and (lo - l2) % st)
                     same = ops[j]["e"] == o["e"] and not (o["dma"] or ops[j]["dma"])
-                    if j != i and hit and (isw or w2 or (ps and not same)):
+                    if j != i and hit and (isw or w2):
                         p[j] = p.get(j, False) or not ((same and o["e"] == "P") or name.startswith("call"))
                     cover = st == 1 and lo <= max(l2, 256 * bk) and min(h2, 256 * bk + 256) <= hi
-                    if not (hit and isw and cover and j != i and not (ps and same and w2 and o["e"] != "P")):
+                    if not (hit and isw and cover and j != i):
                         keep.append((j, l2, h2, w2, s2))
                 keep.append((i, lo, hi, isw, st))
                 hist[(name, bk)] = keep
+        for bank, begins, stays in o["acc"]:
+            if begins:
+                for j in ([held[bank]] if bank in held else []) + (starts.pop(bank, []) if stays else []):
+                    p.setdefault(j, False)
+                if not stays:
+                    starts.setdefault(bank, []).append(i)
+            else:
+                if bank in held and held[bank] != i:
+                    p.setdefault(held[bank], False)
+            if stays or not begins:
+                held[bank] = i
         preds.append(p)
+    return preds
+
+
+def arrange(ops):
+    n, lat = len(ops), OPT["lat"]
+    preds = depend(ops)
     succ = [[] for _ in range(n)]
     for i in range(n):
         for j in preds[i]:
             succ[j].append(i)
-    eng, c = [o["e"] for o in ops], [max(o["c"], 0.001) for o in ops]
+    fixed = [o["dma"] or o["ext"] or o["x"] > 1 or o["c"] == 1.0 for o in ops]
+    eng, c = [o["e"] for o in ops], [max(ops[i]["c"] * (1.0 if fixed[i] else OPT["slow"]), 0.001) for i in range(n)]
+    banks = [sorted({(a[0], b) for a in o["r"] + o["w"] if a[0] in PSUM for b in range(a[1] // 512, (a[2] - 1) // 512 + 1)}) for o in ops]
     lag = [{j: (ops[j]["x"] + lat if sem or ops[j]["x"] > 1 else 0.0) for j, sem in preds[k].items()} for k in range(n)]
     fw = [list(lag[k].items()) for k in range(n)]
     bw = [[(k, lag[k][j]) for k in succ[j]] for j in range(n)]
+    pad = lat + 0.05
 
     def place(seq, dep, head):
-        end = [0.0] * n
-        busy = {e: ([], []) for e in "VAPGS"}
+        end, why = [0.0] * n, [-1] * n
+        busy = {e: ([], [], []) for e in "VAPGS"}
+        used = {b: ([], [], []) for bs in banks for b in bs}
         for i in seq:
-            t = head[i]
+            t, ci, w, e = head[i], c[i], -1, eng[i]
             for j, d in dep[i]:
                 if end[j] + d > t:
-                    t = end[j] + d
-            los, his = busy[eng[i]]
-            a, b = 0, len(his)
-            while a < b:
-                m = (a + b) // 2
-                if his[m] <= t:
-                    a = m + 1
-                else:
-                    b = m
-            while a < len(los) and los[a] < t + c[i] - 1e-9:
-                t = max(t, his[a])
-                a += 1
+                    t, w = end[j] + d, j
+            los, his, who = busy[e]
+            m = a = len(los)
+            while a and his[a - 1] > t:
+                a -= 1
+            while True:
+                while a < m and los[a] < t + ci - 1e-9:
+                    if his[a] > t:
+                        t, w = his[a], who[a]
+                    a += 1
+                if not banks[i]:
+                    break
+                t0 = t
+                for b in banks[i]:
+                    l2, h2, w2 = used[b]
+                    k = len(l2)
+                    while k and h2[k - 1] > t - pad + 1e-9:
+                        k -= 1
+                    while k < len(l2) and l2[k] < t + ci + pad - 1e-9:
+                        if eng[w2[k]] != e:
+                            t, w = h2[k] + pad, w2[k]
+                        k += 1
+                if t == t0:
+                    break
             los.insert(a, t)
-            his.insert(a, t + c[i])
-            end[i] = t + c[i]
-        return end
+            his.insert(a, t + ci)
+            who.insert(a, i)
+            end[i], why[i] = t + ci, w
+            for b in banks[i]:
+                l2, h2, w2 = used[b]
+                k = len(l2)
+                while k and h2[k - 1] > t:
+                    k -= 1
+                l2.insert(k, t)
+                h2.insert(k, t + ci)
+                w2.insert(k, i)
+        return end, why
 
     def feasible(key, dep, forward):
         k2 = list(key)
@@ -184,180 +254,130 @@ def arrange(ops):
         return sorted(range(n), key=lambda i: k2[i])
 
     zero, tailx = [0.0] * n, [o["x"] for o in ops]
-    prio = [0.0] * n
-    for i in range(n - 1, -1, -1):
-        prio[i] = c[i] + max([prio[k] + d for k, d in bw[i]] + [ops[i]["x"]])
     cases = []
     for f, ga, wake in OPT["cases"]:
-        cc = [c[i] if ops[i]["dma"] or ops[i]["ext"] or ops[i]["x"] > 1 else f * (c[i] + ops[i]["g"] * (ga - OPT["ga"])) for i in range(n)]
-        cases.append((cc, [[(j, d + wake - lat if preds[k][j] else d) for j, d in fw[k]] for k in range(n)]))
+        cc = [c[i] if fixed[i] else f * (ops[i]["c"] + ops[i]["g"] * (ga - OPT["ga"])) for i in range(n)]
+        cases.append((cc, [[(j, d + wake - lat if preds[k][j] else d) for j, d in fw[k]] for k in range(n)], wake))
+    outs = [i for i in range(n) if not succ[i]]
 
-    def replay(seq, cc, dep):
-        end, free = [0.0] * n, {e: 0.0 for e in "VAPGS"}
+    def replay(seq, cc, dep, wake):
+        end, free, last = [0.0] * n, {e: 0.0 for e in "VAPGS"}, {}
         for i in seq:
-            t = free[eng[i]]
+            e = eng[i]
+            t = free[e]
             for j, d in dep[i]:
                 if end[j] + d > t:
                     t = end[j] + d
-            end[i] = free[eng[i]] = t + cc[i]
-        return max(end[i] + tailx[i] for i in outs)
-    outs = [i for i in range(n) if not succ[i]]
+            for b in banks[i]:
+                for e2 in "VAP":
+                    if e2 != e and last.get((b, e2), 0.0) > t:
+                        t = last[(b, e2)]
+            end[i] = free[e] = t + cc[i]
+            for b in banks[i]:
+                last[(b, e)] = end[i] + tailx[i] + wake
+        return max(end[i] + tailx[i] for i in outs), end
+
     twins = {}
     for i, o in enumerate(ops):
         twins.setdefault(o["tie"], []).append(i)
-    steps = {}
-    for i, o in enumerate(ops):
-        if o["tie"][0] != "once":
-            steps.setdefault((o["tie"][0], o["tie"][1] // OPT["span"], o["e"] if o["c"] > 0.4 else ""), []).append(i)
-    steps = list(steps.values())
-    key, best, top, seed = [-p for p in prio], None, None, OPT["seed"]
-    for it in range(OPT["iters"]):
-        if it and it % OPT["leg"] == 0 and it <= OPT["leg"] * OPT["starts"]:
-            if it < OPT["leg"] * OPT["starts"]:
-                key, best = [-p for p in prio], None
-            else:
-                key, best = [top[1][i] - c[i] for i in range(n)], top
-        end = place(feasible(key, fw, True), fw, zero)
-        span = max(end[i] + tailx[i] for i in outs)
-        if best is None or span <= best[2] + OPT["slack"]:
-            seq = sorted(range(n), key=lambda i: (end[i] - c[i], i))
-            tot = span + sum(replay(seq, cc, dep) for cc, dep in cases)
-            if best is None or tot <= best[0] + OPT["give"] * (1.0 - it / OPT["iters"]):
-                best = (tot, end, span)
-                if top is None or tot < top[0]:
-                    top = best
-        src = best[1] if it % 2 == 1 else end
-        noise = [0.0] * n
-        if it % 2 == 1:
-            seed = (seed * 1103515245 + 12345) % 2147483648
-            lo = best[2] * seed / 2147483648.0 - 4.0
-            amp = OPT["amp"] * (1 + seed // 64 % 6)
-            tied = seed // 1024 % 4 < OPT["tied"]
-            if seed // 8192 % 4 < OPT["whole"]:
-                lo = -9.0
-                for _ in range(2):
-                    seed = (seed * 1103515245 + 12345) % 2147483648
-                    step = steps[seed // 256 % len(steps)]
-                    seed = (seed * 1103515245 + 12345) % 2147483648
-                    for i in step:
-                        noise[i] = 2 * amp * (seed / 2147483648.0 - 0.5)
-            for i in range(n):
-                if lo < src[i] < lo + 8.0:
-                    seed = (seed * 1103515245 + 12345) % 2147483648
-                    for j in (twins[ops[i]["tie"]] if tied else (i,)):
-                        noise[j] = amp * (seed / 2147483648.0 - 0.5)
-        back = place(feasible([-src[i] + noise[i] for i in range(n)], bw, False), bw, tailx)
-        key = [-back[i] for i in range(n)]
-    best = top
-    order = feasible([best[1][i] - c[i] for i in range(n)], fw, True)
-    cases = [(c, fw)] + cases
-    qi = ["VAPGS".index(e) for e in eng]
+    seed = [OPT["seed"]]
 
-    def times(seq, cc, dep, old, k0):
-        end, why = (list(old[0]), list(old[1])) if old else ([0.0] * n, [-1] * n)
-        lastq = [-1] * 5
-        k, miss = k0 - 1, 5
-        while k >= 0 and miss:
-            if lastq[qi[seq[k]]] < 0:
-                lastq[qi[seq[k]]] = seq[k]
-                miss -= 1
-            k -= 1
-        for k in range(k0, n):
-            i = seq[k]
-            w = lastq[qi[i]]
-            t = end[w] if w >= 0 else 0.0
-            for j, d in dep[i]:
-                if end[j] + d > t:
-                    t, w = end[j] + d, j
-            end[i], why[i] = t + cc[i], w
-            lastq[qi[i]] = i
+    def draw():
+        seed[0] = (seed[0] * 1103515245 + 12345) % 2147483648
+        return (seed[0] + 1) / 2147483649.0
+
+    def forth(key):
+        end, why = place(feasible(key, fw, True), fw, zero)
         e = max(outs, key=lambda i: end[i] + tailx[i])
-        return end, why, end[e] + tailx[e], e
+        return end[e] + tailx[e], end, why, e
 
-    def ahead(seq, v, u):
-        a, b = seq.index(u), seq.index(v)
-        if a > b:
-            return None
-        must, lastq, front = set(preds[v]), set(), []
-        for k in range(b - 1, a - 1, -1):
-            i = seq[k]
-            if i in must or qi[i] in lastq:
-                if qi[i] == qi[v]:
-                    return None
-                front.append(i)
-                lastq.add(qi[i])
-                must.update(preds[i])
-        moved = set(front)
-        return seq[:a] + front[::-1] + [v] + [i for i in seq[a:b] if i not in moved] + seq[b + 1:], a
+    def again(s):
+        back = place(feasible([-t for t in s[1]], bw, False), bw, tailx)[0]
+        return min(s, forth([-t for t in back]), key=lambda x: x[0])
 
-    cases = cases[:OPT["ncase"]]
-    if OPT["same"]:
-        st = [best[1][i] - c[i] for i in range(n)]
-        mark = twins[("round", OPT["same"])]
-        key = list(st)
-        for tw in twins.values():
-            if len(tw) > 1:
-                for r, i in enumerate(tw):
-                    key[i] = st[tw[1]] - st[mark[1]] + st[mark[r]]
-        alike = feasible(key, fw, True)
-        if sum(times(alike, cc, dep, None, 0)[2] for cc, dep in cases) < sum(times(order, cc, dep, None, 0)[2] for cc, dep in cases) + 6:
-            order = alike
-    cur = [times(order, cc, dep, None, 0) for cc, dep in cases]
-    tot = sum(x[2] for x in cur)
-    keep = (tot, order, cur[0][0])
-    for it in range(OPT["moves"]):
-        seed = (seed * 1103515245 + 12345) % 2147483648
-        end, why, span, i = cur[seed // 4096 % len(cases)]
-        arcs = []
+    marks, table = {}, dict(OPT["table"])
+    for i, o in enumerate(ops):
+        k = o["tie"][0].strip("!-")
+        r = 2 if "!" in o["tie"][0] else twins[o["tie"]].index(i)
+        if k in table and (k, r) not in marks.values() and (o["g"] > 0.2 if k[0] in "HBC" else eng[i] in "VA" and o["c"] > 0.3 if k[0] == "S" else eng[i] == "V"):
+            marks[i] = (k, r)
+
+    def timed(tb):
+        key = [0.0] * n
+        for i in range(n - 1, -1, -1):
+            t = min([key[k] - d for k, d in bw[i]] + [OPT["slow"] * (3 * tb["round"] + 12) - tailx[i]]) - c[i]
+            key[i] = min(t, OPT["slow"] * (tb[marks[i][0]] + marks[i][1] * tb["round"])) if i in marks else t
+        return again(forth(key))
+    cur, names = timed(table), sorted(table)
+    for it in range(OPT["rough"]):
+        tb = dict(table)
+        for _ in range(1 + int(3 * draw())):
+            tb[names[int(draw() * len(names))]] += (draw() - 0.5) * (1.0, 3.0, 6.0)[int(3 * draw())]
+        new = timed(tb)
+        if new[0] <= cur[0] - 0.4 * (1.0 - it / OPT["rough"]) * math.log(draw()):
+            cur, table = new, tb
+    def judged(s, m):
+        seq = sorted(range(n), key=lambda i: (s[1][i] - c[i], i))
+        return (s[0] + sum(replay(seq, cc, dep, wake)[0] for cc, dep, wake in cases[:m])) / (m + 1)
+    top, now, m, heat = None, 0.0, 0, OPT["heat"]
+    for it in range(OPT["iters"] + OPT["polish"]):
+        if it == OPT["iters"]:
+            cur, m = top[1], len(cases)
+            now = judged(cur, m)
+            top = (now, cur)
+        heat = OPT["heat"] * (1.0 - it / OPT["iters"]) if m == 0 else 0.03
+        span, end, why, i = cur
+        key, arcs = [end[k] - c[k] for k in range(n)], []
         while why[i] >= 0:
-            if qi[why[i]] == qi[i] and why[i] not in preds[i]:
+            if why[i] not in preds[i]:
                 arcs.append(i)
             i = why[i]
-        if not arcs:
-            break
-        seed = (seed * 1103515245 + 12345) % 2147483648
-        v = arcs[seed // 256 % len(arcs)]
-        a = order.index(why[v])
-        for _ in range(seed // 16 % 3):
-            k = a - 1
-            while k >= 0 and qi[order[k]] != qi[v]:
-                k -= 1
-            if k >= 0:
-                a = k
-        u = order[a]
-        tv, tu = twins[ops[v]["tie"]], twins[ops[u]["tie"]]
-        shift = tu.index(u) - tv.index(v)
-        pairs = [(tv[r], tu[r + shift]) for r in range(len(tv)) if 0 <= r + shift < len(tu)] if seed // 4 % 4 < OPT["tied"] else [(v, u)]
-        seq, low = order, n
-        for v2, u2 in pairs:
-            got = ahead(seq, v2, u2)
-            if got:
-                seq, low = got[0], min(low, got[1])
-        if low == n:
-            continue
-        new = [times(seq, cc, dep, cur[k], low) for k, (cc, dep) in enumerate(cases)]
-        t2 = sum(x[2] for x in new)
-        seed = (seed * 1103515245 + 12345) % 2147483648
-        if t2 <= tot - OPT["heat"] * (1.0 - it / OPT["moves"]) * math.log((seed + 1) / 2147483649.0):
-            order, cur, tot = seq, new, t2
-            if tot < keep[0]:
-                keep = (tot, order, cur[0][0])
-    order = keep[1]
-    start = [keep[2][i] - c[i] for i in range(n)]
-    fin = [keep[2][i] + tailx[i] for i in range(n)]
+        if arcs and draw() < 0.75:
+            v = arcs[int(draw() * len(arcs))]
+            u = why[v]
+            d = key[v] - key[u] + (0.01, 0.01, 0.3, 0.8, 1.5)[int(draw() * 5)]
+            if draw() < 0.5:
+                todo = [(j, key[j] - d) for j in twins[ops[v]["tie"]]]
+                while todo:
+                    j, t = todo.pop()
+                    if key[j] > t:
+                        key[j] = t
+                        todo += [(k, t - 1e-4) for k in preds[j]]
+            else:
+                for j in twins[ops[u]["tie"]]:
+                    key[j] += d
+        else:
+            lo, amp = span * draw() - 3.0, 0.5 * (1 + int(4 * draw()))
+            for k in range(n):
+                if lo < key[k] < lo + 6.0:
+                    d = amp * (draw() - 0.5)
+                    for j in twins[ops[k]["tie"]]:
+                        key[j] = end[j] - c[j] + d
+        new = forth(key)
+        if new[0] < span + OPT["near"] and draw() < OPT["again"]:
+            new = again(new)
+        if new[0] < span + (OPT["slack"] if m == 0 else 0.6):
+            tot = judged(new, m) if m else new[0]
+            if top is None or tot <= now - heat * math.log(draw()):
+                cur, now = new, tot
+                if top is None or tot < top[0]:
+                    top = (tot, cur)
+    order = feasible([top[1][1][i] - c[i] for i in range(n)], fw, True)
+    end = replay(order, *cases[0])[1]
+    start = [end[i] - cases[0][0][i] for i in range(n)]
+    fin = [end[i] + tailx[i] for i in range(n)]
     pos, cnt = {}, {e: 0 for e in "VAPGS"}
     for i in order:
-        cnt[ops[i]["e"]] += 1
-        pos[i] = cnt[ops[i]["e"]]
+        cnt[eng[i]] += 1
+        pos[i] = cnt[eng[i]]
     known = {e: {} for e in "VAPGS"}
-    snap, waits, need = {}, {}, set()
+    snap, waits, need, last = {}, {}, set(), {}
     for i in order:
-        kn = known[ops[i]["e"]]
+        kn = known[eng[i]]
         best = {}
-        for j, sem in preds[i].items():
-            if not sem:
-                continue
-            key = ("d", j) if ops[j]["dma"] else ops[j]["e"]
+        turn = [last[(b, e)] for b in banks[i] for e in "VAP" if e != eng[i] and (b, e) in last]
+        for j in [j for j, sem in preds[i].items() if sem] + turn:
+            key = ("d", j) if ops[j]["dma"] else eng[j]
             if key not in best or pos[j] > pos[best[key]]:
                 best[key] = j
         ws = []
@@ -372,13 +392,15 @@ def arrange(ops):
                     kn[k2] = v
         waits[i] = ws
         snap[i] = dict(kn)
-    return order, waits, need, start, fin
+        for b in banks[i]:
+            last[(b, eng[i])] = i
+    return order, waits, need, start, fin, [replay(order, *cs)[0] for cs in cases]
 
 
 def emit(g, T, ops):
     if "p" not in PLAN:
         PLAN["p"] = arrange(ops)
-    order, waits, need, start, fin = PLAN["p"]
+    order, waits, need = PLAN["p"][:3]
     q = {"V": g.vector, "A": g.scalar, "P": g.tensor, "G": g, "S": g.sync}
     num, cnt, nd, tail = {}, {e: 0 for e in "VAPG"}, 0, []
     for i in order:
@@ -410,6 +432,7 @@ def build(g, core, rank, T, topo, way):
     CY, GA, PC = 0.00083, OPT["ga"], 0.00042
     two = ("B", "U", "H")
     tie = ["once", 0]
+    EN = OPT["eng"]
 
     def new(pool, n):
         lo = top[pool]
@@ -445,7 +468,7 @@ def build(g, core, rank, T, topo, way):
     def val(x):
         return ap(x) if isref(x) else x
 
-    def add(e, f, r, w, c, x=0.0, dma=False, ext=()):
+    def add(e, f, r, w, c, x=0.0, dma=False, ext=(), acc=()):
         rr = []
         for a in r:
             if isref(a):
@@ -459,7 +482,8 @@ def build(g, core, rank, T, topo, way):
                 ww.append(a)
         gathered = sum(16 * width(a[2]) * CY for a in r if isref(a) and a[0] == "ind")
         tie[1] += 1
-        ops.append({"e": e, "f": f, "r": rr, "w": ww, "c": c, "x": x, "dma": dma, "ext": list(ext), "end": [], "g": gathered, "tie": tuple(tie)})
+        ops.append({"e": e, "f": f, "r": rr, "w": ww, "c": c, "x": x, "dma": dma, "ext": list(ext), "end": [], "g": gathered, "tie": tuple(tie),
+                    "acc": list(acc)})
 
     def vcost(out, a, k=1.0):
         if a[0] == "ind":
@@ -468,7 +492,7 @@ def build(g, core, rank, T, topo, way):
             return 0.05 + width(a) * 3.8 * CY
         if k == 1.0 and out[0] in two and a[0] in two:
             k = 0.5
-        return 0.02 + max(64, width(a) * k) * CY
+        return OPT["vfix"] + max(64, width(a) * k) * CY
 
     def copy(out, a):
         add("V", lambda: g.vector.tensor_copy(ap(out), ap(a)), [a], [out], vcost(out, a))
@@ -484,11 +508,16 @@ def build(g, core, rank, T, topo, way):
             f = lambda: g.vector.tensor_scalar(ap(out), ap(a), val(s1), val(s2), op0, op1)
         add("V", f, [a, s1, s2], [out], vcost(out, a))
 
+    def scan(out, a, b, op0, op1):
+        add("V", lambda: g.vector.tensor_tensor_scan(ap(out), ap(a), ap(b), 0.0, op0, op1), [a, b], [out],
+            OPT["vfix"] + width(out) * CY * (0.5 if out[0] == a[0] == b[0] == "B" else 1.0))
+
     def tr(out, a):
         add("V", lambda: g.vector.transpose(ap(out), ap(a)), [a], [out], vcost(out, a))
 
     def fill(out, v):
         add("V", lambda: g.vector.memset(ap(out), v), [], [out], vcost(out, out))
+        return out
 
     def reduce(out, a, op):
         add("V", lambda: g.vector.tensor_reduce(ap(out), ap(a), AX.X, op), [a], [out], 0.07)
@@ -499,19 +528,25 @@ def build(g, core, rank, T, topo, way):
                 return g.scalar.activation(ap(out), ap(a), fn)
             if bias is None:
                 return g.scalar.activation(ap(out), ap(a), fn, scale=val(scale))
-            return g.scalar.activation(ap(out), ap(a), fn, bias=val(bias), scale=scale)
-        c = 0.065 + width(out) * GA * CY if a[0] == "ind" else 0.1 + max(64, width(out)) * CY
+            return g.scalar.activation(ap(out), ap(a), fn, bias=val(bias), scale=val(scale))
+        c = 0.065 + width(out) * GA * CY if a[0] == "ind" else OPT["afix"] + max(64, width(out)) * CY
         add("A", f, [a, bias, scale], [out], c)
 
-    def scaled(out, a, w):
-        act(out, a, AF.Identity, None, w)
+    def scaled(out, a, w, e="A"):
+        if e == "A":
+            act(out, a, AF.Identity, None, w)
+        else:
+            ts(out, a, w, ALU.mult)
         return out
+
+    def select(out, a, pattern, op, cm):
+        add("G", lambda: g.affine_select(ap(out), ap(a), pattern, op, 0.0, 0, cm), [a], [out], 0.17 + 2 * CY * width(a))
 
     def move(e, out, a):
         if e == "A":
             act(out, a, AF.Copy)
         elif e == "G":
-            add("G", lambda: g.affine_select(ap(out), ap(a), [[0, width(a)]], ALU.is_ge, 0.0, 0, 0), [a], [out], 0.17 + 2 * CY * width(a))
+            select(out, a, [[0, width(a)]], ALU.is_ge, 0)
         else:
             copy(out, a)
 
@@ -521,26 +556,38 @@ def build(g, core, rank, T, topo, way):
             for out, l, r, st, sp in items:
                 last = g.tensor.matmul(ap(out), ap(l), ap(r), st, sp)
             return last
-        c = sum(max(64, width(r)) * (4 if l[0] == "F" else 1) * PC for out, l, r, st, sp in items)
-        add("P", f, [x for it in items for x in it[1:3]], [it[0] for it in items], c, x=0.1)
+        c = sum(max(min(64, width(l)), width(r)) * (4 if l[0] == "F" else 1) * PC for out, l, r, st, sp in items)
+        acc = {}
+        for out, l, r, st, sp in items:
+            b = (out[0], out[1] // 512)
+            acc[b] = (acc[b][0] if b in acc else st, not sp)
+        add("P", f, [x for it in items for x in it[1:3]], [it[0] for it in items], c, x=0.1, acc=[(b, v[0], v[1]) for b, v in acc.items()])
 
-    def group(items):
-        mm([(o, l, r, i == 0, i == len(items) - 1) for i, (o, l, r) in enumerate(items)])
+    def group(items, most=9.0):
+        run, t = [], 0.0
+        for i, (o, l, r) in enumerate(items):
+            c = max(min(64, width(l)), width(r)) * (4 if l[0] == "F" else 1) * PC
+            if run and t + c > most:
+                mm(run)
+                run, t = [], 0.0
+            run.append((o, l, r, i == 0, i == len(items) - 1))
+            t += c
+        mm(run)
 
     def apart(items):
         mm([(o, l, r, True, True) for o, l, r in items])
 
-    def iota(out, rd=()):
-        n = width(out)
-        if out[0] == "F":
-            f = lambda: g.iota(ap(out), [[1, n]], 0, 0, allow_small_or_imprecise_dtypes=True)
+    def iota(out, pattern, cm=0, rd=(), base=0):
+        if out[0] == "I":
+            f = lambda: g.iota(ap(out), pattern, base, cm)
         else:
-            f = lambda: g.iota(ap(out), [[1, n]], 0, 1 if n == 1 else 0)
-        add("G", f, list(rd), [out], 0.13 + 2 * CY * n)
+            f = lambda: g.iota(ap(out), pattern, base, cm, allow_small_or_imprecise_dtypes=True)
+        add("G", f, list(rd), [out], 0.13 + 2 * CY * width(out))
+        return out
 
     def dma(e, out, a, r, w, us, ext=()):
         qq = {"S": g.sync, "A": g.scalar, "G": g}[e]
-        add(e, lambda: qq.dma_start(out, a), r, w, 0.1 if e != "G" else 1.0, x=2.0 + us, dma=True, ext=ext)
+        add(e, lambda: qq.dma_start(out, a), r, w, 0.1 if e != "G" else 1.0, x=OPT["dma"] + us, dma=True, ext=ext)
 
     sent = [0]
 
@@ -556,8 +603,15 @@ def build(g, core, rank, T, topo, way):
         add("G", lambda: None, [("call%d" % ci, 0, 1)], [("call%d" % ci, 0, 1)], 0.0,
             x=OPT["hop"] + KINDS[CALLS[ci][0]][0] / 64.0)
 
-    def arr(ci):
+    def arr(k):
+        ci = call_of(k)
         return [(T.sem["arr%d" % ci], arrivals(T, topo, way, rank, ci))]
+
+    def call_of(k):
+        return [k in c for c in CALLS].index(True)
+
+    def mark(k):
+        return ("call%d" % call_of(k), 0, 1)
 
     def own(e, k, src, rd):
         dma(e, T["l" + k][rank], src, rd, [("l" + k, 0, 1)], 0.1)
@@ -565,12 +619,16 @@ def build(g, core, rank, T, topo, way):
     P = {k: (k, 0, SCRATCH[k][1][1], 1) for k in PSUM}
     rows = slice(16 * rank, 16 * rank + 16)
 
-    X0 = 2080
-    WIN = new("F", 2 * X0)
+    X0, NONE = 512, 2600
+    WIN = new("F", X0 + 2080)
     XW, SW = sl(WIN, X0, X0 + 2048), sl(WIN, 0, 512)
-    Xb = new("B", 2048)
+    WB = new("B", X0 + 2080)
+    Xb = sl(WB, X0, X0 + 2048)
     CZ = [pair("B", 512), pair("B", 512)]
-    KW = [pair("F", 384), pair("F", 384)]
+    LISTS = new("F", 8 * 144 + 16)
+    lst = [sl(LISTS, 144 * i, 144 * i + 160) for i in range(8)]
+    KK, QP, QG = [lst[0:2], lst[6:8]], lst[2:4], lst[4:6]
+    KW = pair("F", 384)
     L = new("F", 16)
     KU, LU = new("U", 256), new("U", 16)
     KI, LI, SI = new("I", 256), new("I", 16), new("I", 512)
@@ -588,349 +646,261 @@ def build(g, core, rank, T, topo, way):
     own("S", "ix", T.x0[rows, 0:1024], [])
     own("S", "iy", T.x0[rows, 1024:2048], [])
     own("S", "ia", T.asc[rows, :], [])
-    for ci in range(5):
-        remote(ci)
-    dma("S", ap(ZO), T.liz[:], [("liz", 0, 8), ("call0", 0, 1)], [ZO], 0.3, ext=arr(0))
-    dma("S", ap(LI), T.lil[:, rows, :], [("lil", 0, 8), ("call0", 0, 1)], [LI], 0.1, ext=arr(0))
-    dma("S", ap(KI), T.lik[:], [("lik", 0, 8), ("call1", 0, 1)], [KI], 0.4, ext=arr(1))
+    for ci in range(len(CALLS)):
+        if CALLS[ci][0][0] == "i":
+            remote(ci)
+    dma("S", ap(ZO), T.liz[:], [("liz", 0, 8), mark("iz")], [ZO], 0.3, ext=arr("iz"))
+    dma("S", ap(LI), T.lil[:, rows, :], [("lil", 0, 8), mark("il")], [LI], 0.1, ext=arr("il"))
+    dma("S", ap(KI), T.lik[:], [("lik", 0, 8), mark("ik")], [KI], 0.4, ext=arr("ik"))
+    for h, k in enumerate(("ix", "iy")):
+        dma("S", ap(part(Xb, h, 1024)), T["l" + k][:], [("l" + k, 0, 8), mark(k)], [part(Xb, h, 1024)], 0.8, ext=arr(k))
+    dma("S", ap(SI), T.lia[:], [("lia", 0, 8), mark("ia")], [SI], 0.8, ext=arr("ia"))
     for h, k in enumerate(("lix", "liy")):
-        dma("S", ap(part(Xb, h, 1024)), T[k][:], [(k, 0, 8), ("call%d" % (2 + h), 0, 1)], [part(Xb, h, 1024)], 0.8, ext=arr(2 + h))
-    dma("S", ap(SI), T.lia[:], [("lia", 0, 8), ("call4", 0, 1)], [SI], 0.8, ext=arr(4))
-    for h, k in enumerate(("lix", "liy")):
-        dma("G", ap(part(XW, h, 1024)), T[k][:], [(k, 0, 8), ("call4", 0, 1), Xb, SI], [part(XW, h, 1024)], 1.5)
+        dma("G", ap(part(XW, h, 1024)), T[k][:], [(k, 0, 8), ("callo", 0, 1), Xb, SI], [part(XW, h, 1024)], 1.5)
 
-    pI, cI = new("I", 1), new("I", 256)
-    iota(pI)
-    iota(cI)
-    IOTA = new("F", 2 * X0 + 16)
-    iota(IOTA, [("callo", 0, 1)])
-    cF = new("F", 256)
-    copy(cF, cI)
-    c16 = sl(cF, 0, 16)
-
+    after = [("callo", 0, 1)]
     def col(pool="F"):
         return new(pool, 1)
 
-    def icol(src, s1, op0, s2=None, op1=None):
-        i, f = col("I"), col()
-        ts(i, src, s1, op0, s2, op1)
-        copy(f, i)
-        return f
-    pF = col()
-    copy(pF, pI)
-    uF = icol(pI, 15, ALU.bitwise_and)
-    kF = icol(pI, 112, ALU.bitwise_and)
-    hF = icol(pI, 4, ALU.arith_shift_right, 1, ALU.bitwise_and)
-    u7 = icol(pI, 7, ALU.bitwise_and)
-    u8 = icol(pI, 3, ALU.arith_shift_right, 1, ALU.bitwise_and)
-    pm = col("I")
-    ts(pm, pI, 112.0, ALU.add)
-    kM = icol(pm, 112, ALU.bitwise_and)
-    ones = new("B", 128)
-    fill(ones, 1.0)
-    k16, k16m = col(), col()
-    ts(k16, kF, 16.0, ALU.add)
-    ts(k16m, kM, 16.0, ALU.add)
-    wcb, wc, wqb, wq, wv = col("B"), col(), col("B"), col(), col()
-    LN2 = math.log(2.0)
-    b15, b17, b21, b30 = col(), col(), col(), col()
-    fill(b15, 15 * LN2)
-    fill(b17, 17 * LN2)
-    fill(b21, 21 * LN2)
-    fill(b30, 30 * LN2)
-    act(wcb, uF, AF.Exp, b15, -LN2)
-    copy(wc, wcb)
-    act(wqb, uF, AF.Exp, b21, -3 * LN2)
-    copy(wq, wqb)
-    ts(wv, uF, 15.0, ALU.mult, 7.0, ALU.add)
+    def const(n, v, pool="B"):
+        return fill(new(pool, n), v)
 
-    def slide(pool, w, at=k16):
-        z = new(pool, 160)
-        ts(z, sl(cF, 0, 160), at, ALU.is_equal, w, ALU.mult)
-        return z
-    Z0, Zh, Zf = slide("B", 1.0), slide("H", 1.0), slide("B", 256.0, k16m)
-    Zd, Zc, Zv, Ze, Z1, Zq = (scaled(new("B", 160), Z0, w) for w in (-256.0, wc, wv, 256.0, 8192.0, wq))
+    def line(out, a, w, b):
+        act(out, a, AF.Identity, b, w)
+        return out
+    pI, pF = iota(col("I"), [[1, 1]], 1), iota(col(), [[1, 1]], 1)
+    one2, Y, YF = iota(new("B", 256), [[0, 256]], 0, (), 1), new("B", 256), new("F", 256)
+    ones = sl(one2, 0, 128)
+    select(Y, one2, [[0, 2], [-1, 128]], ALU.is_equal, 1)
+    cM = iota(new("F", 176), [[1, 176]], 0, (), -16)
+    cF, c16 = sl(cM, 16, 176), sl(cM, 16, 32)
+    c144 = iota(new("F", 144), [[0, 9], [1, 16]])
+    c15 = sl(c144, 0, 128)
+    c112 = iota(new("F", 128), [[16, 8], [0, 16]], 0, after)
+    lists, cols = new("F", 29), new("F", 4)
+    iota(sl(lists, 12, 20), [[16, 8]], 0, after, 15)
+    iota(sl(lists, 20, 21), [[1, 1]], 0, after, 127)
+    iota(sl(lists, 21, 29), [[16, 8]], 0, after, 15)
+    iota(sl(cols, 0, 2), [[896, 2]], 0, after, 1024)
+    iota(sl(cols, 2, 4), [[16, 2]], 0, after, X0 + 2048)
+    iota(sl(lists, 0, 8), [[2, 4], [0, 2]], 0, after)
+    iota(sl(lists, 8, 12), [[2, 4]], 0, after, 1)
+    c421 = iota(new("F", 16), [[17, 2], [0, 8]], 0, after, 4)
+    c31 = iota(new("F", 128), [[0, 4], [1, 32]], 0, after)
+    ramp = iota(new("B", 2048), [[1, 16], [0, 128]], 0, after)
+    IOTA = iota(new("F", NONE + 8), [[1, NONE + 8]], 0, after, 4096)
+    uI, uF, kF, hF, u7, u8, Sel1 = col("I"), col(), col(), col(), col(), col(), new("B", 8)
+    ts(uI, pI, 15, ALU.bitwise_and)
+    copy(uF, uI)
+    tt(kF, pF, uF, ALU.subtract)
+    ts(Sel1, sl(cF, 0, 128, 16), kF, ALU.is_equal)
+    reduce(hF, sl(Sel1, 1, 8, 2), ALU.add)
+    ts(u8, uF, 8.0, ALU.is_ge)
+    ts(u7, u8, -8.0, ALU.mult, uF, ALU.add)
+    LN2 = math.log(2.0)
+    wcb, wc, wqb, wq, wr, wv = col("B"), col(), col("B"), col(), col(), col()
+    b20, b21, b27 = const(1, 20 * LN2, "F"), const(1, 21 * LN2, "F"), const(1, 27 * LN2, "F")
+    act(wcb, uF, AF.Exp, b20, -LN2)
+    ops[-1]["c"] += 1.3
+    move("A", wc, wcb)
+    act(wqb, uF, AF.Exp, b21, -3 * LN2)
+    move("A", wq, wqb)
+    scaled(wr, wqb, 128.0)
+    ts(wv, uF, 15.0, ALU.mult, 7.0, ALU.add)
+    Z0, Zh = new("B", 160), new("H", 160)
+    ts(Z0, sl(cM, 0, 160), kF, ALU.is_equal)
+    move("A", Zh, Z0)
+    Zv, Zq, Zr = (scaled(new("B", 160), Z0, w) for w in (wv, wq, wr))
 
     def zu(z, u):
         return sl(z, 16 - u, 144 - u)
-    tri = new("B", 2048)
-    gt16 = new("F", 16)
-    ts(gt16, c16, uF, ALU.is_lt)
-    for u in range(16):
-        scaled(part(tri, u, 128), zu(Z1, u), sl(gt16, u, u + 1))
-    c127I, c127 = new("I", 256), new("F", 256)
-    ts(c127I, cI, 127, ALU.bitwise_and)
-    copy(c127, c127I)
-
-    def shifts(pool, w, a=0):
-        y = new(pool, 256)
-        ts(sl(y, a, 256), sl(c127, a, 256), pF, ALU.is_equal, w, ALU.mult)
-        return y
-    Y, YF = shifts("B", 1.0), shifts("F", 1.0)
+    move("A", YF, Y)
 
     def sh(y, k):
         k %= 8
         return sl(y, 128 - 16 * k, 256 - 16 * k)
 
     def eye(pool, w):
-        return scaled(new(pool, 128), sh(Y, 0), w)
-    I1, IN, IH, I2, IS, ISN = sh(Y, 0), eye("B", -1.0), eye("B", 0.5), eye("B", 2.0), eye("B", 1.3125), eye("B", -1.3125)
-    INF, I20, I5 = eye("F", -1.0), eye("F", 20.0), eye("F", 5.0)
-    IB, IR, IRN, IR2 = eye("B", 524288.0), eye("B", MAGIC), eye("B", -MAGIC), eye("B", 2048.0 * MAGIC)
-    bR, bR2, bhalf = col(), col(), col()
-    fill(bR, -MAGIC)
-    fill(bR2, -2048.0 * MAGIC)
-    fill(bhalf, 0.5)
-    IM, I2K, ones4, bM = eye("B", MAGIC128), eye("B", float(X0)), new("B", 512), col()
-    fill(ones4, 1.0)
-    fill(bM, -MAGIC128)
-    c112I, c112 = new("I", 128), new("F", 128)
-    ts(c112I, sl(cI, 0, 128), 112, ALU.bitwise_and)
-    copy(c112, c112I)
-    BOh, BOn, BOv, BO1 = new("H", 128), new("H", 128), new("B", 128), new("B", 128)
-    ts(BOh, c112, kF, ALU.is_equal)
-    ts(BOn, c112, kF, ALU.is_equal, -1.0, ALU.mult)
+        return scaled(new(pool, 128), sh(Y, 0), w, "V" if pool == "B" else "A")
+    I1, IF = sh(Y, 0), sh(YF, 0)
+    YN = scaled(new("B", 256), Y, -1.0, "V")
+    IN = sh(YN, 0)
+    IH, I2, IS, ISN, I4K = (eye("B", w) for w in (0.5, 2.0, 1.3125, -1.3125, 4096.0))
+    INF, INH, I20, I4, I5N, YH = eye("F", -1.0), eye("H", -1.0), eye("H", 20.0), eye("H", 4.0), eye("H", -5.0), new("H", 256)
+    move("A", YH, Y)
+    M0, M7, M11, M22 = const(128, MAGIC), const(512, MAGIC * 2 ** 7), const(128, MAGIC * 2 ** 11), const(128, MAGIC * 2 ** 22)
+    M8, M9, M19 = const(8, MAGIC * 2 ** 8), const(8, MAGIC * 2 ** 9), const(8, MAGIC * 2 ** 19)
+    bR, bM = const(1, -MAGIC, "F"), const(1, -MAGIC * 2 ** 7, "F")
+
+    def rnd(o, m):
+        m = sl(m, 0, width(o))
+        return [(o, I1, m), (o, IN, m)]
+    BO1, BOh = new("B", 128), new("H", 128)
     ts(BO1, c112, kF, ALU.is_equal)
-    scaled(BOv, BO1, wv)
-    BOq = scaled(new("B", 128), BOv, 0.25)
-    c38, c1k = new("B", 128), new("B", 128)
-    fill(c38, -0.375)
-    fill(c1k, -1024.0)
-    BO0 = new("B", 128)
-    fill(BO0, 0.0)
+    move("A", sl(BOh, 0, 112), sl(BO1, 16, 128))
+    move("A", sl(BOh, 112, 128), sl(BO1, 0, 16))
+    BOn, BOv = scaled(new("H", 128), BO1, -1.0), scaled(new("B", 128), BO1, wv)
+    BOq, BOqn = scaled(new("B", 128), BOv, 0.25, "V"), scaled(new("B", 128), BOv, -0.25, "V")
+    c38, quarter, cX, c18 = const(128, -0.375), const(128, -0.25), const(8, float(X0)), const(8, -2.0 ** 18)
+    p0, p1, p2 = (sl(IF, i, i + 1) for i in range(3))
+    r1k, c1k = col(), new("B", 128)
+    ts(r1k, p0, 1024.0 + 2.0 ** -10, ALU.mult, -2.0 ** -10, ALU.add)
+    scaled(c1k, ones, r1k)
+    q3, t3, t4, t5, t6, up = new("I", 3), new("F", 3), new("I", 3), new("I", 3), new("F", 3), col()
+    ts(q3, sl(cM, 15, 18), uF, ALU.add, 1.0 / 3, ALU.mult)
+    line(up, uF, -16.0, pF)
+    ts(t3, sl(cF, 0, 3), -16.0, ALU.mult, up, ALU.add)
+    ts(t4, q3, 48.0, ALU.mult, 112.0, ALU.add)
+    tt(t4, t4, t3, ALU.add)
+    ts(t5, t4, 127, ALU.bitwise_and)
+    copy(t6, t5)
     PB, PN = [], []
     for be in range(3):
-        qi, tc, t2, t3 = col("I"), col(), col("I"), col("I")
-        ts(qi, uF, 1.0 / 3, ALU.mult, (be - 1) / 3.0, ALU.add)
-        ts(tc, qi, 48.0, ALU.mult, kF, ALU.add)
-        ts(t2, uF, -15.0, ALU.mult, tc, ALU.add)
-        ts(t3, t2, float(128 - 16 - 16 * be), ALU.add)
-        t4 = icol(t3, 127, ALU.bitwise_and)
-        pb, pn = new("B", 128), new("B", 128)
-        ts(pb, sl(cF, 0, 128), t4, ALU.is_equal)
-        scaled(pn, pb, -1.0)
+        pb = new("B", 128)
+        ts(pb, sl(cF, 0, 128), sl(t6, be, be + 1), ALU.is_equal)
         PB.append(pb)
-        PN.append(pn)
-    eq16 = new("F", 16)
-    ts(eq16, c16, uF, ALU.is_equal)
+        PN.append(scaled(new("B", 128), pb, -1.0))
     IBIG = new("B", 2048)
-    for j in range(16):
-        scaled(part(IBIG, j, 128), ones, sl(eq16, j, j + 1))
-    cB = new("B", 128)
-    copy(cB, sl(cF, 0, 128))
-    quarter = new("B", 128)
-    fill(quarter, -0.25)
-    cz = new("B", 16)
+    ts(IBIG, ramp, uF, ALU.is_equal)
+    cz, ca = new("B", 16), new("B", 8)
     for i in range(2):
-        ts(part(cz, i, 8), sl(cF, 0, 8), 0.125, ALU.mult)
-    spare, spare2 = col(), col()
-    ts(spare, uF, X0 + 2048.0, ALU.add)
-    ts(spare2, uF, X0 + 2064.0, ALU.add)
-    c421 = new("F", 16)
-    fill(sl(c421, 0, 8), 4.0)
-    fill(sl(c421, 8, 16), 21.0)
-    THR, l1, l2 = new("F", 16), new("F", 16), new("F", 16)
-    ts(l1, c16, 15.0, ALU.not_equal)
-    ts(l2, c16, 1.0, ALU.add)
-    tt(l2, l2, l1, ALU.mult)
-    act(THR, l2, AF.Exp, b30, -3 * LN2)
-    repb, repo, repk, pickW = (new("U", 8) for _ in range(4))
-    pickL = new("U", 1)
-    copy(repb, sl(cF, 0, 8))
-    ro1 = new("I", 8)
-    ts(ro1, sl(cI, 0, 8), 6, ALU.bitwise_and)
-    ts(repo, ro1, 1.0, ALU.add)
-    ts(repk, sl(cF, 0, 8), 0.0, ALU.mult, u7, ALU.add)
-    s1, s3, e5 = col("I"), col(), col()
+        scaled(part(cz, i, 8), sl(cF, 0, 8), 0.125)
+    scaled(ca, sl(cF, 0, 8), -65536.0)
+    E144, RST, cP, bF, listU, colu = new("B", 144), new("F", 128), new("B", 128), col(), new("U", 29), new("F", 4)
+    ts(E144, c144, uF, ALU.is_equal)
+    E128 = sl(E144, 0, 128)
+    ts(colu, cols, uF, ALU.add)
+    u1k, u2k, spare, spare2 = (sl(colu, i, i + 1) for i in range(4))
+    THR = new("F", 32)
+    act(THR, sl(c15, 0, 32), AF.Exp, b27, -3 * LN2)
+    fill(sl(THR, 15, 16), 2.0 ** 30)
+    FIT, f1 = new("B", 32), new("B", 32)
+    act(f1, sl(c15, 0, 32), AF.Exp, b21, -LN2)
+    line(FIT, f1, scaled(col(), sl(E128, 1, 2), -1.0), scaled(col(), sl(E128, 0, 1), -2.0 ** 21))
+    pickW, pickL, mapK = new("U", 8), new("U", 1), new("U", 1)
+    copy(listU, lists)
+    repK, rep15, rep9 = sl(listU, 0, 12), sl(listU, 12, 20), sl(listU, 20, 29)
+    mk1, RSK = col(), new("B", 192)
+    ts(mk1, u7, 1.0, ALU.add, u8, ALU.mult)
+    ts(mapK, mk1, u7, ALU.add, 7.0, ALU.min)
+    ts(sl(RSK, 0, 128), c31, uF, ALU.not_equal)
+    ts(sl(RSK, 128, 192), sl(c15, 0, 64), uF, ALU.not_equal)
+    s1, s2, s3, e5 = col("I"), col("I"), col(), col()
     tt(s1, uF, hF, ALU.add)
-    s2 = icol(s1, 1, ALU.bitwise_and)
+    ts(s2, s1, 1, ALU.bitwise_and)
     ts(e5, u7, 16.0, ALU.mult, u8, ALU.add)
     ts(s3, s2, 144.0, ALU.mult, e5, ALU.add)
     ts(pickW, sl(cF, 0, 8), 2.0, ALU.mult, s3, ALU.add)
     ts(pickL, hF, 16.0, ALU.mult, uF, ALU.add)
 
-    Sel1, SelF, SelG = new("B", 8), new("F", 8), new("B", 8)
-    ts(Sel1, sl(cF, 0, 128, 16), kF, ALU.is_equal)
-    ts(SelF, sl(cF, 0, 128, 16), kF, ALU.is_equal)
-    ts(SelG, sl(cF, 0, 128, 16), kM, ALU.is_equal, 256.0, ALU.mult)
-    SelD, SelC, SelE = (scaled(new("B", 8), Sel1, w) for w in (-256.0, wc, 256.0))
-    BOm = scaled(new("B", 128), BO1, -1.0)
-    c15I, c15, E128, RST, cP, bF = new("I", 128), new("F", 128), new("B", 128), new("F", 128), new("B", 128), col()
-    ts(c15I, sl(cI, 0, 128), 15, ALU.bitwise_and)
-    copy(c15, c15I)
-    ts(E128, c15, uF, ALU.is_equal)
+    SelF, SelG, SelDV = new("F", 8), new("B", 8), new("B", 16)
+    move("A", SelF, Sel1)
+    scaled(sl(SelG, 0, 7), sl(Sel1, 1, 8), 256.0)
+    scaled(sl(SelG, 7, 8), sl(Sel1, 0, 1), 256.0)
+    SelC, SelE, SelN = scaled(new("B", 8), Sel1, wc), scaled(new("B", 8), Sel1, 256.0), scaled(new("F", 8), Sel1, -1.0)
+    SelD = scaled(part(SelDV, 0, 8), Sel1, -256.0)
+    scaled(part(SelDV, 1, 8), Sel1, wv)
     ts(RST, c15, 0.0, ALU.is_equal, 8388608.0, ALU.mult)
     ts(bF, kF, 1.0 / 16, ALU.mult, -64.0, ALU.add)
-    SelN, IM8, IM8N, u1k = scaled(new("F", 8), Sel1, -1.0), eye("B", 256.0 * MAGIC), eye("B", -256.0 * MAGIC), col()
-    ts(u1k, uF, 1024.0, ALU.add)
-    ts(cP, c15, 8.0, ALU.mult, bF, ALU.add)
-    rep15, repb2 = new("U", 8), new("U", 8)
-    ts(rep15, sl(cF, 0, 8), 16.0, ALU.mult, 15.0, ALU.add)
-    ts(repb2, sl(cF, 0, 8), 8.0, ALU.add)
-    run16, wide = pair("F", 128), pair("F", 128)
-    SelDV, cP2, E256, RS0, half128 = new("B", 16), new("B", 256), new("B", 256), new("F", 128), new("B", 128)
-    scaled(part(SelDV, 0, 8), Sel1, -256.0)
-    scaled(part(SelDV, 1, 8), Sel1, wv)
-    copy(part(cP2, 0, 128), cP)
-    fill(part(cP2, 1, 128), -256.0)
-    fill(half128, 0.5)
-    for i in range(2):
-        move("A", part(E256, i, 128), E128)
-    ts(RS0, c15, 0.0, ALU.not_equal)
-    IM9, IM9N = eye("B", 512.0 * MAGIC), eye("B", -512.0 * MAGIC)
-    away, cc = pair("U", 16), new("F", 16)
-    ts(part(cc, 0, 8), sl(cF, 0, 8), 7.0, ALU.add)
-    ts(part(cc, 1, 8), sl(cF, 0, 8), 6.0, ALU.add)
-    for h in range(2):
+    line(cP, c15, 8.0, bF)
+    cV = new("B", 256)
+    fill(part(cV, 0, 128), 0.0)
+    v1 = line(col(), p0, 15 * 2.0 ** 19, line(col(), p1, 256.0, scaled(col(), p2, 0.5)))
+    line(part(cV, 1, 128), c15, scaled(col(), p0, -2.0 ** 19), v1)
+    away = pair("U", 16)
+    for h in OPT["fast"]:
         q3, m3, m4, a1, a2 = col("I"), col(), col(), new("I", 16), new("I", 16)
         ts(q3, pF, 1.0 / 3, ALU.mult, (2 * h - 1) / 3.0, ALU.add)
         ts(m3, q3, 3.0, ALU.mult, -2.0 * h, ALU.add)
         tt(m4, m3, pF, ALU.subtract)
-        ts(a1, cc, m4, ALU.add)
+        for i in range(2):
+            ts(part(a1, i, 8), sl(cF, 7 - i, 15 - i), m4, ALU.add)
         ts(a2, a1, 7, ALU.bitwise_and)
         ts(away[h], a2, 16.0, ALU.mult, 15.0, ALU.add)
-    eqm, vm, runV, cbF = pair("F", 128), pair("F", 128), pair("F", 128), pair("F", 8)
-    wideV = pair("F", 256)
 
     GW = OPT["gw"]
     uH, uB, uC, aH, aB, aC, fB, fC, bad, q6 = (new("B", 4096) for _ in range(10))
-    a6 = aC
+    a6 = aB
     Z8, ZB4, ZC4 = pair("B", 2048), pair("B", GW), pair("B", GW)
-    Z4 = [sl(z, 0, GW) for z in Z8]
-    DD = pair("B", 256)
-    D, us, uj, eq, eq2, mkB, thrR, thr6, sgn, kr, zm = (pair("B", 128) for _ in range(11))
-    for h in range(2):
-        scaled(part(Z8[h], 1, 1024), sl(IBIG, 0, 1024), 0.0)
-    QP, QG, TP, TG, TK = new("F", 288), new("F", 288), pair("F", 288), pair("F", 288), pair("F", 288)
-    for qq in (QP, QG):
-        fill(qq, 0.0)
-    move("G", sl(WIN, 512, X0), sl(IOTA, 512, X0))
-    fill(sl(WIN, X0 + 2048, 2 * X0), 0.0)
-    for kw in KW:
-        for h in range(2):
-            fill(sl(kw[h], 112, 128), 0.0)
-            fill(sl(kw[h], 256, 272), 0.0)
+    DD, ZS = pair("B", 256), pair("B", 256)
+    D, us, uj, mkB, zm, nf = (pair("B", 128) for _ in range(6))
+    thr2, thr62 = new("B", 256), new("B", 256)
+    thrN, thr6 = [part(thr2, h, 128) for h in range(2)], [part(thr62, h, 128) for h in range(2)]
+    mixed = [("H%d0" % h in OPT["raw"]) != ("H%d1" % h in OPT["raw"]) for h in range(2)]
+    TP, TG, TK = pair("F", 288), pair("F", 288), pair("F", 288)
+    for z in [sl(LISTS, 144 * i, 144 * i + 16) for i in range(9)] + [part(Z8[h], 1, 1024) for h in range(2) if mixed[h]] \
+            + [part(KW[h], 1, 128) for h in range(2)] + [sl(WIN, X0 + 2048, X0 + 2080), sl(WB, 0, X0), sl(WB, X0 + 2048, X0 + 2080)]:
+        fill(z, 0.0)
     PU, GU = new("U", 256), new("U", 256)
     CV = pair("F", 256)
-    krow, vals, GnB, pen, keys, asb, off = (pair("F", 128) for _ in range(7))
+    vals, GnB, off, run16, runV, wide, wideB, wideC = (pair("F", 128) for _ in range(8))
     k1, k2 = pair("I", 128), pair("I", 128)
-    PM, GM = pair("H", 128), pair("H", 128)
-    lv = [[new("F", 64), new("F", 64), new("F", 32), new("F", 16), new("F", 8)] for _ in range(2)]
-    thr, NH_, s3w = new("B", 16), new("B", 16), new("B", 16)
-    joff, moff, soff, kvU, scU = (pair("U", 8) for _ in range(5))
-    cU, zs = pair("U", 16), pair("U", 16)
+    PM, GM, Kh, Ph = (pair("H", 128) for _ in range(4))
+    wide9 = pair("F", 144)
+    NH_, s3w = new("B", 16), new("B", 16)
+    joff, moff, soff, scU = (pair("U", 8) for _ in range(4))
+    cU, zs, kvU = pair("U", 16), pair("U", 16), pair("U", 16)
+    krow, eq, cnt, kvc = pair("F", 192), pair("B", 192), pair("B", 192), pair("F", 8)
     zoff, selU = [sl(z, 0, 8) for z in zs], [sl(z, 8, 16) for z in zs]
-    kS, kE, kG, lo1, lo2, lo3 = (pair("I", 8) for _ in range(6))
     vI, cIi = pair("I", 16), pair("I", 16)
-    cp1, addB, thrE, kv, kvm = (pair("F", 8) for _ in range(5))
+    cp1 = pair("B", 8)
+    addB, thrE, kv, cbF = (pair("F", 8) for _ in range(4))
     LL, LT, LO, lw, L2 = new("F", 32), new("F", 32), new("F", 16), new("F", 16), new("F", 16)
     a256, ar = col(), [col(), col()]
-    aI, aI2 = col("I"), col("I")
-    fill(a256, 128.0)
-    repk2 = new("U", 8)
-    ts(repk2, repk, 8.0, ALU.add)
+    aI, aI2, aF = col("I"), col("I"), col()
+    fill(a256, 128.0 - 2.0 ** 21)
 
     def turn(t, qq, at):
         tr(sl(t, 0, 128), sl(qq, at, at + 128))
         tr(sl(t, 128, 288), sl(qq, at - 16, at + 144))
         return t
 
-    def spread(e, z4):
-        n = 128
-        while n < GW:
-            if n == 128:
-                move(e, sl(z4, 128, 256), sl(z4, 0, 128))
-            else:
-                move(e, sl(z4, n, 2 * n), sl(z4, 0, n))
-            n *= 2
+    def spread(e, z4, src, n):
+        move(e, sl(z4, 0, 128), src)
+        move(e, sl(z4, 128, 256), src)
+        m = 256
+        while m < n:
+            move(e, sl(z4, m, 2 * m), sl(z4, 0, m))
+            m *= 2
 
     for h in range(2):
-        copy(sl(KW[0][h], 128, 256), part(KI, h, 128))
-        copy(part(KU, h, 128), ind(turn(TK[h], KW[0][h], 128), pickW))
+        copy(sl(KK[0][h], 16, 144), part(KI, h, 128))
+        copy(part(KU, h, 128), ind(turn(TK[h], KK[0][h], 16), pickW))
         copy(sl(CZ[0][h], 0, 128), part(ZO, h, 128))
     copy(sl(LL, 0, 16), LI)
     copy(sl(LL, 16, 32), LI)
     tr(LT, LL)
     copy(L, ind(LT, pickL))
-    copy(LU, L)
-    copy(SW, SI)
+    copy(LU, ind(LT, pickL))
+    move("A", SW, SI) if OPT.get("swa") else copy(SW, SI)
 
-    def least(out, a, h, name, first=None):
-        b = lv[h]
-        if name in OPT["red"]:
-            for i in range(8):
-                reduce(sl(b[4], i, i + 1), sl(a, i, 128, 8), ALU.min)
-            copy(out, b[4])
-            return b[4]
-        tt(b[1], sl(a, 64, 128), first if first else sl(a, 0, 64), ALU.min)
-        tt(b[2], sl(b[1], 0, 32), sl(b[1], 32, 64), ALU.min)
-        tt(b[3], sl(b[2], 0, 16), sl(b[2], 16, 32), ALU.min)
-        tt(out, sl(b[3], 0, 8), sl(b[3], 8, 16), ALU.min)
-        return out
+    def sums(ps, sel, src, a0, n, stop):
+        ks = range(a0 // 128, (a0 + n) // 128)
+        mm([(sl(ps, k % 16, width(ps), 16), part(src, k, 128), sel, False, stop and k % 16 == 15) for k in ks])
 
-    def sums_t(ps, sel, src, c, stop=True):
-        mm([(sl(ps, k % 16, width(ps), 16), part(src, k, 128), sel, False, stop and k % 16 == 15) for k in range(8 * c, 8 * c + 8)])
-
-    def hashed(h):
-        tt(eqm[h], ind(run16[h], rep15), keys[h], ALU.is_equal)
-        tt(vm[h], sl(S2[h], 128, 256), eqm[h], ALU.mult)
-        add("V", lambda: g.vector.tensor_tensor_scan(ap(runV[h]), ap(RS0), ap(vm[h]), 0.0, ALU.mult, ALU.add), [RS0, vm[h]], [runV[h]], 0.13)
-        for i in range(2):
-            tt(part(wideV[h], i, 128), ind(runV[h], part(away[h], i, 8)), E128, ALU.mult)
-        o, w = sl(Mh[h], 256, 264), part(wideV[h], 0, 128)
-        group([(o, w, SelN), (o, IM9, sl(ones, 0, 8)), (o, IM9N, sl(ones, 0, 8)), (o, w, SelF)])
-        ts(part(cU[h], 0, 8), o, 255.5, ALU.add)
-        ts(cbF[h], o, 255.5, ALU.add)
-        o = sl(Mh[h], 264, 272)
-        apart([(o, part(wideV[h], 1, 128), SelF)])
-        ts(part(vI[h], 1, 8), o, 255.5, ALU.add, 21.0, ALU.mult)
-        ts(part(cIi[h], 1, 8), part(vI[h], 1, 8), 2, ALU.arith_shift_right, 511, ALU.bitwise_and)
-        copy(part(cU[h], 1, 8), part(cIi[h], 1, 8))
-
-    def least_t(out, a, h, key=None, then=None):
-        add("V", lambda: g.vector.tensor_tensor_scan(ap(run16[h]), ap(RST), ap(a), 0.0, ALU.add, ALU.min), [RST, a], [run16[h]], 0.13)
-        if then:
-            then()
-        tt(wide[h], ind(run16[h], rep15), E128, ALU.mult)
-        o, p = sl(S2[h], 384, 392), sl(S2[h], 392, 400)
-        if key:
-            apart([(o, wide[h], SelF)])
-        if key and out is moff[h]:
-            key(o)
-        group([(p, wide[h], SelN), (p, IM8, sl(ones, 0, 8)), (p, IM8N, sl(ones, 0, 8)), (p, wide[h], SelF)])
-        if key and out is not moff[h]:
-            key(o)
-        ts(out, p, 16.0, ALU.mult, u1k, ALU.add)
-
-    def place(o, lo, k):
-        ts(lo, k, 255, ALU.bitwise_and)
-        ts(o, lo, 16.0, ALU.mult, uF, ALU.add)
-
-    def pieces(tag, c):
-        n = 512 if tag in OPT["cut"] else 1024
-        return [(a0, a0 + n) for a0 in range(1024 * c, 1024 * c + 1024, n)]
-
-    def sums(ps, z, src, c, first, stop=True):
-        out = part(ps, c % 2, 64)
-        mm(([(out, first[0], part(first[1], c % 2, 64), True, False)] if first else [])
-           + [(out, zu(z, u), sl(src, 1024 * c + u, 1024 * c + 1024, 16), False, stop and u == 15) for u in range(16)])
-
-    def rounded(out, ps, items):
-        if OPT["rnd"] == "V":
-            group(items)
+    def evac(e, out, ps, items):
+        if e == "V":
+            group(items, OPT["split"])
             ts(out, ps, MAGIC, ALU.add, MAGIC, ALU.subtract)
         else:
-            group(items + [(ps, IR, ones)])
+            group(items + [(ps, I1, M0)], OPT["split"])
             act(out, ps, AF.Identity, bR, 1.0)
 
-    def gathers(u, win, o, z4, c, n=GW):
-        for i in range(1024 * c // n, 1024 * (c + 1) // n):
-            tt(part(u, i, n), ind(win, part(o, i, n // 16)), sl(z4, 0, n), ALU.subtract)
+    def pieces(tag, c):
+        n = OPT["cut"].get(tag, 1024)
+        return [(1024 * c + n * i, n, n * i if n > 256 else 512 * (i % 2) + 256 * (i // 2)) for i in range(1024 // n)]
 
-    def minus(w, terms, c, d, neg=IN, rounds=False):
-        for b in range(2):
-            it = [(part(w, b, 512), l, part(s, 2 * c + b, 512)) for l, s in terms]
-            group(it + [(part(w, 4 * b + i, 128), neg, d) for i in range(4)] + ([(part(w, b, 512), IM, ones4)] if rounds else []))
+    def minus(w, terms, a0, n, at, d, neg=IN, more=None):
+        for b in range(0, n, 512):
+            m = min(n, 512)
+            o = sl(w, at + b, at + b + m)
+            group([(o, l, sl(s, a0 + b, a0 + b + m)) for l, s in terms] + [(part(o, i, 128), neg, d) for i in range(m // 128)]
+                  + ([(o, I1, sl(more, 0, m))] if more else []))
+
+    def gather(u, win, o, z4, a0, n, most):
+        for b in range(a0, a0 + n, most):
+            m = min(n, most)
+            tt(sl(u, b, b + m), ind(win, sl(o, b // 16, (b + m) // 16)), sl(z4, 0, m), ALU.subtract)
 
     def lanes(out, src, k0, sg, h, y=Y):
         return [(sl(out, (m + h) % 3, 128, 3), sh(y, sg * (k0 + m)), sl(src, (m + h) % 3, 128, 3)) for m in range(3)]
@@ -941,327 +911,298 @@ def build(g, core, rank, T, topo, way):
     wb = [P["W0"], P["W1"]]
     S2 = [P["SA"], P["SB"]]
     Mh = [P["M0"], P["M1"]]
-    nw, found = [0], [None, None]
+    nw = [0]
 
     def nextw():
         nw[0] += 1
         return wb[nw[0] % 2]
 
-    def one_round(rnd):
-        last = rnd == 2
-        win = Xb if rnd == 0 else XW
-        cz_, kw_ = CZ[rnd % 2], KW[rnd % 2]
+    def small(h, i, n=1):
+        return sl(Mh[h], 384 + 8 * i, 384 + 8 * (i + n))
+
+    def least(out, a, h, at, key, on=False):
+        scan(run16[h], RST, a, ALU.add, ALU.min)
+        w = sl(wide9[h], 16, 144)
+        if on:
+            tt(wide9[h], ind(run16[h], rep9), E144, ALU.mult)
+        else:
+            tt(w, ind(run16[h], rep15), E128, ALU.mult)
+        if key:
+            key(small(h, at), w)
+        p, w = small(h, at + 1), sl(wide9[h], 0, 128) if on else w
+        group([(p, w, SelN)] + rnd(p, M8) + [(p, w, SelF)])
+        ts(out, p, 16.0, ALU.mult, u1k, ALU.add)
+
+    def one_round(rnd_):
+        last = rnd_ == 2
+        win = Xb if rnd_ == 0 else XW
+        cz_ = CZ[rnd_ % 2]
         Z = [sl(cz_[h], 0, 128) for h in range(2)]
-        K = [sl(kw_[h], 128, 256) for h in range(2)]
-        Pn = [sl(QP, 16 + 128 * h, 144 + 128 * h) for h in range(2)]
-        Gn = [sl(QG, 16 + 128 * h, 144 + 128 * h) for h in range(2)]
+        K = [sl(KK[rnd_ % 2][h], 16, 144) for h in range(2)]
+        Pn, Gn = [sl(q, 16, 144) for q in QP], [sl(q, 16, 144) for q in QG]
+        keys = [sl(S2[h], 0, 128) for h in range(2)]
+
+        def home(h, half):
+            M, c, tag, fast = Mh[h], 2 * h + half, "H%d%d" % (h, half), h in OPT["fast"]
+            if half == 0:
+                if not all("H%d%d" % (h, i) in OPT["raw"] for i in range(2)):
+                    spread("V" if rnd_ == 0 else "G", Z8[h], Z[h], 1024 if mixed[h] else OPT["gwH"])
+                move("G", Kh[h], K[h])
+                if h == 0:
+                    move(EN["thr"][h], thr2, ind(FIT, LU))
+                else:
+                    move(EN["t6"][h], thr62, ind(THR, LU))
+                if fast:
+                    mm([(sl(S2[h], 0, 256), ones, cV, True, False), (keys[h], thrN[h], BO1, False, False)])
+                else:
+                    mm([(keys[h], thrN[h], BO1, True, False)])
+                apart(lanes(sl(M, 0, 128), Z[h], 1, 1, h) + lanes(sl(M, 128, 256), Z[h], 2, 1, h))
+                move(EN["zs"][h], ZS[h], sl(M, 0, 256))
+                for i, zz in enumerate((ZB4[h], ZC4[h])):
+                    spread("G", zz, part(ZS[h], i, 128), GW)
+            raw = tag in OPT["raw"]
+            w = nextw() if raw else None
+            for a0, n, at in pieces(tag, c):
+                if raw:
+                    act(sl(uH, a0, a0 + n), ind(win, sl(KU, a0 // 16, (a0 + n) // 16)), AF.Copy)
+                    minus(w, [(I1, uH)], a0, n, at, Z[h])
+                    act(sl(aH, a0, a0 + n), sl(w, at, at + n), AF.Abs)
+                else:
+                    gather(uH, win, KU, Z8[h], a0, n, OPT["gwH"])
+                    act(sl(aH, a0, a0 + n), sl(uH, a0, a0 + n), AF.Abs)
+                ts(sl(bad, a0, a0 + n), sl(aH, a0, a0 + n), 48.0, ALU.is_gt)
+                sums(keys[h], SelC, bad, a0, n, False)
 
         def speaker(h):
-            M, raws = Mh[h], [c in OPT["rawH"] for c in (2 * h, 2 * h + 1)]
-            if not all(raws):
-                e = "V" if rnd == 0 else "G"
-                move(e, sl(Z4[h], 0, 128), Z[h])
-                spread(e, Z4[h])
-            turned, fast = "H%d" % h in OPT["T"], h in OPT["fast"]
-            if turned:
-                tt(thrR[h], ind(thr, repb2 if h else repb), E128, ALU.mult)
-            elif OPT["thr"][h] != "P":
-                move(OPT["thr"][h], thrR[h], ind(thr, repk2 if h else repk))
-            apart(lanes(sl(M, 0, 128), Z[h], 1, 1, h) + lanes(sl(M, 128, 256), Z[h], 2, 1, h))
-            for i, zz in enumerate((ZB4[h], ZC4[h])):
-                act(sl(zz, 0, 128), part(M, i, 128), AF.Copy)
-                spread("G", zz)
-            ds, cs = sl(S2[h], 0, 128), sl(M, 0, 128)
+            M, S, fast = Mh[h], S2[h], h in OPT["fast"]
+            raws = ["H%d%d" % (h, i) in OPT["raw"] for i in range(2)]
+            mm([(o, l, r, False, False) for o, l, r in rnd(keys[h], M22) + [(keys[h], I1, cP)]])
             for c in (2 * h, 2 * h + 1):
-                cut, raw = pieces("H%d%d" % (h, c % 2), c), raws[c % 2]
-                if raw:
-                    w = nextw()
-                    act(part(uH, c, 1024), ind(win, part(KU, c, 64)), AF.Copy)
-                    minus(w, [(I1, uH)], c, Z[h])
-                else:
-                    gathers(uH, win, KU, Z4[h], c, OPT["gwH"][h])
-                    if c == 0 and OPT["early"]:
-                        ops[-OPT["early"]]["r"].append(KU)
-                for a0, a1 in cut:
-                    act(sl(aH, a0, a1), sl(w, a0 - 1024 * c, a1 - 1024 * c) if raw else sl(uH, a0, a1), AF.Abs)
-                    ts(sl(bad, a0, a1), sl(aH, a0, a1), 48.0, ALU.is_gt, 2.0, ALU.mult)
-                if turned:
-                    both = sl(S2[h], 0, 256)
-                    if c % 2 == 0:
-                        if fast:
-                            mm([(both, I1, cP2, True, False), (part(both, 1, 128), I1, half128, False, False)])
-                        else:
-                            mm([(ds, I1, cP, True, False)])
-                        mm([(cs, thrR[h], BOm, True, False)])
-                    if fast:
-                        sums_t(both, SelDV, aH, c)
-                    else:
-                        sums_t(ds, SelD, aH, c, OPT["pen"][h] == "V")
-                    sums_t(cs, SelC, bad, c)
-                    continue
-                if OPT["pen"][h] == "V":
-                    sums(ds, Zd, aH, c, (I1, cB))
-                else:
-                    if c % 2 == 0:
-                        mm([(ds, I1, cB, True, False)])
-                    sums(ds, Zd, aH, c, None, False)
-                if OPT["thr"][h] == "P":
-                    mm([(part(cs, c % 2, 64), BO0, sl(cB, 0, 64), True, False)]
-                       + [(part(cs, k, 8), IN, part(thr, h, 8), False, False) for k in range(8 * (c % 2), 8 * (c % 2) + 8)])
-                    sums(cs, Zc, bad, c, None)
-                else:
-                    sums(cs, Zc, bad, c, (IN, thrR[h]))
-            if OPT["pen"][h] == "V":
-                ts(pen[h], cs, 0.0, ALU.is_ge, 1048576.0, ALU.mult)
-                tt(keys[h], ds, pen[h], ALU.add)
-                if fast:
-                    least_t(soff[h], keys[h], h, None, lambda: hashed(h))
-                elif turned:
-                    least_t(soff[h], keys[h], h)
-                else:
-                    least(kS[h], keys[h], h, "H%d" % h)
+                sums(sl(S, 0, 256) if fast else keys[h], SelDV if fast else SelD, aH, 1024 * c, 1024, True)
+            if fast:
+                scan(run16[h], RST, keys[h], ALU.add, ALU.min)
+                tt(nf[h], keys[h], run16[h], ALU.not_equal)
+                scan(runV[h], nf[h], sl(S, 128, 256), ALU.mult, ALU.max)
+                o, w = small(h, 0), wideB[h]
+                tt(w, ind(runV[h], part(away[h], 0, 8)), E128, ALU.mult)
+                group([(o, w, SelN)] + rnd(o, M9) + [(o, w, SelF)])
+                ts(part(cU[h], 0, 8), o, 255.5, ALU.add)
+                ts(cbF[h], o, 4096 + 255.5, ALU.add)
+                o, w = small(h, 1), wide[h]
+                tt(w, ind(runV[h], rep15), E128, ALU.mult)
+                group([(o, w, SelF), (o, I1, c18)] + rnd(o, M19) + [(o, I1, ca)])
+                ts(soff[h], o, -2.0 ** -12, ALU.mult, u2k, ALU.add)
+                o, w = small(h, 2), wideC[h]
+                tt(w, ind(runV[h], part(away[h], 1, 8)), E128, ALU.mult)
+                group([(o, w, SelN)] + rnd(o, M11) + [(o, w, SelF)])
+                ts(part(vI[h], 1, 8), o, -256.5, ALU.add, 21.0, ALU.mult)
+                ts(part(cIi[h], 1, 8), part(vI[h], 1, 8), 2, ALU.arith_shift_right, 511, ALU.bitwise_and)
+                copy(part(cU[h], 1, 8), part(cIi[h], 1, 8))
             else:
-                act(sgn[h], cs, AF.Sign, bhalf, 1.0)
-                mm([(ds, IB, sgn[h], False, True)])
-                if turned:
-                    least_t(soff[h], ds, h)
-                else:
-                    if "H%d" % h not in OPT["red"]:
-                        move(OPT["ev"], lv[h][0], sl(ds, 0, 64))
-                    least(kS[h], ds, h, "H%d" % h, lv[h][0])
-            if not turned:
-                place(soff[h], lo1[h], kS[h])
-            move(OPT["dg"][h], D[h], ind(part(aH, h, 2048), soff[h]))
-            act(us[h], ind(part(uH, h, 2048), soff[h]), AF.Copy)
-            apart(lanes(sl(M, 0, 128), D[h], 1, 1, h) + lanes(sl(M, 128, 256), D[h], 2, 1, h))
-            move(OPT["dd"][h], DD[h], sl(M, 0, 256))
+                least(soff[h], keys[h], h, 0, None)
+            move(EN["dg"][h], D[h], ind(part(aH, h, 2048), soff[h]))
+            move(EN["us"][h], us[h], ind(part(uH, h, 2048), soff[h]))
+            apart(lanes(sl(M, 0, 128), D[h], 1, 1, h) + ([] if fast else lanes(sl(M, 128, 256), D[h], 2, 1, h)))
+            move(EN["dd"][h], sl(DD[h], 0, 128 if fast else 256), sl(M, 0, 128 if fast else 256))
             if not fast:
-                group(wsum(sl(M, 256, 272), Zv, DD[h]))
-                tt(vI[h], sl(M, 256, 272), c421, ALU.mult)
+                o = small(h, 2, 2)
+                group(wsum(o, Zv, DD[h]))
+                tt(vI[h], o, c421, ALU.mult)
                 ts(cIi[h], vI[h], 2, ALU.arith_shift_right, 511, ALU.bitwise_and)
                 copy(cU[h], cIi[h])
-            for qq, t, o, i, e in ((QP, TP, PU, 0, OPT["plist"][h]), (QG, TG, GU, 1, OPT["glist"][h])):
-                move(e, sl(qq, 16 + 128 * h, 144 + 128 * h), ind(SW, part(cU[h], i, 8)))
-                copy(part(o, h, 128), ind(turn(t[h], qq, 16 + 128 * h), pickW))
-            S = S2[h]
-            o = sl(S, 0, 128)
+                ts(cbF[h], part(cIi[h], 0, 8), 4096.0, ALU.add)
+            for qq, t, o, i, e in ((QP, TP, PU, 0, EN["pl"][h]), (QG, TG, GU, 1, EN["gl"][h])):
+                move(e, sl(qq[h], 16, 144), ind(SW, part(cU[h], i, 8)))
+                copy(part(o, h, 128), ind(turn(t[h], qq[h], 16), pickW))
+            o = sl(S, 256, 384)
             if OPT["kh"][h] == "V":
-                group([(o, I20, K[h]), (o, BOv, D[h])])
+                group([(o, I20, Kh[h]), (o, BOv, D[h])])
                 copy(k1[h], o)
                 ts(k2[h], k1[h], 2, ALU.arith_shift_right, 2047, ALU.bitwise_and)
-                copy(sl(kw_[h], 0, 128), k2[h])
+                tt(part(KW[h], 0, 128), k2[h], K[h], ALU.subtract)
             else:
-                o2 = sl(S, 256, 384)
-                group([(o2, I5, K[h]), (o2, BOq, D[h]), (o2, I1, c1k), (o2, IH, quarter), (o2, IN, quarter), (o2, IR2, ones)])
-                act(kr[h], o2, AF.Identity, bR2, 1.0)
-                group([(o, I5, K[h]), (o, BOq, D[h]), (o, I1, c38), (o, IR, ones), (o, IRN, ones), (o, IN, kr[h])])
-                move("A", sl(kw_[h], 0, 128), o)
-            o = sl(S, 128, 256)
+                evac(EN["kh"][h], part(KW[h], 0, 128), o,
+                     [(o, I5N, Kh[h]), (o, BOqn, D[h]), (o, ones, c1k)] + rnd(o, M11) + [(o, I4, Kh[h]), (o, BOq, D[h]), (o, I1, c38)])
+            o = sl(S, 384, 512)
             aim = [(o, IH if any(raws) else I1, Z[h])]
-            if raws[0] != raws[1]:
-                move(OPT["zm"], zm[h], ind(Z8[h], soff[h]))
+            if mixed[h]:
+                move(EN["zm"][h], zm[h], ind(Z8[h], soff[h]))
                 aim.append((o, IH, zm[h]))
-            rounded(sl(cz_[h], 128, 256), o, [(o, I1, quarter), (o, IH, us[h])] + aim)
-            apart([(sl(M, 0, 128), sh(YF, -1), Gn[h])])
-            act(GnB[h], sl(M, 0, 128), AF.Copy)
+            evac(EN["zf"][h], sl(cz_[h], 128, 256), o, [(o, I1, quarter), (o, IH, us[h])] + aim)
+            o = sl(S, 128, 256)
+            move("G", Ph[h], Pn[h])
+            group([(o, INH, Kh[h])] + lanes(o, Ph[h], 1, -1, h, YH))
 
-        def look(name, h, u, a, f, o, z4, d, z, kk):
-            es = sl(S2[h], 0, 128)
-            for c in (2 * h, 2 * h + 1):
-                tag = "%s%d%d" % (name, h, c % 2)
-                if tag in OPT["rawC"] or (name == "B" and h in OPT["rawB"]):
-                    w = nextw()
-                    act(part(u, c, 1024), ind(win, part(o, c, 64)), AF.Copy)
-                    minus(w, [(I1, u)], c, sl(z4, 0, 128))
-                    act(part(a, c, 1024), w, AF.Abs)
-                    terms = [(I1, a)]
+        def look(name, h, half):
+            u, a, f, o, z4, i = (uB, aB, fB, PU, ZB4[h], 0) if name == "B" else (uC, aC, fC, GU, ZC4[h], 1)
+            c, tag = 2 * h + half, "%s%d%d" % (name, h, half)
+            w = nextw()
+            if half == 0:
+                mm([(keys[h], I1, cP, True, False)])
+            for a0, n, at in pieces(tag, c):
+                terms = [(I1, a)]
+                if tag in OPT["raw"]:
+                    act(sl(u, a0, a0 + n), ind(win, sl(o, a0 // 16, (a0 + n) // 16)), AF.Copy)
+                    minus(w, [(I1, u)], a0, n, at, part(ZS[h], i, 128))
+                    act(sl(a, a0, a0 + n), sl(w, at, at + n), AF.Abs)
                 else:
-                    gathers(u, win, o, z4, c)
-                    for a0, a1 in pieces(tag, c):
-                        if tag in OPT["relu"]:
-                            ts(sl(a, a0, a1), sl(u, a0, a1), 0.0, ALU.max)
-                        else:
-                            act(sl(a, a0, a1), sl(u, a0, a1), AF.Abs)
-                    terms = [(I2, a), (IN, u)] if tag in OPT["relu"] else [(I1, a)]
-                w = nextw()
-                minus(w, terms, c, d)
-                for a0, a1 in pieces(tag, c):
-                    act(sl(f, a0, a1), sl(w, a0 - 1024 * c, a1 - 1024 * c), AF.Abs)
-                if c % 2 == 0:
-                    mm([(es, I1, cP, True, False)])
-                sums_t(es, SelE if name == "B" else SelG, f, c)
-            least_t(kk, es, h, z)
+                    gather(u, win, o, z4, a0, n, GW)
+                    if tag in OPT["relu"]:
+                        ts(sl(a, a0, a0 + n), sl(u, a0, a0 + n), 0.0, ALU.max)
+                        terms = [(I2, a), (IN, u)]
+                    else:
+                        act(sl(a, a0, a0 + n), sl(u, a0, a0 + n), AF.Abs)
+                minus(w, terms, a0, n, at, part(DD[h], 0, 128), sh(YN, i))
+                act(sl(f, a0, a0 + n), sl(w, at, at + n), AF.Abs)
+                sums(keys[h], SelE if name == "B" else SelG, f, a0, n, True)
 
         def partner(h):
-            M, raw, rawb = Mh[h], 2 * h in OPT["rawH"] and 2 * h + 1 in OPT["rawH"], h in OPT["rawB"]
-            def bounds(key):
-                ts(cp1[h], key, 640.0 * 256 - 100, ALU.is_lt, 1.0, ALU.add)
-                ts(thrE[h], key, a256, ALU.add)
-            look("B", h, uB, aB, fB, PU, ZB4[h], sl(DD[h], 0, 128), bounds, joff[h])
-            if h in OPT["dp"]:
-                o = sl(S2[h], 256, 384)
-                group([(o, INF, K[h])] + lanes(o, Pn[h], 1, -1, h, YF))
+            M = Mh[h]
+            raw = all("H%d%d" % (h, i) in OPT["raw"] for i in range(2))
+
+            def bounds(o, w):
+                apart([(o, w, SelF)])
+                ts(cp1[h], o, 640.0 * 256 - 100, ALU.is_lt, 1.0, ALU.add)
+                ts(thrE[h], o, a256, ALU.add)
+            least(joff[h], keys[h], h, 4, bounds)
             tt(PM[h], ind(IBIG, joff[h]), Pn[h], ALU.mult)
-            act(uj[h], ind(part(uB, h, 2048), joff[h]), AF.Copy)
-            act(mkB[h], ind(IBIG, joff[h]), AF.Copy)
-            group([(sl(M, 384, 392), I2K, sl(ones, 0, 8))] + wsum(sl(M, 384, 392), Zh, PM[h]))
-            tt(addB[h], sl(M, 384, 392), cp1[h], ALU.mult)
+            move(EN["uj"][h], uj[h], ind(part(uB, h, 2048), joff[h]))
+            move(EN["mk"][h], mkB[h], ind(IBIG, joff[h]))
+            o = small(h, 6)
+            group([(o, I1, cX)] + wsum(o, Zh, PM[h]) + [(o, I4K, cp1[h])])
+            ts(addB[h], o, NONE + 4096.0, ALU.min)
             back = lambda out: lanes(out, uj[h], 1, -1, h)
             if not raw:
-                if rawb:
-                    group([(sl(M, 128, 256), IN, Z[h])] + back(sl(M, 128, 256)))
-                else:
-                    apart(back(sl(M, 128, 256)))
-            if rawb:
-                apart(back(sl(M, 0, 128)))
-            else:
-                group([(sl(M, 0, 128), I1, Z[h])] + back(sl(M, 0, 128)))
+                apart(back(sl(M, 128, 256)))
+            group([(sl(M, 0, 128), I1, Z[h])] + back(sl(M, 0, 128)))
             n = 128 if raw else 256
-            act(sl(cz_[h], 256, 256 + n), sl(M, 0, n), AF.Copy)
+            move(EN["cz"][h], sl(cz_[h], 256, 256 + n), sl(M, 0, n))
             o = sl(M, 256, 384)
-            rounded(sl(CV[h], 128, 256), o, [(o, I1, quarter), (o, IH, uj[h]), (o, IH, sl(DD[h], 0, 128))] + ([] if rawb else [(o, IH, sl(ZB4[h], 0, 128))]))
+            group([(o, I1, quarter), (o, IH, uj[h]), (o, IH, part(DD[h], 0, 128)), (o, IH, part(ZS[h], 0, 128))] + rnd(o, M0) + [(o, INH, Ph[h])])
+            move(EN["cv"][h], part(CV[h], 1, 128), o)
 
-        def contact(h):
-            for c in (2 * h, 2 * h + 1):
-                if OPT["s6w"][h]:
-                    d = sl(cz_[h], 256, 384) if c in OPT["rawH"] else sl(cz_[h], 384, 512)
-                    for b in (2 * c, 2 * c + 1):
-                        w, onact = P[OPT["s6w"][h][b % len(OPT["s6w"][h])]], OPT["s6"][c] == "P"
-                        group([(w, IS, part(uH, b, 512))] + [(part(w, i, 128), ISN, d) for i in range(4)] + ([(w, IM, ones4)] if onact else []))
-                        if onact:
-                            act(part(q6, b, 512), w, AF.Abs, bM, 1.0)
-                        else:
-                            ts(part(q6, b, 512), w, MAGIC128, ALU.add, MAGIC128, ALU.subtract)
-                    continue
-                w = nextw()
-                minus(w, [(IS, uH)], c, sl(cz_[h], 256, 384) if c in OPT["rawH"] else sl(cz_[h], 384, 512), ISN, OPT["s6"][c] == "P")
-                if OPT["s6"][c] == "V":
-                    ts(part(q6, c, 1024), w, MAGIC128, ALU.add, MAGIC128, ALU.subtract)
-                elif OPT["s6"][c] == "P":
-                    act(part(q6, c, 1024), w, AF.Abs, bM, 1.0)
+        def contact(h, half):
+            c, tag = 2 * h + half, "S%d%d" % (h, half)
+            how, w = OPT["s6"][c], nextw()
+            d = sl(cz_[h], 256, 384) if "H%d%d" % (h, half) in OPT["raw"] else sl(cz_[h], 384, 512)
+            for a0, n, at in pieces(tag, c):
+                minus(w, [(IS, uH)], a0, n, at, d, ISN, M7 if how == "P" else None)
+                q, src = sl(q6, a0, a0 + n), sl(w, at, at + n)
+                if how == "V":
+                    ts(q, src, MAGIC * 2 ** 7, ALU.add, MAGIC * 2 ** 7, ALU.not_equal)
+                elif how == "P":
+                    act(q, src, AF.Abs, bM, 1.0)
                 else:
-                    act(part(a6, c, 1024), w, AF.Abs)
-                    ts(part(q6, c, 1024), part(a6, c, 1024), 63.5, ALU.is_gt, 128.0, ALU.mult)
+                    act(sl(a6, a0, a0 + n), src, AF.Abs)
+                    ts(q, sl(a6, a0, a0 + n), 63.5, ALU.is_gt)
 
         def replace(h):
-            S = P[OPT["s6bank"][h]]
-            cs, dp = sl(S, 0, 128), sl(S, 128, 256)
-            sizes = "V" not in OPT["s6"][2 * h:2 * h + 2]
-            if sizes:
-                act(thr6[h], ind(THR, part(LU, h, 8)), AF.Copy)
-                mm([(cs, IN, thr6[h], True, False)])
-            for c in range(2):
-                mm([(cs, zu(Zq, k), part(q6, 16 * h + k, 128), k == 0 and not sizes, k == 15) for k in range(8 * c, 8 * c + 8)])
-            if h in OPT["dp"]:
-                dp = sl(S2[h], 256, 384)
-            else:
-                group([(dp, INF, K[h])] + lanes(dp, Pn[h], 1, -1, h, YF))
-            if sizes:
-                ts(off[h], cs, 0.0, ALU.is_ge)
-            else:
-                act(asb[h], cs, AF.Abs)
-                tt(off[h], ind(THR, part(LU, h, 8)), asb[h], ALU.is_le)
-            tt(dp, dp, off[h], ALU.mult)
-            tt(sl(kw_[h], 256, 384), dp, K[h], ALU.add)
+            cs = sl(S2[0], 256 + 128 * h, 384 + 128 * h) if OPT["cs"][h] == "A" else sl(S2[1], 256, 384)
+            mm([(cs, IN, thr6[h], True, False)])
+            for c in (2 * h, 2 * h + 1):
+                mm([(cs, zu(Zq if OPT["s6"][c] == "P" else Zr, k % 16), part(q6, k, 128), False, k % 16 == 15) for k in range(8 * c, 8 * c + 8)])
+            ts(off[h], cs, 0.0, ALU.is_ge)
+            tt(part(KW[h], 2, 128), sl(S2[h], 128, 256), off[h], ALU.mult)
 
         def guesser(h):
-            look("C", h, uC, aC, fC, GU, ZC4[h], sl(DD[h], 128, 256), lambda key: tt(part(NH_, h, 8), key, thrE[h], ALU.is_ge), moff[h])
+            def outcome(o, w):
+                group([(o, w, SelF), (o, INF, thrE[h])] + rnd(o, M22) + [(o, IF, cbF[h])])
+                tt(kv[h], o, addB[h], ALU.min)
+                ts(part(NH_, h, 8), o, 2.0 ** 21, ALU.is_ge)
+            least(moff[h], keys[h], h, 7, outcome, True)
 
         def decide(h):
             M = Mh[h]
             nh, s3 = part(NH_, h, 8), part(s3w, h, 8)
-            tt(kvm[h], nh, addB[h], ALU.mult)
-            tt(kv[h], kvm[h], cbF[h] if h in OPT["fast"] else sl(cIi[h], 0, 8), ALU.max)
-            ts(kvU[h], kv[h], 2.0 * X0, ALU.min)
+            ts(kvU[h], ind(kv[h], mapK), -4096.0, ALU.add)
             tt(s3, nh, cp1[h], ALU.mult)
-            group([(sl(M, 0, 16), I1, cz), (sl(M, 8, 16), I1, nh)]
-                  + [(sl(M, b, 8, 3), PB[(b + 2 * h) % 3], sl(s3, b, 8, 3)) for b in range(3)])
-            ts(zs[h], sl(M, 0, 16), 128.0, ALU.mult, uF, ALU.add)
-            tt(GM[h], ind(IBIG, moff[h]), GnB[h], ALU.mult)
-            act(krow[h], ind(IOTA, kvU[h]), AF.Copy)
-            o = sl(M, 128, 256)
+            o = small(h, 9, 2)
+            group([(o, I1, cz), (part(o, 1, 8), I1, nh)] + [(sl(o, b, 8, 3), PB[(b + 2 * h) % 3], sl(s3, b, 8, 3)) for b in range(3)])
+            ts(zs[h], o, 128.0, ALU.mult, uF, ALU.add)
+            tt(GM[h], ind(IBIG, moff[h]), Gn[h], ALU.mult)
+            move(EN["kr"][h], krow[h], ind(IOTA, sl(kvU[h], 0, 12)))
+            o = sl(M, 256, 384)
             group([(o, BOh, GM[h]), (o, BOn, PM[h])])
-            tt(o, o, mkB[h], ALU.mult)
-            tt(sl(CV[h], 0, 128), o, Pn[h], ALU.add)
-            act(vals[h], ind(CV[h], selU[h]), AF.Copy)
-            tt(eq[h], ind(kv[h], repb), krow[h], ALU.is_equal)
-            tt(eq2[h], ind(kv[h], repo), krow[h], ALU.is_equal)
-            o = sl(S2[h] if h else M, 16, 24)
-            mm([(o, sh(YF, 0), kv[h], True, False)])
-            mm([(o, part(tri, u, 128), sl(eq[h], u, 128, 16), False, False) for u in range(16)])
-            mm([(sl(o, 0, 8, 2), zu(Z1, u), sl(eq2[h], u, 128, 32), False, u == 15) for u in range(16)])
-            ts(sl(scU[h], 0, 8, 2), sl(o, 0, 8, 2), spare, ALU.min)
-            ts(sl(scU[h], 1, 8, 2), sl(o, 1, 8, 2), spare2, ALU.min)
+            tt(part(CV[h], 0, 128), o, mkB[h], ALU.mult)
+            tt(vals[h], ind(CV[h], selU[h]), Pn[h], ALU.add)
+            tt(eq[h], ind(kv[h], repK), krow[h], ALU.is_equal)
+            scan(cnt[h], RSK, eq[h], ALU.mult, ALU.add)
+            for i, (ends, sp) in enumerate(((sl(cnt[h], 31, 128, 32), spare), (sl(cnt[h], 143, 192, 16), spare2))):
+                tt(sl(kvc[h], i, 8, 2), ends, sl(kv[h], i, 8, 2), ALU.mult)
+                ts(sl(scU[h], i, 8, 2), sl(kvc[h], i, 8, 2), -4096.0, ALU.add, sp, ALU.min)
 
         def prefix():
-            o = sl(P[OPT["pbank"]], 48, 64)
+            o = small(1, 12, 2)
             mm([(sl(o, b, 16, 3), l[b], sl(s, b, 16, 3), l is PB, l is PN) for b in range(3) for l, s in ((PB, s3w), (PN, NH_))])
-            tt(L2, o, L, ALU.add)
-            ts(lw, L2, 16.0, ALU.is_ge, -16.0, ALU.mult)
-            tt(L, L2, lw, ALU.add)
+            tt(L, o, L, ALU.add)
+            if last:
+                ts(lw, L, 16.0, ALU.is_ge, -16.0, ALU.mult)
+                tt(L, L, lw, ALU.add)
 
         def settle(h):
             if last:
-                act(part(ZO, h, 128), ind(sl(cz_[h], 0, 384), zoff[h]), AF.Copy)
-                move(OPT["kg"], part(KO, h, 128), ind(kw_[h], zoff[h]))
+                move(EN["zz"][h], part(ZO, h, 128), ind(sl(cz_[h], 0, 384), zoff[h]))
+                tt(part(KO, h, 128), ind(KW[h], zoff[h]), K[h], ALU.add)
                 return
-            nk = KW[(rnd + 1) % 2][h]
-            act(sl(CZ[(rnd + 1) % 2][h], 0, 128), ind(sl(cz_[h], 0, 384), zoff[h]), AF.Copy)
-            move(OPT["kg"], sl(nk, 128, 256), ind(kw_[h], zoff[h]))
-            copy(part(KU, h, 128), ind(turn(TK[h], nk, 128), pickW))
+            nk = KK[(rnd_ + 1) % 2][h]
+            move(EN["zz"][h], sl(CZ[(rnd_ + 1) % 2][h], 0, 128), ind(sl(cz_[h], 0, 384), zoff[h]))
+            tt(sl(nk, 16, 144), ind(KW[h], zoff[h]), K[h], ALU.add)
+            copy(part(KU, h, 128), ind(turn(TK[h], nk, 16), pickW))
 
-        tie[0:2] = ["round", 0]
-        act(thr, L, AF.Exp, b17, -LN2)
-        for h in range(2):
-            speaker(h)
-        step = {"B": partner, "C": guesser, "S": contact, "T": replace, "D": decide}
-        for s in OPT["order"]:
-            step[s[0]](int(s[1]))
-        for h in range(2):
+        def write(h):
+            tie[0] += "!" * last
+            if last and h == 0:
+                dma("G", ap(Xb), ap(XW), [XW], [Xb], 1.5)
             for b in range(4):
-                copy(ind(WIN, part(scU[h], b, 2)), part(vals[h], b, 32))
-        tie[0:2] = ["end" if last else "next", 0]
-        for h in range(2):
-            settle(h)
-        prefix()
-        if last:
-            for i in range(2):
-                copy(part(LL, i, 16), L)
-        else:
-            copy(LU, L)
-            o = sl(Mh[1], 32, 48)
-            apart([(o, BO1, NH_)])
-            reduce(ar[rnd], o, ALU.add)
-            if rnd == 0:
-                ts(aI, ar[0], -1.0, ALU.mult, 1024.0, ALU.add)
-            else:
-                tt(ar[1], ar[1], ar[0], ALU.add)
-                ts(aI, ar[1], -1.0, ALU.mult, 1024.0, ALU.add)
-            ts(aI2, aI, 31, ALU.bitwise_and)
-            ts(a256, aI2, 0.5, ALU.add, 256.0, ALU.mult)
+                for win_ in ([WB] if last else []) + [WIN]:
+                    copy(ind(win_, part(scU[h], b, 2)), part(vals[h], b, 32))
 
-    for rnd in range(3):
-        one_round(rnd)
+        def count(h):
+            prefix()
+            if last:
+                for i in range(2):
+                    copy(part(LL, i, 16), L)
+                return
+            copy(LU, L)
+            o = small(0, 12, 2)
+            apart([(o, BO1, NH_)])
+            reduce(ar[rnd_], o, ALU.add)
+            if rnd_ == 1:
+                tt(ar[1], ar[1], ar[0], ALU.add)
+            ts(aI, ar[rnd_], -1.0, ALU.mult, 1024.0, ALU.add)
+            ts(aI2, aI, 31, ALU.bitwise_and)
+            ts(a256, aI2, 256.0, ALU.mult, 128.0 - 2.0 ** 21, ALU.add)
+
+        return {"h": speaker, "b": partner, "c": guesser, "t": replace, "d": decide, "w": write, "e": settle, "p": count, "H": home, "S": contact,
+                "B": lambda h, i: look("B", h, i), "C": lambda h, i: look("C", h, i)}
+
+    rounds = [one_round(r) for r in range(3)]
+    for r in range(4):
+        for s in OPT["order"].split():
+            late = s[-1] == "-"
+            if 0 <= r - late < 3:
+                tie[0:2] = [s + ("!" if r - late == 2 and s[0] in "ep" else ""), 0]
+                rounds[r - late][s[0]](*[int(x) for x in s[1:].strip("-")])
+    tie[0:2] = ["end", 0]
 
     tr(LT, LL)
     copy(LO, ind(LT, pickL))
-    for h, e in enumerate("VA"):
-        move(e, part(Xb, h, 1024), part(XW, h, 1024))
     out = {"oz": (ZO, T.yz[:], 0.3), "ol": (LO, T.yl[:], 0.1), "oa": (SW, T.ya[:], 0.8), "ox": (part(Xb, 0, 1024), T.yx[:, 0:1024], 0.8),
            "oy": (part(Xb, 1, 1024), T.yx[:, 1024:2048], 0.8), "ok": (KO, T.yk[:], 0.4)}
-    for ci in range(5, len(CALLS)):
+    home_calls = [ci for ci in range(len(CALLS)) if CALLS[ci][0][0] == "o"]
+    for ci in home_calls:
         for k in CALLS[ci]:
             dma("S", T["s" + k][:], ap(out[k][0]), [out[k][0]], [("s" + k, 0, 8)], out[k][2])
             own("S", k, T["s" + k][0 if k == "ol" else rank], [("s" + k, 0, 8)])
         remote(ci)
-    for ci in range(5, len(CALLS)):
+    for ci in home_calls:
         for k in CALLS[ci]:
             src = T.lol[:, rows, :] if k == "ol" else T["l" + k][:]
-            dma("A", out[k][1], src, [("l" + k, 0, 8), ("call%d" % ci, 0, 1), KO, Xb], [("y" + k, 0, 1)], out[k][2], ext=arr(ci))
+            dma("A", out[k][1], src, [("l" + k, 0, 8), mark(k), KO, Xb], [("y" + k, 0, 1)], out[k][2], ext=arr(k))
     ops[0]["end"] = [(T.sem.sent, sent[0])]
     used, kept = {}, []
     for o in ops[::-1]:
-        if o["tie"][0] == "once" and o["e"] in "VA" and not o["dma"] and not any(
+        if o["tie"][0] == "once" and o["w"][0][0] in top and not o["dma"] and not any(
                 lo < w[2] and w[1] < hi for w in o["w"] for lo, hi in used.get(w[0], ())):
             continue
         kept.append(o)

import math
from concourse.bass import DstId, RemoteDMATransfer
from concourse.mybir import AluOpType as ALU, AxisListType as AX, ActivationFunctionType as AF

NF, NB, NI, NU, NH = 17408, 71680, 3072, 1536, 2560
SCRATCH = {
    "F": ("sbuf", [128, NF], "float32"), "B": ("sbuf", [128, NB], "bfloat16"), "I": ("sbuf", [128, NI], "int32"),
    "U": ("sbuf", [128, NU], "uint16"), "H": ("sbuf", [128, NH], "float16"),
    "W0": ("psum", [128, 1024], "float32"), "W1": ("psum", [128, 1024], "float32"),
    "SA": ("psum", [128, 512], "float32"), "SB": ("psum", [128, 512], "float32"),
    "M0": ("psum", [128, 512], "float32"), "M1": ("psum", [128, 512], "float32"),
}
KINDS = {"iz": (32, "bfloat16"), "il": (16, "int32"), "ik": (32, "int32"), "ix": (128, "bfloat16"), "iy": (128, "bfloat16"), "ia": (64, "int32"),
         "oz": (32, "bfloat16"), "ol": (16, "float32"), "ox": (128, "bfloat16"), "oy": (128, "bfloat16"), "oa": (64, "float32"), "ok": (32, "float32")}
CALLS = [("ik",), ("ix",), ("iy",), ("iz", "il"), ("ia",), ("oz", "ol"), ("ox",), ("oy",), ("oa",), ("ok",)]
for _k, (_n, _d) in KINDS.items():
    SCRATCH["s" + _k] = ("dram", [1 if _k[1] == "l" else 8, 128, _n], _d)
    SCRATCH["l" + _k] = ("dram", [8, 128, _n], _d)
NDMA, WORLD = 44, 256
PLAN = {}
SEMAPHORES = ["cV", "cA", "cP", "cG", "sent"] + ["arr%d" % i for i in range(len(CALLS))] + ["d%d" % i for i in range(NDMA)]
PSUM = ("W0", "W1", "SA", "SB", "M0", "M1")
MAGIC = 12582912.0
OPT = {"split": 9.0, "raw": ("H01", "H11"), "relu": (), "cut": {"H00": 512, "H01": 512, "C10": 512, "C11": 512}, "s6": "VVPP", "fast": (0,), "kh": "PP",
       "order": "H00 H01 h0 H10 H11 h1 B00 B01 b0 C00 C01 c0 B10 S00 B11 b1 S01 t0 C10 C11 c1 S10 S11 t1 d0 d1 w0 w1 e0 e1 p0", "cs": "AA",
       "eng": {"thr": "AA", "dg": "AA", "us": "AA", "dd": "AA", "pl": "AA", "gl": "AA", "kh": "VV", "zm": "AA", "uj": "AA", "mk": "AA", "cz": "AA",
               "cv": "AA", "gn": "AA", "kr": "AA", "t6": "AA", "zz": "AA", "zs": "AA", "zf": "AA"},
       "gw": 1024, "gwH": 512, "cases": ((1.0, 1.56, 0.22), (1.0, 1.56, 0.32), (1.4, 2.0, 0.15), (1.15, 1.56, 0.42), (1.25, 1.1, 0.18)), "slack": 1.5, "seed": 2,
       "vfix": 0.005, "afix": 0.065, "dma": 1.5, "hop": 2.8, "lat": 0.25, "slow": 1.12, "ga": 1.56, "iters": 5200, "polish": 4000, "heat": 0.2, "rough": 200, "near": 3.0, "again": 0.6,
       "table": {"H00": 0, "H01": 0, "H10": 3, "H11": 6, "B00": 7, "B01": 9, "C00": 12, "C01": 14, "B10": 16, "B11": 18, "C10": 20, "C11": 22, "S00": 16,
                 "S01": 19, "S10": 26, "S11": 27, "h0": 4, "h1": 10, "b0": 13, "c0": 18, "b1": 21, "c1": 25, "w0": 23, "w1": 29, "e0": 26, "e1": 32, "round": 34}}


def routes(T, topo):
    if "way" in PLAN:
        return PLAN["way"]
    cores = T.cores
    chip = lambda c: topo.cores_of(c)[0]
    mate = {chip(c): [m for m in range(WORLD) if topo.mates(c, m)] for c in cores}
    mate.update({chip(m[0]): topo.cores_of(c) for c, m in list(mate.items())})

    def links(a, b):
        if chip(a) == chip(b):
            return []
        if topo.same_plane(a, b):
            return [("out", chip(a), topo.die(a)), ("in", chip(b), topo.die(a))]
        over = [("mate", chip(a), topo.die(a))]
        return over if topo.mates(a, b) else over + [("out", chip(mate[chip(a)][0]), topo.die(a)), ("in", chip(b), topo.die(a))]

    can = {}
    for s, a in enumerate(cores):
        for r, b in enumerate(cores):
            if s != r:
                can[(s, r)] = [c for c in topo.cores_of(a) + mate[chip(b)] if (c == a or (c not in cores and topo.may_write(a, c))) and topo.may_write(c, b)]
    cost = {p: {c: links(cores[p[0]], c) + links(c, cores[p[1]]) + [("off", p[0])] * (c == cores[p[0]] or chip(c) != chip(cores[p[0]]))
                for c in cs} for p, cs in can.items()}

    def price(way):
        load = {}
        for p, c in way.items():
            for l in cost[p][c]:
                load[l] = load.get(l, 0) + 1
        return sum((v + (l[0] == "off")) ** 4 for l, v in load.items())
    way = {}
    for p in sorted(can, key=lambda p: len(can[p])):
        way[p] = min((c for c in can[p] if c == cores[p[0]] or c not in way.values()), key=lambda c: price(dict(way, **{}) | {p: c}))
    best, moved = price(way), True
    while moved:
        moved = False
        for p in can:
            for q in can:
                for c in can[p]:
                    for d in (can[q] if p < q and (p[0] == q[0] or p[1] == q[1]) else [way[q]] if p == q else []):
                        new = dict(way)
                        new[q] = d
                        new[p] = c
                        relays = [x for x in new.values() if x not in cores]
                        if len(set(relays)) == len(relays) and price(new) < best:
                            way, best, moved = new, price(new), True
    PLAN["way"] = way
    return way


def bits(es):
    m = 0
    for e in es:
        m |= 1 << e
    return m


def first_hop(T, topo, way, s, ci):
    me = T.cores[s]
    items = [(k, r) for r in range(len(T.cores)) if r != s for k in CALLS[ci]]
    to = {r: T.cores[r] if way[(s, r)] == me else way[(s, r)] for k, r in items}
    items.sort(key=lambda it: len(topo.engines(me, to[it[1]])))
    per = 2 if len(CALLS[ci]) == 1 else 1
    spare = len(topo.engines(me, me)) - per * len(items)
    used, out = [], []
    for k, r in items:
        more = per if spare >= per and to[r] not in topo.cores_of(me) else 0
        spare -= more
        es = [e for e in topo.engines(me, to[r]) if e not in used][:per + more]
        used += es
        out.append((k, r, to[r], es))
    return out


def second_hop(T, topo, relay, r, ci):
    es = topo.engines(relay, T.cores[r])
    n = len(es) // len(CALLS[ci])
    return [(k, es[i * n:(i + 1) * n]) for i, k in enumerate(CALLS[ci])]


def arrivals(T, topo, way, r, ci):
    tot = 0
    for s in range(len(T.cores)):
        if s == r:
            continue
        if way[(s, r)] == T.cores[s]:
            tot += sum(len(es) for k, d, to, es in first_hop(T, topo, way, s, ci) if d == r)
        else:
            tot += sum(len(es) for k, es in second_hop(T, topo, way[(s, r)], r, ci))
    return tot


def relay_program(g, core, T, topo, way):
    for (s, r), c in way.items():
        if c != core:
            continue
        rid, pid = topo.addr(T.cores[r], core)
        sent = 0
        for ci in range(len(CALLS)):
            g.wait_ge(T.sem["arr%d" % ci], sum(len(es) for k, d, to, es in first_hop(T, topo, way, s, ci) if d == r))
            tr = []
            for k, es in second_hop(T, topo, core, r, ci):
                tr.append(RemoteDMATransfer(dst_ids=[DstId(rid=rid, pnc=pid)], dma_engine_mask=bits(es), remote_sem=T.sem["arr%d" % ci],
                                            src=T["l" + k][s], dst=T["l" + k][s]))
                sent += len(es)
            g.remote_dma_fused(tr, local_sem=T.sem.sent)
        g.wait_ge(T.sem.sent, sent)


def rank_program(g, core, T, topo):
    way = routes(T, topo)
    rank = T.rank_of(core)
    if rank is None:
        relay_program(g, core, T, topo, way)
        return
    ops = build(g, core, rank, T, topo, way)
    emit(g, T, ops)


def depend(ops):
    hist, preds, starts, held = {}, [], {}, {}
    for i, o in enumerate(ops):
        p = {}
        for acc, isw in [(a, False) for a in o["r"]] + [(a, True) for a in o["w"]]:
            name, lo, hi = acc[0], acc[1], acc[2]
            st = acc[3] if len(acc) > 3 else 1
            for bk in range(lo // 256, (hi - 1) // 256 + 1):
                keep = []
                for (j, l2, h2, w2, s2) in hist.get((name, bk), []):
                    hit = l2 < hi and lo < h2 and not (st == s2 and (lo - l2) % st)
                    same = ops[j]["e"] == o["e"] and not (o["dma"] or ops[j]["dma"])
                    if j != i and hit and (isw or w2):
                        p[j] = p.get(j, False) or not ((same and o["e"] == "P") or name.startswith("call"))
                    cover = st == 1 and lo <= max(l2, 256 * bk) and min(h2, 256 * bk + 256) <= hi
                    if not (hit and isw and cover and j != i):
                        keep.append((j, l2, h2, w2, s2))
                keep.append((i, lo, hi, isw, st))
                hist[(name, bk)] = keep
        for bank, begins, stays in o["acc"]:
            if begins:
                for j in ([held[bank]] if bank in held else []) + (starts.pop(bank, []) if stays else []):
                    p.setdefault(j, False)
                if not stays:
                    starts.setdefault(bank, []).append(i)
            else:
                if bank in held and held[bank] != i:
                    p.setdefault(held[bank], False)
            if stays or not begins:
                held[bank] = i
        preds.append(p)
    return preds


def arrange(ops):
    n, lat = len(ops), OPT["lat"]
    preds = depend(ops)
    succ = [[] for _ in range(n)]
    for i in range(n):
        for j in preds[i]:
            succ[j].append(i)
    fixed = [o["dma"] or o["ext"] or o["x"] > 1 or o["c"] == 1.0 for o in ops]
    eng, c = [o["e"] for o in ops], [max(ops[i]["c"] * (1.0 if fixed[i] else OPT["slow"]), 0.001) for i in range(n)]
    banks = [sorted({(a[0], b) for a in o["r"] + o["w"] if a[0] in PSUM for b in range(a[1] // 512, (a[2] - 1) // 512 + 1)}) for o in ops]
    lag = [{j: (ops[j]["x"] + lat if sem or ops[j]["x"] > 1 else 0.0) for j, sem in preds[k].items()} for k in range(n)]
    fw = [list(lag[k].items()) for k in range(n)]
    bw = [[(k, lag[k][j]) for k in succ[j]] for j in range(n)]
    pad = lat + 0.05

    def place(seq, dep, head):
        end, why = [0.0] * n, [-1] * n
        busy = {e: ([], [], []) for e in "VAPGS"}
        used = {b: ([], [], []) for bs in banks for b in bs}
        for i in seq:
            t, ci, w, e = head[i], c[i], -1, eng[i]
            for j, d in dep[i]:
                if end[j] + d > t:
                    t, w = end[j] + d, j
            los, his, who = busy[e]
            m = a = len(los)
            while a and his[a - 1] > t:
                a -= 1
            while True:
                while a < m and los[a] < t + ci - 1e-9:
                    if his[a] > t:
                        t, w = his[a], who[a]
                    a += 1
                if not banks[i]:
                    break
                t0 = t
                for b in banks[i]:
                    l2, h2, w2 = used[b]
                    k = len(l2)
                    while k and h2[k - 1] > t - pad + 1e-9:
                        k -= 1
                    while k < len(l2) and l2[k] < t + ci + pad - 1e-9:
                        if eng[w2[k]] != e:
                            t, w = h2[k] + pad, w2[k]
                        k += 1
                if t == t0:
                    break
            los.insert(a, t)
            his.insert(a, t + ci)
            who.insert(a, i)
            end[i], why[i] = t + ci, w
            for b in banks[i]:
                l2, h2, w2 = used[b]
                k = len(l2)
                while k and h2[k - 1] > t:
                    k -= 1
                l2.insert(k, t)
                h2.insert(k, t + ci)
                w2.insert(k, i)
        return end, why

    def feasible(key, dep, forward):
        k2 = list(key)
        for i in (range(n) if forward else range(n - 1, -1, -1)):
            for j, d in dep[i]:
                if k2[j] >= k2[i]:
                    k2[i] = k2[j] + 1e-7
        return sorted(range(n), key=lambda i: k2[i])

    zero, tailx = [0.0] * n, [o["x"] for o in ops]
    cases = []
    for f, ga, wake in OPT["cases"]:
        cc = [c[i] if fixed[i] else f * (ops[i]["c"] + ops[i]["g"] * (ga - OPT["ga"])) for i in range(n)]
        cases.append((cc, [[(j, d + wake - lat if preds[k][j] else d) for j, d in fw[k]] for k in range(n)], wake))
    outs = [i for i in range(n) if not succ[i]]

    def replay(seq, cc, dep, wake):
        end, free, last = [0.0] * n, {e: 0.0 for e in "VAPGS"}, {}
        for i in seq:
            e = eng[i]
            t = free[e]
            for j, d in dep[i]:
                if end[j] + d > t:
                    t = end[j] + d
            for b in banks[i]:
                for e2 in "VAP":
                    if e2 != e and last.get((b, e2), 0.0) > t:
                        t = last[(b, e2)]
            end[i] = free[e] = t + cc[i]
            for b in banks[i]:
                last[(b, e)] = end[i] + tailx[i] + wake
        return max(end[i] + tailx[i] for i in outs), end

    twins = {}
    for i, o in enumerate(ops):
        twins.setdefault(o["tie"], []).append(i)
    seed = [OPT["seed"]]

    def draw():
        seed[0] = (seed[0] * 1103515245 + 12345) % 2147483648
        return (seed[0] + 1) / 2147483649.0

    def forth(key):
        end, why = place(feasible(key, fw, True), fw, zero)
        e = max(outs, key=lambda i: end[i] + tailx[i])
        return end[e] + tailx[e], end, why, e

    def again(s):
        back = place(feasible([-t for t in s[1]], bw, False), bw, tailx)[0]
        return min(s, forth([-t for t in back]), key=lambda x: x[0])

    marks, table = {}, dict(OPT["table"])
    for i, o in enumerate(ops):
        k = o["tie"][0].strip("!-")
        r = 2 if "!" in o["tie"][0] else twins[o["tie"]].index(i)
        if k in table and (k, r) not in marks.values() and (o["g"] > 0.2 if k[0] in "HBC" else eng[i] in "VA" and o["c"] > 0.3 if k[0] == "S" else eng[i] == "V"):
            marks[i] = (k, r)

    def timed(tb):
        key = [0.0] * n
        for i in range(n - 1, -1, -1):
            t = min([key[k] - d for k, d in bw[i]] + [OPT["slow"] * (3 * tb["round"] + 12) - tailx[i]]) - c[i]
            key[i] = min(t, OPT["slow"] * (tb[marks[i][0]] + marks[i][1] * tb["round"])) if i in marks else t
        return again(forth(key))
    cur, names = timed(table), sorted(table)
    for it in range(OPT["rough"]):
        tb = dict(table)
        for _ in range(1 + int(3 * draw())):
            tb[names[int(draw() * len(names))]] += (draw() - 0.5) * (1.0, 3.0, 6.0)[int(3 * draw())]
        new = timed(tb)
        if new[0] <= cur[0] - 0.4 * (1.0 - it / OPT["rough"]) * math.log(draw()):
            cur, table = new, tb
    def judged(s, m):
        seq = sorted(range(n), key=lambda i: (s[1][i] - c[i], i))
        return (s[0] + sum(replay(seq, cc, dep, wake)[0] for cc, dep, wake in cases[:m])) / (m + 1)
    top, now, m, heat = None, 0.0, 0, OPT["heat"]
    for it in range(OPT["iters"] + OPT["polish"]):
        if it == OPT["iters"]:
            cur, m = top[1], len(cases)
            now = judged(cur, m)
            top = (now, cur)
        heat = OPT["heat"] * (1.0 - it / OPT["iters"]) if m == 0 else 0.03
        span, end, why, i = cur
        key, arcs = [end[k] - c[k] for k in range(n)], []
        while why[i] >= 0:
            if why[i] not in preds[i]:
                arcs.append(i)
            i = why[i]
        if arcs and draw() < 0.75:
            v = arcs[int(draw() * len(arcs))]
            u = why[v]
            d = key[v] - key[u] + (0.01, 0.01, 0.3, 0.8, 1.5)[int(draw() * 5)]
            if draw() < 0.5:
                todo = [(j, key[j] - d) for j in twins[ops[v]["tie"]]]
                while todo:
                    j, t = todo.pop()
                    if key[j] > t:
                        key[j] = t
                        todo += [(k, t - 1e-4) for k in preds[j]]
            else:
                for j in twins[ops[u]["tie"]]:
                    key[j] += d
        else:
            lo, amp = span * draw() - 3.0, 0.5 * (1 + int(4 * draw()))
            for k in range(n):
                if lo < key[k] < lo + 6.0:
                    d = amp * (draw() - 0.5)
                    for j in twins[ops[k]["tie"]]:
                        key[j] = end[j] - c[j] + d
        new = forth(key)
        if new[0] < span + OPT["near"] and draw() < OPT["again"]:
            new = again(new)
        if new[0] < span + (OPT["slack"] if m == 0 else 0.6):
            tot = judged(new, m) if m else new[0]
            if top is None or tot <= now - heat * math.log(draw()):
                cur, now = new, tot
                if top is None or tot < top[0]:
                    top = (tot, cur)
    order = feasible([top[1][1][i] - c[i] for i in range(n)], fw, True)
    end = replay(order, *cases[0])[1]
    start = [end[i] - cases[0][0][i] for i in range(n)]
    fin = [end[i] + tailx[i] for i in range(n)]
    pos, cnt = {}, {e: 0 for e in "VAPGS"}
    for i in order:
        cnt[eng[i]] += 1
        pos[i] = cnt[eng[i]]
    known = {e: {} for e in "VAPGS"}
    snap, waits, need, last = {}, {}, set(), {}
    for i in order:
        kn = known[eng[i]]
        best = {}
        turn = [last[(b, e)] for b in banks[i] for e in "VAP" if e != eng[i] and (b, e) in last]
        for j in [j for j, sem in preds[i].items() if sem] + turn:
            key = ("d", j) if ops[j]["dma"] else eng[j]
            if key not in best or pos[j] > pos[best[key]]:
                best[key] = j
        ws = []
        for key, j in sorted(best.items(), key=lambda kv: -fin[kv[1]]):
            if kn.get(key, 0) >= pos[j]:
                continue
            ws.append(j)
            need.add(j)
            kn[key] = pos[j]
            for k2, v in snap[j].items():
                if kn.get(k2, 0) < v:
                    kn[k2] = v
        waits[i] = ws
        snap[i] = dict(kn)
        for b in banks[i]:
            last[(b, eng[i])] = i
    return order, waits, need, start, fin, [replay(order, *cs)[0] for cs in cases]


def emit(g, T, ops):
    if "p" not in PLAN:
        PLAN["p"] = arrange(ops)
    order, waits, need = PLAN["p"][:3]
    q = {"V": g.vector, "A": g.scalar, "P": g.tensor, "G": g, "S": g.sync}
    num, cnt, nd, tail = {}, {e: 0 for e in "VAPG"}, 0, []
    for i in order:
        o = ops[i]
        for j in waits[i]:
            q[o["e"]].wait_ge(num[j][0], num[j][1])
        for sem, v in o["ext"]:
            q[o["e"]].wait_ge(sem, v)
        ins = o["f"]()
        if o["dma"]:
            num[i] = (T.sem["d%d" % nd], 16)
            nd += 1
            ins.then_inc(num[i][0], 16)
            if i not in need:
                tail.append(i)
        elif i in need:
            cnt[o["e"]] += 1
            num[i] = (T.sem["c" + o["e"]], cnt[o["e"]])
            ins.then_inc(num[i][0], 1)
    for i in tail:
        g.wait_ge(num[i][0], 16)
    for sem, v in ops[0]["end"]:
        g.wait_ge(sem, v)


def build(g, core, rank, T, topo, way):
    ops = []
    top = {"F": 0, "B": 0, "I": 0, "U": 0, "H": 0}
    CY, GA, PC = 0.00083, OPT["ga"], 0.00042
    two = ("B", "U", "H")
    tie = ["once", 0]
    EN = OPT["eng"]

    def new(pool, n):
        lo = top[pool]
        top[pool] = lo + (n + 15) // 16 * 16
        assert top[pool] <= SCRATCH[pool][1][1], pool
        return (pool, lo, lo + n, 1)

    def pair(pool, n):
        return [new(pool, n), new(pool, n)]

    def sl(r, a, b, s=1):
        return (r[0], r[1] + a, r[1] + b, s)

    def part(r, i, n):
        return sl(r, n * i, n * i + n)

    def width(r):
        return (r[2] - r[1] + r[3] - 1) // r[3]

    def ind(win, off):
        return ("ind", win, off)

    def ap(r):
        if r[0] == "ind":
            return ap(r[1]).indirect(ap(r[2]))
        if r[3] == 1:
            return T[r[0]][:, r[1]:r[2]]
        return T[r[0]][:, r[1]:r[2]:r[3]]

    def isref(x):
        return isinstance(x, tuple)

    def val(x):
        return ap(x) if isref(x) else x

    def add(e, f, r, w, c, x=0.0, dma=False, ext=(), acc=()):
        rr = []
        for a in r:
            if isref(a):
                rr += [a[1], a[2]] if a[0] == "ind" else [a]
        ww = []
        for a in w:
            if a[0] == "ind":
                ww.append(a[1])
                rr += [a[1], a[2]]
            else:
                ww.append(a)
        gathered = sum(16 * width(a[2]) * CY for a in r if isref(a) and a[0] == "ind")
        tie[1] += 1
        ops.append({"e": e, "f": f, "r": rr, "w": ww, "c": c, "x": x, "dma": dma, "ext": list(ext), "end": [], "g": gathered, "tie": tuple(tie),
                    "acc": list(acc)})

    def vcost(out, a, k=1.0):
        if a[0] == "ind":
            return 0.05 + width(out) * GA * CY
        if out[0] == "ind":
            return 0.05 + width(a) * 3.8 * CY
        if k == 1.0 and out[0] in two and a[0] in two:
            k = 0.5
        return OPT["vfix"] + max(64, width(a) * k) * CY

    def copy(out, a):
        add("V", lambda: g.vector.tensor_copy(ap(out), ap(a)), [a], [out], vcost(out, a))

    def tt(out, a, b, op):
        k = 1.001 if a[0] in PSUM or b[0] in PSUM else 2.0
        add("V", lambda: g.vector.tensor_tensor(ap(out), ap(a), ap(b), op), [a, b], [out], vcost(out, a, k))

    def ts(out, a, s1, op0, s2=None, op1=None):
        if op1 is None:
            f = lambda: g.vector.tensor_scalar(ap(out), ap(a), val(s1), None, op0)
        else:
            f = lambda: g.vector.tensor_scalar(ap(out), ap(a), val(s1), val(s2), op0, op1)
        add("V", f, [a, s1, s2], [out], vcost(out, a))

    def scan(out, a, b, op0, op1):
        add("V", lambda: g.vector.tensor_tensor_scan(ap(out), ap(a), ap(b), 0.0, op0, op1), [a, b], [out],
            OPT["vfix"] + width(out) * CY * (0.5 if out[0] == a[0] == b[0] == "B" else 1.0))

    def tr(out, a):
        add("V", lambda: g.vector.transpose(ap(out), ap(a)), [a], [out], vcost(out, a))

    def fill(out, v):
        add("V", lambda: g.vector.memset(ap(out), v), [], [out], vcost(out, out))
        return out

    def reduce(out, a, op):
        add("V", lambda: g.vector.tensor_reduce(ap(out), ap(a), AX.X, op), [a], [out], 0.07)

    def act(out, a, fn, bias=None, scale=None):
        def f():
            if bias is None and scale is None:
                return g.scalar.activation(ap(out), ap(a), fn)
            if bias is None:
                return g.scalar.activation(ap(out), ap(a), fn, scale=val(scale))
            return g.scalar.activation(ap(out), ap(a), fn, bias=val(bias), scale=val(scale))
        c = 0.065 + width(out) * GA * CY if a[0] == "ind" else OPT["afix"] + max(64, width(out)) * CY
        add("A", f, [a, bias, scale], [out], c)

    def scaled(out, a, w, e="A"):
        if e == "A":
            act(out, a, AF.Identity, None, w)
        else:
            ts(out, a, w, ALU.mult)
        return out

    def select(out, a, pattern, op, cm):
        add("G", lambda: g.affine_select(ap(out), ap(a), pattern, op, 0.0, 0, cm), [a], [out], 0.17 + 2 * CY * width(a))

    def move(e, out, a):
        if e == "A":
            act(out, a, AF.Copy)
        elif e == "G":
            select(out, a, [[0, width(a)]], ALU.is_ge, 0)
        else:
            copy(out, a)

    def mm(items):
        def f():
            last = None
            for out, l, r, st, sp in items:
                last = g.tensor.matmul(ap(out), ap(l), ap(r), st, sp)
            return last
        c = sum(max(min(64, width(l)), width(r)) * (4 if l[0] == "F" else 1) * PC for out, l, r, st, sp in items)
        acc = {}
        for out, l, r, st, sp in items:
            b = (out[0], out[1] // 512)
            acc[b] = (acc[b][0] if b in acc else st, not sp)
        add("P", f, [x for it in items for x in it[1:3]], [it[0] for it in items], c, x=0.1, acc=[(b, v[0], v[1]) for b, v in acc.items()])

    def group(items, most=9.0):
        run, t = [], 0.0
        for i, (o, l, r) in enumerate(items):
            c = max(min(64, width(l)), width(r)) * (4 if l[0] == "F" else 1) * PC
            if run and t + c > most:
                mm(run)
                run, t = [], 0.0
            run.append((o, l, r, i == 0, i == len(items) - 1))
            t += c
        mm(run)

    def apart(items):
        mm([(o, l, r, True, True) for o, l, r in items])

    def iota(out, pattern, cm=0, rd=(), base=0):
        if out[0] == "I":
            f = lambda: g.iota(ap(out), pattern, base, cm)
        else:
            f = lambda: g.iota(ap(out), pattern, base, cm, allow_small_or_imprecise_dtypes=True)
        add("G", f, list(rd), [out], 0.13 + 2 * CY * width(out))
        return out

    def dma(e, out, a, r, w, us, ext=()):
        qq = {"S": g.sync, "A": g.scalar, "G": g}[e]
        add(e, lambda: qq.dma_start(out, a), r, w, 0.1 if e != "G" else 1.0, x=OPT["dma"] + us, dma=True, ext=ext)

    sent = [0]

    def remote(ci):
        trs = []
        for k, r, to, es in first_hop(T, topo, way, rank, ci):
            rid, pid = topo.addr(to, core)
            trs.append(RemoteDMATransfer(dst_ids=[DstId(rid=rid, pnc=pid)], dma_engine_mask=bits(es), remote_sem=T.sem["arr%d" % ci],
                                         src=T["s" + k][0 if k[1] == "l" else r], dst=T["l" + k][rank]))
            sent[0] += len(es)
        add("G", lambda: g.remote_dma_fused(trs, local_sem=T.sem.sent), [("s" + k, 0, 8) for k in CALLS[ci]] + [("callo", 0, 1)],
            [("call%d" % ci, 0, 1), ("callo", 0, 1)], 1.0, x=0.0)
        add("G", lambda: None, [("call%d" % ci, 0, 1)], [("call%d" % ci, 0, 1)], 0.0,
            x=OPT["hop"] + KINDS[CALLS[ci][0]][0] / 64.0)

    def arr(k):
        ci = call_of(k)
        return [(T.sem["arr%d" % ci], arrivals(T, topo, way, rank, ci))]

    def call_of(k):
        return [k in c for c in CALLS].index(True)

    def mark(k):
        return ("call%d" % call_of(k), 0, 1)

    def own(e, k, src, rd):
        dma(e, T["l" + k][rank], src, rd, [("l" + k, 0, 1)], 0.1)

    P = {k: (k, 0, SCRATCH[k][1][1], 1) for k in PSUM}
    rows = slice(16 * rank, 16 * rank + 16)

    X0, NONE = 512, 2600
    WIN = new("F", X0 + 2080)
    XW, SW = sl(WIN, X0, X0 + 2048), sl(WIN, 0, 512)
    WB = new("B", X0 + 2080)
    Xb = sl(WB, X0, X0 + 2048)
    CZ = [pair("B", 512), pair("B", 512)]
    LISTS = new("F", 8 * 144 + 16)
    lst = [sl(LISTS, 144 * i, 144 * i + 160) for i in range(8)]
    KK, QP, QG = [lst[0:2], lst[6:8]], lst[2:4], lst[4:6]
    KW = pair("F", 384)
    L = new("F", 16)
    KU, LU = new("U", 256), new("U", 16)
    KI, LI, SI = new("I", 256), new("I", 16), new("I", 512)
    ZO, KO = new("B", 256), new("F", 256)

    dma("S", T["six"][:], T.x0[:, 0:1024], [], [("six", 0, 8)], 0.8)
    dma("S", T.siy[:], T.x0[:, 1024:2048], [], [("siy", 0, 8)], 1.5)
    dma("A", T.siz[:], T.z0[:], [], [("siz", 0, 8)], 0.2)
    dma("A", T.sil[:], T.l0[:], [], [("sil", 0, 8)], 0.1)
    dma("A", T.sik[:], T.kw[:], [], [("sik", 0, 8)], 0.4)
    dma("S", T.sia[:], T.asc[:], [], [("sia", 0, 8)], 0.8)
    own("A", "iz", T.z0[rows, :], [])
    own("A", "il", T.l0[:], [])
    own("A", "ik", T.kw[rows, :], [])
    own("S", "ix", T.x0[rows, 0:1024], [])
    own("S", "iy", T.x0[rows, 1024:2048], [])
    own("S", "ia", T.asc[rows, :], [])
    for ci in range(len(CALLS)):
        if CALLS[ci][0][0] == "i":
            remote(ci)
    dma("S", ap(ZO), T.liz[:], [("liz", 0, 8), mark("iz")], [ZO], 0.3, ext=arr("iz"))
    dma("S", ap(LI), T.lil[:, rows, :], [("lil", 0, 8), mark("il")], [LI], 0.1, ext=arr("il"))
    dma("S", ap(KI), T.lik[:], [("lik", 0, 8), mark("ik")], [KI], 0.4, ext=arr("ik"))
    for h, k in enumerate(("ix", "iy")):
        dma("S", ap(part(Xb, h, 1024)), T["l" + k][:], [("l" + k, 0, 8), mark(k)], [part(Xb, h, 1024)], 0.8, ext=arr(k))
    dma("S", ap(SI), T.lia[:], [("lia", 0, 8), mark("ia")], [SI], 0.8, ext=arr("ia"))
    for h, k in enumerate(("lix", "liy")):
        dma("G", ap(part(XW, h, 1024)), T[k][:], [(k, 0, 8), ("callo", 0, 1), Xb, SI], [part(XW, h, 1024)], 1.5)

    after = [("callo", 0, 1)]
    def col(pool="F"):
        return new(pool, 1)

    def const(n, v, pool="B"):
        return fill(new(pool, n), v)

    def line(out, a, w, b):
        act(out, a, AF.Identity, b, w)
        return out
    pI, pF = iota(col("I"), [[1, 1]], 1), iota(col(), [[1, 1]], 1)
    one2, Y, YF = iota(new("B", 256), [[0, 256]], 0, (), 1), new("B", 256), new("F", 256)
    ones = sl(one2, 0, 128)
    select(Y, one2, [[0, 2], [-1, 128]], ALU.is_equal, 1)
    cM = iota(new("F", 176), [[1, 176]], 0, (), -16)
    cF, c16 = sl(cM, 16, 176), sl(cM, 16, 32)
    c144 = iota(new("F", 144), [[0, 9], [1, 16]])
    c15 = sl(c144, 0, 128)
    c112 = iota(new("F", 128), [[16, 8], [0, 16]], 0, after)
    lists, cols = new("F", 29), new("F", 4)
    iota(sl(lists, 12, 20), [[16, 8]], 0, after, 15)
    iota(sl(lists, 20, 21), [[1, 1]], 0, after, 127)
    iota(sl(lists, 21, 29), [[16, 8]], 0, after, 15)
    iota(sl(cols, 0, 2), [[896, 2]], 0, after, 1024)
    iota(sl(cols, 2, 4), [[16, 2]], 0, after, X0 + 2048)
    iota(sl(lists, 0, 8), [[2, 4], [0, 2]], 0, after)
    iota(sl(lists, 8, 12), [[2, 4]], 0, after, 1)
    c421 = iota(new("F", 16), [[17, 2], [0, 8]], 0, after, 4)
    c31 = iota(new("F", 128), [[0, 4], [1, 32]], 0, after)
    ramp = iota(new("B", 2048), [[1, 16], [0, 128]], 0, after)
    IOTA = iota(new("F", NONE + 8), [[1, NONE + 8]], 0, after, 4096)
    uI, uF, kF, hF, u7, u8, Sel1 = col("I"), col(), col(), col(), col(), col(), new("B", 8)
    ts(uI, pI, 15, ALU.bitwise_and)
    copy(uF, uI)
    tt(kF, pF, uF, ALU.subtract)
    ts(Sel1, sl(cF, 0, 128, 16), kF, ALU.is_equal)
    reduce(hF, sl(Sel1, 1, 8, 2), ALU.add)
    ts(u8, uF, 8.0, ALU.is_ge)
    ts(u7, u8, -8.0, ALU.mult, uF, ALU.add)
    LN2 = math.log(2.0)
    wcb, wc, wqb, wq, wr, wv = col("B"), col(), col("B"), col(), col(), col()
    b20, b21, b27 = const(1, 20 * LN2, "F"), const(1, 21 * LN2, "F"), const(1, 27 * LN2, "F")
    act(wcb, uF, AF.Exp, b20, -LN2)
    ops[-1]["c"] += 1.3
    move("A", wc, wcb)
    act(wqb, uF, AF.Exp, b21, -3 * LN2)
    move("A", wq, wqb)
    scaled(wr, wqb, 128.0)
    ts(wv, uF, 15.0, ALU.mult, 7.0, ALU.add)
    Z0, Zh = new("B", 160), new("H", 160)
    ts(Z0, sl(cM, 0, 160), kF, ALU.is_equal)
    move("A", Zh, Z0)
    Zv, Zq, Zr = (scaled(new("B", 160), Z0, w) for w in (wv, wq, wr))

    def zu(z, u):
        return sl(z, 16 - u, 144 - u)
    move("A", YF, Y)

    def sh(y, k):
        k %= 8
        return sl(y, 128 - 16 * k, 256 - 16 * k)

    def eye(pool, w):
        return scaled(new(pool, 128), sh(Y, 0), w, "V" if pool == "B" else "A")
    I1, IF = sh(Y, 0), sh(YF, 0)
    YN = scaled(new("B", 256), Y, -1.0, "V")
    IN = sh(YN, 0)
    IH, I2, IS, ISN, I4K = (eye("B", w) for w in (0.5, 2.0, 1.3125, -1.3125, 4096.0))
    INF, INH, I20, I4, I5N, YH = eye("F", -1.0), eye("H", -1.0), eye("H", 20.0), eye("H", 4.0), eye("H", -5.0), new("H", 256)
    move("A", YH, Y)
    M0, M7, M11, M22 = const(128, MAGIC), const(512, MAGIC * 2 ** 7), const(128, MAGIC * 2 ** 11), const(128, MAGIC * 2 ** 22)
    M8, M9, M19 = const(8, MAGIC * 2 ** 8), const(8, MAGIC * 2 ** 9), const(8, MAGIC * 2 ** 19)
    bR, bM = const(1, -MAGIC, "F"), const(1, -MAGIC * 2 ** 7, "F")

    def rnd(o, m):
        m = sl(m, 0, width(o))
        return [(o, I1, m), (o, IN, m)]
    BO1, BOh = new("B", 128), new("H", 128)
    ts(BO1, c112, kF, ALU.is_equal)
    move("A", sl(BOh, 0, 112), sl(BO1, 16, 128))
    move("A", sl(BOh, 112, 128), sl(BO1, 0, 16))
    BOn, BOv = scaled(new("H", 128), BO1, -1.0), scaled(new("B", 128), BO1, wv)
    BOq, BOqn = scaled(new("B", 128), BOv, 0.25, "V"), scaled(new("B", 128), BOv, -0.25, "V")
    c38, quarter, cX, c18 = const(128, -0.375), const(128, -0.25), const(8, float(X0)), const(8, -2.0 ** 18)
    p0, p1, p2 = (sl(IF, i, i + 1) for i in range(3))
    r1k, c1k = col(), new("B", 128)
    ts(r1k, p0, 1024.0 + 2.0 ** -10, ALU.mult, -2.0 ** -10, ALU.add)
    scaled(c1k, ones, r1k)
    q3, t3, t4, t5, t6, up = new("I", 3), new("F", 3), new("I", 3), new("I", 3), new("F", 3), col()
    ts(q3, sl(cM, 15, 18), uF, ALU.add, 1.0 / 3, ALU.mult)
    line(up, uF, -16.0, pF)
    ts(t3, sl(cF, 0, 3), -16.0, ALU.mult, up, ALU.add)
    ts(t4, q3, 48.0, ALU.mult, 112.0, ALU.add)
    tt(t4, t4, t3, ALU.add)
    ts(t5, t4, 127, ALU.bitwise_and)
    copy(t6, t5)
    PB, PN = [], []
    for be in range(3):
        pb = new("B", 128)
        ts(pb, sl(cF, 0, 128), sl(t6, be, be + 1), ALU.is_equal)
        PB.append(pb)
        PN.append(scaled(new("B", 128), pb, -1.0))
    IBIG = new("B", 2048)
    ts(IBIG, ramp, uF, ALU.is_equal)
    cz, ca = new("B", 16), new("B", 8)
    for i in range(2):
        scaled(part(cz, i, 8), sl(cF, 0, 8), 0.125)
    scaled(ca, sl(cF, 0, 8), -65536.0)
    E144, RST, cP, bF, listU, colu = new("B", 144), new("F", 128), new("B", 128), col(), new("U", 29), new("F", 4)
    ts(E144, c144, uF, ALU.is_equal)
    E128 = sl(E144, 0, 128)
    ts(colu, cols, uF, ALU.add)
    u1k, u2k, spare, spare2 = (sl(colu, i, i + 1) for i in range(4))
    THR = new("F", 32)
    act(THR, sl(c15, 0, 32), AF.Exp, b27, -3 * LN2)
    fill(sl(THR, 15, 16), 2.0 ** 30)
    FIT, f1 = new("B", 32), new("B", 32)
    act(f1, sl(c15, 0, 32), AF.Exp, b21, -LN2)
    line(FIT, f1, scaled(col(), sl(E128, 1, 2), -1.0), scaled(col(), sl(E128, 0, 1), -2.0 ** 21))
    pickW, pickL, mapK = new("U", 8), new("U", 1), new("U", 1)
    copy(listU, lists)
    repK, rep15, rep9 = sl(listU, 0, 12), sl(listU, 12, 20), sl(listU, 20, 29)
    mk1, RSK = col(), new("B", 192)
    ts(mk1, u7, 1.0, ALU.add, u8, ALU.mult)
    ts(mapK, mk1, u7, ALU.add, 7.0, ALU.min)
    ts(sl(RSK, 0, 128), c31, uF, ALU.not_equal)
    ts(sl(RSK, 128, 192), sl(c15, 0, 64), uF, ALU.not_equal)
    s1, s2, s3, e5 = col("I"), col("I"), col(), col()
    tt(s1, uF, hF, ALU.add)
    ts(s2, s1, 1, ALU.bitwise_and)
    ts(e5, u7, 16.0, ALU.mult, u8, ALU.add)
    ts(s3, s2, 144.0, ALU.mult, e5, ALU.add)
    ts(pickW, sl(cF, 0, 8), 2.0, ALU.mult, s3, ALU.add)
    ts(pickL, hF, 16.0, ALU.mult, uF, ALU.add)

    SelF, SelG, SelDV = new("F", 8), new("B", 8), new("B", 16)
    move("A", SelF, Sel1)
    scaled(sl(SelG, 0, 7), sl(Sel1, 1, 8), 256.0)
    scaled(sl(SelG, 7, 8), sl(Sel1, 0, 1), 256.0)
    SelC, SelE, SelN = scaled(new("B", 8), Sel1, wc), scaled(new("B", 8), Sel1, 256.0), scaled(new("F", 8), Sel1, -1.0)
    SelD = scaled(part(SelDV, 0, 8), Sel1, -256.0)
    scaled(part(SelDV, 1, 8), Sel1, wv)
    ts(RST, c15, 0.0, ALU.is_equal, 8388608.0, ALU.mult)
    ts(bF, kF, 1.0 / 16, ALU.mult, -64.0, ALU.add)
    line(cP, c15, 8.0, bF)
    cV = new("B", 256)
    fill(part(cV, 0, 128), 0.0)
    v1 = line(col(), p0, 15 * 2.0 ** 19, line(col(), p1, 256.0, scaled(col(), p2, 0.5)))
    line(part(cV, 1, 128), c15, scaled(col(), p0, -2.0 ** 19), v1)
    away = pair("U", 16)
    for h in OPT["fast"]:
        q3, m3, m4, a1, a2 = col("I"), col(), col(), new("I", 16), new("I", 16)
        ts(q3, pF, 1.0 / 3, ALU.mult, (2 * h - 1) / 3.0, ALU.add)
        ts(m3, q3, 3.0, ALU.mult, -2.0 * h, ALU.add)
        tt(m4, m3, pF, ALU.subtract)
        for i in range(2):
            ts(part(a1, i, 8), sl(cF, 7 - i, 15 - i), m4, ALU.add)
        ts(a2, a1, 7, ALU.bitwise_and)
        ts(away[h], a2, 16.0, ALU.mult, 15.0, ALU.add)

    GW = OPT["gw"]
    uH, uB, uC, aH, aB, aC, fB, fC, bad, q6 = (new("B", 4096) for _ in range(10))
    a6 = aB
    Z8, ZB4, ZC4 = pair("B", 2048), pair("B", GW), pair("B", GW)
    DD, ZS = pair("B", 256), pair("B", 256)
    D, us, uj, mkB, zm, nf = (pair("B", 128) for _ in range(6))
    thr2, thr62 = new("B", 256), new("B", 256)
    thrN, thr6 = [part(thr2, h, 128) for h in range(2)], [part(thr62, h, 128) for h in range(2)]
    mixed = [("H%d0" % h in OPT["raw"]) != ("H%d1" % h in OPT["raw"]) for h in range(2)]
    TP, TG, TK = pair("F", 288), pair("F", 288), pair("F", 288)
    for z in [sl(LISTS, 144 * i, 144 * i + 16) for i in range(9)] + [part(Z8[h], 1, 1024) for h in range(2) if mixed[h]] \
            + [part(KW[h], 1, 128) for h in range(2)] + [sl(WIN, X0 + 2048, X0 + 2080), sl(WB, 0, X0), sl(WB, X0 + 2048, X0 + 2080)]:
        fill(z, 0.0)
    PU, GU = new("U", 256), new("U", 256)
    CV = pair("F", 256)
    vals, GnB, off, run16, runV, wide, wideB, wideC = (pair("F", 128) for _ in range(8))
    k1, k2 = pair("I", 128), pair("I", 128)
    PM, GM, Kh, Ph = (pair("H", 128) for _ in range(4))
    wide9 = pair("F", 144)
    NH_, s3w = new("B", 16), new("B", 16)
    joff, moff, soff, scU = (pair("U", 8) for _ in range(4))
    cU, zs, kvU = pair("U", 16), pair("U", 16), pair("U", 16)
    krow, eq, cnt, kvc = pair("F", 192), pair("B", 192), pair("B", 192), pair("F", 8)
    zoff, selU = [sl(z, 0, 8) for z in zs], [sl(z, 8, 16) for z in zs]
    vI, cIi = pair("I", 16), pair("I", 16)
    cp1 = pair("B", 8)
    addB, thrE, kv, cbF = (pair("F", 8) for _ in range(4))
    LL, LT, LO, lw, L2 = new("F", 32), new("F", 32), new("F", 16), new("F", 16), new("F", 16)
    a256, ar = col(), [col(), col()]
    aI, aI2, aF = col("I"), col("I"), col()
    fill(a256, 128.0 - 2.0 ** 21)

    def turn(t, qq, at):
        tr(sl(t, 0, 128), sl(qq, at, at + 128))
        tr(sl(t, 128, 288), sl(qq, at - 16, at + 144))
        return t

    def spread(e, z4, src, n):
        move(e, sl(z4, 0, 128), src)
        move(e, sl(z4, 128, 256), src)
        m = 256
        while m < n:
            move(e, sl(z4, m, 2 * m), sl(z4, 0, m))
            m *= 2

    for h in range(2):
        copy(sl(KK[0][h], 16, 144), part(KI, h, 128))
        copy(part(KU, h, 128), ind(turn(TK[h], KK[0][h], 16), pickW))
        copy(sl(CZ[0][h], 0, 128), part(ZO, h, 128))
    copy(sl(LL, 0, 16), LI)
    copy(sl(LL, 16, 32), LI)
    tr(LT, LL)
    copy(L, ind(LT, pickL))
    copy(LU, ind(LT, pickL))
    move("A", SW, SI) if OPT.get("swa") else copy(SW, SI)

    def sums(ps, sel, src, a0, n, stop):
        ks = range(a0 // 128, (a0 + n) // 128)
        mm([(sl(ps, k % 16, width(ps), 16), part(src, k, 128), sel, False, stop and k % 16 == 15) for k in ks])

    def evac(e, out, ps, items):
        if e == "V":
            group(items, OPT["split"])
            ts(out, ps, MAGIC, ALU.add, MAGIC, ALU.subtract)
        else:
            group(items + [(ps, I1, M0)], OPT["split"])
            act(out, ps, AF.Identity, bR, 1.0)

    def pieces(tag, c):
        n = OPT["cut"].get(tag, 1024)
        return [(1024 * c + n * i, n, n * i if n > 256 else 512 * (i % 2) + 256 * (i // 2)) for i in range(1024 // n)]

    def minus(w, terms, a0, n, at, d, neg=IN, more=None):
        for b in range(0, n, 512):
            m = min(n, 512)
            o = sl(w, at + b, at + b + m)
            group([(o, l, sl(s, a0 + b, a0 + b + m)) for l, s in terms] + [(part(o, i, 128), neg, d) for i in range(m // 128)]
                  + ([(o, I1, sl(more, 0, m))] if more else []))

    def gather(u, win, o, z4, a0, n, most):
        for b in range(a0, a0 + n, most):
            m = min(n, most)
            tt(sl(u, b, b + m), ind(win, sl(o, b // 16, (b + m) // 16)), sl(z4, 0, m), ALU.subtract)

    def lanes(out, src, k0, sg, h, y=Y):
        return [(sl(out, (m + h) % 3, 128, 3), sh(y, sg * (k0 + m)), sl(src, (m + h) % 3, 128, 3)) for m in range(3)]

    def wsum(out, z, src):
        return [(out, zu(z, u), sl(src, u, width(src), 16)) for u in range(16)]

    wb = [P["W0"], P["W1"]]
    S2 = [P["SA"], P["SB"]]
    Mh = [P["M0"], P["M1"]]
    nw = [0]

    def nextw():
        nw[0] += 1
        return wb[nw[0] % 2]

    def small(h, i, n=1):
        return sl(Mh[h], 384 + 8 * i, 384 + 8 * (i + n))

    def least(out, a, h, at, key, on=False):
        scan(run16[h], RST, a, ALU.add, ALU.min)
        w = sl(wide9[h], 16, 144)
        if on:
            tt(wide9[h], ind(run16[h], rep9), E144, ALU.mult)
        else:
            tt(w, ind(run16[h], rep15), E128, ALU.mult)
        if key:
            key(small(h, at), w)
        p, w = small(h, at + 1), sl(wide9[h], 0, 128) if on else w
        group([(p, w, SelN)] + rnd(p, M8) + [(p, w, SelF)])
        ts(out, p, 16.0, ALU.mult, u1k, ALU.add)

    def one_round(rnd_):
        last = rnd_ == 2
        win = Xb if rnd_ == 0 else XW
        cz_ = CZ[rnd_ % 2]
        Z = [sl(cz_[h], 0, 128) for h in range(2)]
        K = [sl(KK[rnd_ % 2][h], 16, 144) for h in range(2)]
        Pn, Gn = [sl(q, 16, 144) for q in QP], [sl(q, 16, 144) for q in QG]
        keys = [sl(S2[h], 0, 128) for h in range(2)]

        def home(h, half):
            M, c, tag, fast = Mh[h], 2 * h + half, "H%d%d" % (h, half), h in OPT["fast"]
            if half == 0:
                if not all("H%d%d" % (h, i) in OPT["raw"] for i in range(2)):
                    spread("V" if rnd_ == 0 else "G", Z8[h], Z[h], 1024 if mixed[h] else OPT["gwH"])
                move("G", Kh[h], K[h])
                if h == 0:
                    move(EN["thr"][h], thr2, ind(FIT, LU))
                else:
                    move(EN["t6"][h], thr62, ind(THR, LU))
                if fast:
                    mm([(sl(S2[h], 0, 256), ones, cV, True, False), (keys[h], thrN[h], BO1, False, False)])
                else:
                    mm([(keys[h], thrN[h], BO1, True, False)])
                apart(lanes(sl(M, 0, 128), Z[h], 1, 1, h) + lanes(sl(M, 128, 256), Z[h], 2, 1, h))
                move(EN["zs"][h], ZS[h], sl(M, 0, 256))
                for i, zz in enumerate((ZB4[h], ZC4[h])):
                    spread("G", zz, part(ZS[h], i, 128), GW)
            raw = tag in OPT["raw"]
            w = nextw() if raw else None
            for a0, n, at in pieces(tag, c):
                if raw:
                    act(sl(uH, a0, a0 + n), ind(win, sl(KU, a0 // 16, (a0 + n) // 16)), AF.Copy)
                    minus(w, [(I1, uH)], a0, n, at, Z[h])
                    act(sl(aH, a0, a0 + n), sl(w, at, at + n), AF.Abs)
                else:
                    gather(uH, win, KU, Z8[h], a0, n, OPT["gwH"])
                    act(sl(aH, a0, a0 + n), sl(uH, a0, a0 + n), AF.Abs)
                ts(sl(bad, a0, a0 + n), sl(aH, a0, a0 + n), 48.0, ALU.is_gt)
                sums(keys[h], SelC, bad, a0, n, False)

        def speaker(h):
            M, S, fast = Mh[h], S2[h], h in OPT["fast"]
            raws = ["H%d%d" % (h, i) in OPT["raw"] for i in range(2)]
            mm([(o, l, r, False, False) for o, l, r in rnd(keys[h], M22) + [(keys[h], I1, cP)]])
            for c in (2 * h, 2 * h + 1):
                sums(sl(S, 0, 256) if fast else keys[h], SelDV if fast else SelD, aH, 1024 * c, 1024, True)
            if fast:
                scan(run16[h], RST, keys[h], ALU.add, ALU.min)
                tt(nf[h], keys[h], run16[h], ALU.not_equal)
                scan(runV[h], nf[h], sl(S, 128, 256), ALU.mult, ALU.max)
                o, w = small(h, 0), wideB[h]
                tt(w, ind(runV[h], part(away[h], 0, 8)), E128, ALU.mult)
                group([(o, w, SelN)] + rnd(o, M9) + [(o, w, SelF)])
                ts(part(cU[h], 0, 8), o, 255.5, ALU.add)
                ts(cbF[h], o, 4096 + 255.5, ALU.add)
                o, w = small(h, 1), wide[h]
                tt(w, ind(runV[h], rep15), E128, ALU.mult)
                group([(o, w, SelF), (o, I1, c18)] + rnd(o, M19) + [(o, I1, ca)])
                ts(soff[h], o, -2.0 ** -12, ALU.mult, u2k, ALU.add)
                o, w = small(h, 2), wideC[h]
                tt(w, ind(runV[h], part(away[h], 1, 8)), E128, ALU.mult)
                group([(o, w, SelN)] + rnd(o, M11) + [(o, w, SelF)])
                ts(part(vI[h], 1, 8), o, -256.5, ALU.add, 21.0, ALU.mult)
                ts(part(cIi[h], 1, 8), part(vI[h], 1, 8), 2, ALU.arith_shift_right, 511, ALU.bitwise_and)
                copy(part(cU[h], 1, 8), part(cIi[h], 1, 8))
            else:
                least(soff[h], keys[h], h, 0, None)
            move(EN["dg"][h], D[h], ind(part(aH, h, 2048), soff[h]))
            move(EN["us"][h], us[h], ind(part(uH, h, 2048), soff[h]))
            apart(lanes(sl(M, 0, 128), D[h], 1, 1, h) + ([] if fast else lanes(sl(M, 128, 256), D[h], 2, 1, h)))
            move(EN["dd"][h], sl(DD[h], 0, 128 if fast else 256), sl(M, 0, 128 if fast else 256))
            if not fast:
                o = small(h, 2, 2)
                group(wsum(o, Zv, DD[h]))
                tt(vI[h], o, c421, ALU.mult)
                ts(cIi[h], vI[h], 2, ALU.arith_shift_right, 511, ALU.bitwise_and)
                copy(cU[h], cIi[h])
                ts(cbF[h], part(cIi[h], 0, 8), 4096.0, ALU.add)
            for qq, t, o, i, e in ((QP, TP, PU, 0, EN["pl"][h]), (QG, TG, GU, 1, EN["gl"][h])):
                move(e, sl(qq[h], 16, 144), ind(SW, part(cU[h], i, 8)))
                copy(part(o, h, 128), ind(turn(t[h], qq[h], 16), pickW))
            o = sl(S, 256, 384)
            if OPT["kh"][h] == "V":
                group([(o, I20, Kh[h]), (o, BOv, D[h])])
                copy(k1[h], o)
                ts(k2[h], k1[h], 2, ALU.arith_shift_right, 2047, ALU.bitwise_and)
                tt(part(KW[h], 0, 128), k2[h], K[h], ALU.subtract)
            else:
                evac(EN["kh"][h], part(KW[h], 0, 128), o,
                     [(o, I5N, Kh[h]), (o, BOqn, D[h]), (o, ones, c1k)] + rnd(o, M11) + [(o, I4, Kh[h]), (o, BOq, D[h]), (o, I1, c38)])
            o = sl(S, 384, 512)
            aim = [(o, IH if any(raws) else I1, Z[h])]
            if mixed[h]:
                move(EN["zm"][h], zm[h], ind(Z8[h], soff[h]))
                aim.append((o, IH, zm[h]))
            evac(EN["zf"][h], sl(cz_[h], 128, 256), o, [(o, I1, quarter), (o, IH, us[h])] + aim)
            o = sl(S, 128, 256)
            move("G", Ph[h], Pn[h])
            group([(o, INH, Kh[h])] + lanes(o, Ph[h], 1, -1, h, YH))

        def look(name, h, half):
            u, a, f, o, z4, i = (uB, aB, fB, PU, ZB4[h], 0) if name == "B" else (uC, aC, fC, GU, ZC4[h], 1)
            c, tag = 2 * h + half, "%s%d%d" % (name, h, half)
            w = nextw()
            if half == 0:
                mm([(keys[h], I1, cP, True, False)])
            for a0, n, at in pieces(tag, c):
                terms = [(I1, a)]
                if tag in OPT["raw"]:
                    act(sl(u, a0, a0 + n), ind(win, sl(o, a0 // 16, (a0 + n) // 16)), AF.Copy)
                    minus(w, [(I1, u)], a0, n, at, part(ZS[h], i, 128))
                    act(sl(a, a0, a0 + n), sl(w, at, at + n), AF.Abs)
                else:
                    gather(u, win, o, z4, a0, n, GW)
                    if tag in OPT["relu"]:
                        ts(sl(a, a0, a0 + n), sl(u, a0, a0 + n), 0.0, ALU.max)
                        terms = [(I2, a), (IN, u)]
                    else:
                        act(sl(a, a0, a0 + n), sl(u, a0, a0 + n), AF.Abs)
                minus(w, terms, a0, n, at, part(DD[h], 0, 128), sh(YN, i))
                act(sl(f, a0, a0 + n), sl(w, at, at + n), AF.Abs)
                sums(keys[h], SelE if name == "B" else SelG, f, a0, n, True)

        def partner(h):
            M = Mh[h]
            raw = all("H%d%d" % (h, i) in OPT["raw"] for i in range(2))

            def bounds(o, w):
                apart([(o, w, SelF)])
                ts(cp1[h], o, 640.0 * 256 - 100, ALU.is_lt, 1.0, ALU.add)
                ts(thrE[h], o, a256, ALU.add)
            least(joff[h], keys[h], h, 4, bounds)
            tt(PM[h], ind(IBIG, joff[h]), Pn[h], ALU.mult)
            move(EN["uj"][h], uj[h], ind(part(uB, h, 2048), joff[h]))
            move(EN["mk"][h], mkB[h], ind(IBIG, joff[h]))
            o = small(h, 6)
            group([(o, I1, cX)] + wsum(o, Zh, PM[h]) + [(o, I4K, cp1[h])])
            ts(addB[h], o, NONE + 4096.0, ALU.min)
            back = lambda out: lanes(out, uj[h], 1, -1, h)
            if not raw:
                apart(back(sl(M, 128, 256)))
            group([(sl(M, 0, 128), I1, Z[h])] + back(sl(M, 0, 128)))
            n = 128 if raw else 256
            move(EN["cz"][h], sl(cz_[h], 256, 256 + n), sl(M, 0, n))
            o = sl(M, 256, 384)
            group([(o, I1, quarter), (o, IH, uj[h]), (o, IH, part(DD[h], 0, 128)), (o, IH, part(ZS[h], 0, 128))] + rnd(o, M0) + [(o, INH, Ph[h])])
            move(EN["cv"][h], part(CV[h], 1, 128), o)

        def contact(h, half):
            c, tag = 2 * h + half, "S%d%d" % (h, half)
            how, w = OPT["s6"][c], nextw()
            d = sl(cz_[h], 256, 384) if "H%d%d" % (h, half) in OPT["raw"] else sl(cz_[h], 384, 512)
            for a0, n, at in pieces(tag, c):
                minus(w, [(IS, uH)], a0, n, at, d, ISN, M7 if how == "P" else None)
                q, src = sl(q6, a0, a0 + n), sl(w, at, at + n)
                if how == "V":
                    ts(q, src, MAGIC * 2 ** 7, ALU.add, MAGIC * 2 ** 7, ALU.not_equal)
                elif how == "P":
                    act(q, src, AF.Abs, bM, 1.0)
                else:
                    act(sl(a6, a0, a0 + n), src, AF.Abs)
                    ts(q, sl(a6, a0, a0 + n), 63.5, ALU.is_gt)

        def replace(h):
            cs = sl(S2[0], 256 + 128 * h, 384 + 128 * h) if OPT["cs"][h] == "A" else sl(S2[1], 256, 384)
            mm([(cs, IN, thr6[h], True, False)])
            for c in (2 * h, 2 * h + 1):
                mm([(cs, zu(Zq if OPT["s6"][c] == "P" else Zr, k % 16), part(q6, k, 128), False, k % 16 == 15) for k in range(8 * c, 8 * c + 8)])
            ts(off[h], cs, 0.0, ALU.is_ge)
            tt(part(KW[h], 2, 128), sl(S2[h], 128, 256), off[h], ALU.mult)

        def guesser(h):
            def outcome(o, w):
                group([(o, w, SelF), (o, INF, thrE[h])] + rnd(o, M22) + [(o, IF, cbF[h])])
                tt(kv[h], o, addB[h], ALU.min)
                ts(part(NH_, h, 8), o, 2.0 ** 21, ALU.is_ge)
            least(moff[h], keys[h], h, 7, outcome, True)

        def decide(h):
            M = Mh[h]
            nh, s3 = part(NH_, h, 8), part(s3w, h, 8)
            ts(kvU[h], ind(kv[h], mapK), -4096.0, ALU.add)
            tt(s3, nh, cp1[h], ALU.mult)
            o = small(h, 9, 2)
            group([(o, I1, cz), (part(o, 1, 8), I1, nh)] + [(sl(o, b, 8, 3), PB[(b + 2 * h) % 3], sl(s3, b, 8, 3)) for b in range(3)])
            ts(zs[h], o, 128.0, ALU.mult, uF, ALU.add)
            tt(GM[h], ind(IBIG, moff[h]), Gn[h], ALU.mult)
            move(EN["kr"][h], krow[h], ind(IOTA, sl(kvU[h], 0, 12)))
            o = sl(M, 256, 384)
            group([(o, BOh, GM[h]), (o, BOn, PM[h])])
            tt(part(CV[h], 0, 128), o, mkB[h], ALU.mult)
            tt(vals[h], ind(CV[h], selU[h]), Pn[h], ALU.add)
            tt(eq[h], ind(kv[h], repK), krow[h], ALU.is_equal)
            scan(cnt[h], RSK, eq[h], ALU.mult, ALU.add)
            for i, (ends, sp) in enumerate(((sl(cnt[h], 31, 128, 32), spare), (sl(cnt[h], 143, 192, 16), spare2))):
                tt(sl(kvc[h], i, 8, 2), ends, sl(kv[h], i, 8, 2), ALU.mult)
                ts(sl(scU[h], i, 8, 2), sl(kvc[h], i, 8, 2), -4096.0, ALU.add, sp, ALU.min)

        def prefix():
            o = small(1, 12, 2)
            mm([(sl(o, b, 16, 3), l[b], sl(s, b, 16, 3), l is PB, l is PN) for b in range(3) for l, s in ((PB, s3w), (PN, NH_))])
            tt(L, o, L, ALU.add)
            if last:
                ts(lw, L, 16.0, ALU.is_ge, -16.0, ALU.mult)
                tt(L, L, lw, ALU.add)

        def settle(h):
            if last:
                move(EN["zz"][h], part(ZO, h, 128), ind(sl(cz_[h], 0, 384), zoff[h]))
                tt(part(KO, h, 128), ind(KW[h], zoff[h]), K[h], ALU.add)
                return
            nk = KK[(rnd_ + 1) % 2][h]
            move(EN["zz"][h], sl(CZ[(rnd_ + 1) % 2][h], 0, 128), ind(sl(cz_[h], 0, 384), zoff[h]))
            tt(sl(nk, 16, 144), ind(KW[h], zoff[h]), K[h], ALU.add)
            copy(part(KU, h, 128), ind(turn(TK[h], nk, 16), pickW))

        def write(h):
            tie[0] += "!" * last
            if last and h == 0:
                dma("G", ap(Xb), ap(XW), [XW], [Xb], 1.5)
            for b in range(4):
                for win_ in ([WB] if last else []) + [WIN]:
                    copy(ind(win_, part(scU[h], b, 2)), part(vals[h], b, 32))

        def count(h):
            prefix()
            if last:
                for i in range(2):
                    copy(part(LL, i, 16), L)
                return
            copy(LU, L)
            o = small(0, 12, 2)
            apart([(o, BO1, NH_)])
            reduce(ar[rnd_], o, ALU.add)
            if rnd_ == 1:
                tt(ar[1], ar[1], ar[0], ALU.add)
            ts(aI, ar[rnd_], -1.0, ALU.mult, 1024.0, ALU.add)
            ts(aI2, aI, 31, ALU.bitwise_and)
            ts(a256, aI2, 256.0, ALU.mult, 128.0 - 2.0 ** 21, ALU.add)

        return {"h": speaker, "b": partner, "c": guesser, "t": replace, "d": decide, "w": write, "e": settle, "p": count, "H": home, "S": contact,
                "B": lambda h, i: look("B", h, i), "C": lambda h, i: look("C", h, i)}

    rounds = [one_round(r) for r in range(3)]
    for r in range(4):
        for s in OPT["order"].split():
            late = s[-1] == "-"
            if 0 <= r - late < 3:
                tie[0:2] = [s + ("!" if r - late == 2 and s[0] in "ep" else ""), 0]
                rounds[r - late][s[0]](*[int(x) for x in s[1:].strip("-")])
    tie[0:2] = ["end", 0]

    tr(LT, LL)
    copy(LO, ind(LT, pickL))
    out = {"oz": (ZO, T.yz[:], 0.3), "ol": (LO, T.yl[:], 0.1), "oa": (SW, T.ya[:], 0.8), "ox": (part(Xb, 0, 1024), T.yx[:, 0:1024], 0.8),
           "oy": (part(Xb, 1, 1024), T.yx[:, 1024:2048], 0.8), "ok": (KO, T.yk[:], 0.4)}
    home_calls = [ci for ci in range(len(CALLS)) if CALLS[ci][0][0] == "o"]
    for ci in home_calls:
        for k in CALLS[ci]:
            dma("S", T["s" + k][:], ap(out[k][0]), [out[k][0]], [("s" + k, 0, 8)], out[k][2])
            own("S", k, T["s" + k][0 if k == "ol" else rank], [("s" + k, 0, 8)])
        remote(ci)
    for ci in home_calls:
        for k in CALLS[ci]:
            src = T.lol[:, rows, :] if k == "ol" else T["l" + k][:]
            dma("A", out[k][1], src, [("l" + k, 0, 8), mark(k), KO, Xb], [("y" + k, 0, 1)], out[k][2], ext=arr(k))
    ops[0]["end"] = [(T.sem.sent, sent[0])]
    used, kept = {}, []
    for o in ops[::-1]:
        if o["tie"][0] == "once" and o["w"][0][0] in top and not o["dma"] and not any(
                lo < w[2] and w[1] < hi for w in o["w"] for lo, hi in used.get(w[0], ())):
            continue
        kept.append(o)
        for a in o["r"]:
            used.setdefault(a[0], set()).add((a[1], a[2]))
    return kept[::-1]
